import numpy as np
import ml_dtypes


def mxq(x, axis, fmt="e4m3"):
    dtype, down = {"e4m3": (ml_dtypes.float8_e4m3fn, 7), "e5m2": (ml_dtypes.float8_e5m2, 14)}[fmt]
    v = np.moveaxis(np.asarray(x, np.float32).astype(ml_dtypes.bfloat16).astype(np.float64), axis, -1)
    blocks = v.reshape(v.shape[:-1] + (-1, 32))
    amax = np.abs(blocks).max(-1, keepdims=True)
    byte = np.maximum(np.where(amax > 0, np.frexp(amax)[1] - 1 + 127, 0) - down, 1)
    scale = np.exp2(byte - 127.0)
    codes = (blocks / scale).astype(np.float32).astype(dtype).astype(np.float64)
    return np.moveaxis((codes * scale).reshape(v.shape), -1, axis)


WIDE = False


def mx_kscale(k):
    if not WIDE:
        return np.ones(k)
    levels = np.array([10, -10, 5, -5, 0])
    if k % 512:
        return np.exp2(np.random.permutation(np.resize(levels, k // 32))).repeat(32)
    a = np.empty((k // 512, 16))
    for p in range(k // 512):
        a[p, :8] = np.random.permutation(np.resize(levels, 8))
        for g in range(8):
            far = levels[np.abs(levels - a[p, g]) >= 10]
            a[p, g + 8] = far[np.random.randint(len(far))]
    return np.exp2(a.ravel()).repeat(32)


def f64(x):
    return np.asarray(x).astype(np.float64)


def striped(idx):
    return np.tile(idx.reshape(-1, 16).T, (8, 1)).astype(np.uint16)


def unstriped(offs):
    return offs[:16].T.reshape(-1).astype(np.int64)


E2M1 = np.array([0.0, 0.5, 1.0, 1.5, 2.0, 3.0, 4.0, 6.0, -0.0, -0.5, -1.0, -1.5, -2.0, -3.0, -4.0, -6.0])


def pack_weight(w, fmt):
    k, n = w.shape
    w = f64(np.asarray(w, np.float32).astype(ml_dtypes.bfloat16)).reshape(k // 32, 32, n)
    amax = np.abs(w).max(1)
    if fmt == "e4m3":
        byte = np.frexp(amax)[1] - 1 + 127 - 7
    else:
        mant, ex = np.frexp(amax / 6.0)
        byte = np.where(mant > 0.5, ex, ex - 1) + 127
    byte = np.clip(np.where(amax > 0, byte, 1), 1, 254)
    scaled = (w * np.exp2(127.0 - byte)[:, None, :]).reshape(k, n).astype(np.float32)
    by_word = np.ascontiguousarray(scaled.reshape(k // 512, 128, 4, n).transpose(0, 1, 3, 2))
    if fmt == "e4m3":
        words = by_word.astype(ml_dtypes.float8_e4m3fn).view(np.uint8)
    else:
        c = by_word.astype(ml_dtypes.float4_e2m1fn).view(np.uint8) & 0xF
        words = (c[..., 0::2] | (c[..., 1::2] << 4)).reshape(k // 512, 128, 2 * n)
    return np.ascontiguousarray(words), np.ascontiguousarray(byte.astype(np.uint8).reshape(k // 512, 16, n))


def unpack_weight(words, scales, fmt):
    g, _, n = scales.shape
    words = np.ascontiguousarray(words).reshape(g, 128, n, -1)
    if fmt == "e4m3":
        vals = words.view(ml_dtypes.float8_e4m3fn).astype(np.float64)
    else:
        nib = np.empty((g, 128, n, 4), np.uint8)
        nib[..., 0::2] = words & 0xF
        nib[..., 1::2] = words >> 4
        vals = E2M1[nib]
    vals = vals * np.repeat(np.exp2(scales.astype(np.float64) - 127.0), 8, axis=1)[..., None]
    return vals.transpose(0, 1, 3, 2).reshape(g * 512, n)


def d_relu(v):
    return (v > 0).astype(np.float64)


K, T, E, C, H, N = 256, 768, 18, 128, 512, 512
TOP = 3


def by_expert(wq, xq):
    return np.concatenate([wq[e].T @ xq[:, e * C:(e + 1) * C] for e in range(E)], axis=1)


def setup_inputs():
    n = np.random.standard_normal
    s = mx_kscale(N)[:, None]
    u = mx_kscale(H)
    deal = np.repeat(np.arange(E), C).reshape(TOP, T)[:, np.random.permutation(T)]
    deal = np.take_along_axis(deal, np.argsort(np.random.rand(TOP, T), axis=0), axis=0)
    for _ in range(8):
        s_, t_ = np.random.permutation(T).reshape(2, -1); r = np.random.randint(TOP, size=T // 2); x, y = deal[r, s_].copy(), deal[r, t_].copy()
        ok = ~((deal[:, s_] == y).any(0) | (deal[:, t_] == x).any(0)); deal[r[ok], s_[ok]] = y[ok]; deal[r[ok], t_[ok]] = x[ok]
    order = np.lexsort((np.random.rand(TOP * T), deal.reshape(-1)))
    slot_token = order % T; pos = np.empty(TOP * T, np.int64); pos[order] = np.arange(TOP * T); pos = pos.reshape(TOP, T)
    g = np.random.uniform(0.5, 1.5, (TOP, T)); g = g / g.sum(0)
    w_slot = np.empty(E * C)
    for r in range(TOP): w_slot[pos[r]] = g[r]
    dy = pack_weight(n((N, T)) * s, "e4m3")
    return {
        "dy_words": dy[0],
        "dy_scales": dy[1],
        "a": n((H, E * C)).astype(np.float32),
        "w2": (n((E, N, H)) / np.sqrt(N) / s[None] * u[None, None, :]).astype(np.float32),
        "w1": (n((E, H, K)) / np.sqrt(H) / u[None, :, None]).astype(np.float32),
        "gate": np.tile(w_slot, (H, 1)).astype(np.float32),
        "offs": striped(slot_token),
        "pos1": striped(pos[0]),
        "pos2": striped(pos[1]),
        "pos3": striped(pos[2]),
    }


def reference(dy_words, dy_scales, a, w2, w1, gate, offs, pos1, pos2, pos3):
    idx = unstriped(offs)
    gq = unpack_weight(dy_words, dy_scales, "e4m3")[:, idx]
    dh = f64(gate) * by_expert(mxq(f64(w2), 1, "e4m3"), gq)
    da = dh * d_relu(f64(a))
    dx = by_expert(mxq(f64(w1), 1, "e4m3"), mxq(da, 0, "e4m3"))
    return dx[:, unstriped(pos1)] + dx[:, unstriped(pos2)] + dx[:, unstriped(pos3)]

@@ -1,0 +1,195 @@
+from contextlib import ExitStack
+
+import concourse.mybir as mybir
+from concourse.masks import make_identity
+
+K, T, E, C, H, N = 256, 768, 18, 128, 512, 512
+S = E * C
+FLOPS = 2 * S * (N * H + H * K)
+BYTES = 4 * (E * N * H + E * H * K + H * S + S + K * T) + N * T + 16 * T + 2 * 128 * (S + 3 * T) // 16
+
+F32 = mybir.dt.float32
+BF16 = mybir.dt.bfloat16
+I32 = mybir.dt.int32
+U32 = mybir.dt.uint32
+U16 = mybir.dt.uint16
+U8 = mybir.dt.uint8
+FP8X4 = mybir.dt.float8_e4m3fn_x4
+ALU = mybir.AluOpType
+
+P = 128
+PACK = 4
+PAIR = 2 * C
+LIST_COLS = 16
+W1_LAG = 4
+A_CHUNKS = [(0, 256), (256, 512), (768, 512), (1280, 512), (1792, 512)]
+
+
+def tile_moe_bdx_mlp_relu_kernel(
+    tc, dy_words, dy_scales, a, w2, w1, gate, offs, pos1, pos2, pos3, out
+):
+    nc = tc.nc
+    with ExitStack() as ctx:
+        lists = ctx.enter_context(tc.tile_pool(name="lists", bufs=1))
+        keep = ctx.enter_context(tc.tile_pool(name="keep", bufs=1))
+        stream = ctx.enter_context(tc.tile_pool(name="stream", bufs=3))
+        psum = ctx.enter_context(tc.psum_pool(name="psum", bufs=2))
+
+        offs_sb = lists.tile([P, S // LIST_COLS], U16, name="offs_sb")
+        pos_sb = [lists.tile([P, T // LIST_COLS], U16, name="pos_sb%d" % r) for r in range(3)]
+        dy_w = keep.tile([P, T], I32, name="dy_w")
+        dy_s = keep.tile([P, T // 4], I32, name="dy_s")
+        ident = keep.tile([P, P], F32, name="ident")
+        gate_rows = keep.tile([P, C], F32, name="gate_rows")
+        gate_cols = keep.tile([P, 32], F32, name="gate_cols")
+        dx = keep.tile([P, K // P, S], F32, name="dx")
+        a_sb = [keep.tile([P, PACK, width], F32, name="a_sb%d" % n) for n, (first, width) in enumerate(A_CHUNKS)]
+        a_rows = a.rearrange("(p t) s -> p t s", t=PACK)
+
+        w2_raw, w1_raw, da_codes, da_scales, gated, g_words, g_scales, dx_banks = {}, {}, {}, {}, {}, {}, {}, {}
+
+        def load_w2(e):
+            w2_raw[e] = stream.tile([P, PACK, H], F32, name="w2_raw", bufs=6)
+            nc.sync.dma_start(out=w2_raw[e][:], in_=w2[e].rearrange("(p j) i -> p j i", j=PACK))
+
+        def load_w1(e):
+            w1_raw[e] = stream.tile([P, PACK, K], F32, name="w1_raw", bufs=6)
+            nc.sync.dma_start(out=w1_raw[e][:], in_=w1[e].rearrange("(p j) k -> p j k", j=PACK))
+
+        def load_a(n):
+            first, width = A_CHUNKS[n]
+            nc.sync.dma_start(out=a_sb[n][:], in_=a_rows[:, :, first : first + width])
+
+        def prepare_pair(q):
+            cols = offs_sb[:, q * PAIR // LIST_COLS : (q + 1) * PAIR // LIST_COLS]
+            g_words[q] = keep.tile([P, PAIR], U32, name="g_words%d" % q, align_bytes=64)
+            g_scales[q] = keep.tile([P, PAIR], U8, name="g_scales%d" % q, align_bytes=64)
+            nc.vector.tensor_copy(g_words[q][:], dy_w[:].bitcast(U32).indirect(cols))
+            nc.vector.tensor_copy(g_scales[q][:], dy_s[:].bitcast(U8).indirect(cols))
+            gate_bank = psum.tile([P, PAIR], F32, name="gate_bank")
+            for u in range(2):
+                e = 2 * q + u
+                nc.tensor.transpose(
+                    gate_bank[:, u * C : (u + 1) * C], gate_cols[:, e : e + 1].to_broadcast([P, P]), ident[:]
+                )
+            n = [first <= q * PAIR < first + width for first, width in A_CHUNKS].index(True)
+            first = q * PAIR - A_CHUNKS[n][0]
+            gated[q] = stream.tile([P, PACK, PAIR], F32, name="gated")
+            nc.vector.scalar_tensor_tensor(
+                out=gated[q][:],
+                in0=a_sb[n][:, :, first : first + PAIR],
+                scalar=0.0,
+                in1=gate_bank[:].unsqueeze(1).to_broadcast([P, PACK, PAIR]),
+                op0=ALU.is_gt,
+                op1=ALU.mult,
+            )
+
+        def first_product(e):
+            q, u = divmod(e, 2)
+            slots = slice(u * C, (u + 1) * C)
+            w2_bf = stream.tile([P, H * PACK], BF16, name="w2_bf", align_bytes=64)
+            nc.scalar.copy(
+                out=w2_bf[:].rearrange("p (t m j) -> p m j t", t=PACK, j=PACK),
+                in_=w2_raw[e][:].rearrange("p j (m t) -> p m j t", t=PACK),
+            )
+            w2_codes = stream.tile([P, H], U32, name="w2_codes", align_bytes=64)
+            w2_scales = stream.tile([P, H], U8, name="w2_scales", align_bytes=64)
+            nc.vector.quantize_mx(out=w2_codes[:].bitcast(FP8X4), scales=w2_scales[:], in_=w2_bf[:])
+            dh = psum.tile([P, PACK, C], F32, name="dh", bufs=3)
+            for t in range(PACK):
+                cols = slice(t * P, (t + 1) * P)
+                nc.tensor.matmul_mx(
+                    out=dh[:, t, :],
+                    lhsT=w2_codes[:, cols].bitcast(FP8X4),
+                    lhsT_scale=w2_scales[:, cols],
+                    rhs=g_words[q][:, slots].bitcast(FP8X4),
+                    rhs_scale=g_scales[q][:, slots],
+                    start=True,
+                    stop=True,
+                )
+            da_bf = stream.tile([P, C * PACK], BF16, name="da_bf", align_bytes=64)
+            nc.vector.tensor_tensor(
+                out=da_bf[:].rearrange("p (c i t) -> p c t i", i=4, t=PACK),
+                in0=dh[:].rearrange("p t (c i) -> p c t i", i=4),
+                in1=gated[q][:, :, slots].rearrange("p t (c i) -> p c t i", i=4),
+                op=ALU.mult,
+            )
+            da_codes[e] = keep.tile([P, C], U32, name="da_codes%d" % e, align_bytes=64)
+            da_scales[e] = keep.tile([P, C], U8, name="da_scales%d" % e, align_bytes=64)
+            nc.vector.quantize_mx(out=da_codes[e][:].bitcast(FP8X4), scales=da_scales[e][:], in_=da_bf[:])
+
+        def second_product(e):
+            q, u = divmod(e, 2)
+            w1_bf = stream.tile([P, K * PACK], BF16, name="w1_bf", align_bytes=64)
+            for h, cast in ((0, nc.vector.tensor_copy), (1, nc.scalar.copy)):
+                cast(
+                    out=w1_bf[:, h * P * PACK : (h + 1) * P * PACK].rearrange("p (c i j) -> p c j i", i=4, j=PACK),
+                    in_=w1_raw[e][:, :, h * P : (h + 1) * P].rearrange("p j (c i) -> p c j i", i=4),
+                )
+            w1_codes = stream.tile([P, K], U32, name="w1_codes", align_bytes=64)
+            w1_scales = stream.tile([P, K], U8, name="w1_scales", align_bytes=64)
+            nc.vector.quantize_mx(out=w1_codes[:].bitcast(FP8X4), scales=w1_scales[:], in_=w1_bf[:])
+            if u == 0:
+                dx_banks[q] = psum.tile([P, K // P, PAIR], F32, name="dx_bank")
+            for h in range(K // P):
+                cols = slice(h * P, (h + 1) * P)
+                nc.tensor.matmul_mx(
+                    out=dx_banks[q][:, h, u * C : (u + 1) * C],
+                    lhsT=w1_codes[:, cols].bitcast(FP8X4),
+                    lhsT_scale=w1_scales[:, cols],
+                    rhs=da_codes[e][:].bitcast(FP8X4),
+                    rhs_scale=da_scales[e][:],
+                    start=True,
+                    stop=True,
+                )
+            if u == 1:
+                nc.scalar.copy(out=dx[:, :, q * PAIR : (q + 1) * PAIR], in_=dx_banks[q][:])
+
+        nc.vector.memset(dy_s[:], 0)
+        load_w2(0)
+        nc.sync.dma_start(offs_sb[:], offs)
+        nc.sync.dma_start(out=dy_w[:], in_=dy_words[0].rearrange("p t d -> p (t d)").bitcast(I32))
+        for r in range(4):
+            if r == 2:
+                load_w2(1)
+            nc.sync.dma_start(out=dy_s[r:P:32, :], in_=dy_scales[0].bitcast(I32)[r:16:4, :])
+        nc.sync.dma_start(out=gate_rows[:], in_=gate.rearrange("r (e c) -> (r e) c", c=C)[0:P, :])
+        make_identity(nc, ident[:])
+        gate_turned = psum.tile([P, P], F32, name="gate_turned", bufs=1)
+        nc.tensor.transpose(gate_turned[:], gate_rows[:], ident[:])
+        nc.vector.tensor_copy(out=gate_cols[:], in_=gate_turned[:, 0:32])
+
+        for step in range(E + W1_LAG):
+            if step < E:
+                if step > 1:
+                    load_w2(step)
+                for n, (first, width) in enumerate(A_CHUNKS):
+                    if first == step * C:
+                        load_a(n)
+            if step == 2:
+                for r, pos in enumerate((pos1, pos2, pos3)):
+                    nc.sync.dma_start(pos_sb[r][:], pos)
+            if step >= W1_LAG:
+                load_w1(step - W1_LAG)
+            if step < E:
+                if step % 2 == 0:
+                    prepare_pair(step // 2)
+                first_product(step)
+            if step >= W1_LAG:
+                second_product(step - W1_LAG)
+
+        half = T // 2
+        for h in range(K // P):
+            picked = [stream.tile([P, T], F32, name="picked%d" % r, bufs=2) for r in range(3)]
+            window = dx[:, h, :]
+            two = stream.tile([P, T], F32, name="two", bufs=2)
+            three = stream.tile([P, T], F32, name="three", bufs=2)
+            nc.vector.tensor_copy(picked[0][:], window.indirect(pos_sb[0][:]))
+            nc.vector.tensor_copy(picked[1][:], window.indirect(pos_sb[1][:]))
+            nc.vector.tensor_copy(picked[2][:, 0:half], window.indirect(pos_sb[2][:, 0 : half // LIST_COLS]))
+            nc.vector.tensor_tensor(out=two[:], in0=picked[0][:], in1=picked[1][:], op=ALU.add)
+            nc.vector.tensor_copy(picked[2][:, half:T], window.indirect(pos_sb[2][:, half // LIST_COLS : T // LIST_COLS]))
+            for first in (0, half):
+                tokens = slice(first, first + half)
+                nc.vector.tensor_tensor(out=three[:, tokens], in0=two[:, tokens], in1=picked[2][:, tokens], op=ALU.add)
+                nc.sync.dma_start(out=out[h * P : (h + 1) * P, tokens], in_=three[:, tokens])

@@ -21,7 +21,8 @@ P = 128
 PACK = 4
 PAIR = 2 * C
 LIST_COLS = 16
-W1_LAG = 4
+W1_LAG = 6
+WHOLE_W1 = 6
 A_CHUNKS = [(0, 256), (256, 512), (768, 512), (1280, 512), (1792, 512)]
 
 
@@ -43,29 +44,50 @@ def tile_moe_bdx_mlp_relu_kernel(
         gate_rows = keep.tile([P, C], F32, name="gate_rows")
         gate_cols = keep.tile([P, 32], F32, name="gate_cols")
         dx = keep.tile([P, K // P, S], F32, name="dx")
-        a_sb = [keep.tile([P, PACK, width], F32, name="a_sb%d" % n) for n, (first, width) in enumerate(A_CHUNKS)]
+        a_sb = {}
         a_rows = a.rearrange("(p t) s -> p t s", t=PACK)
 
-        w2_raw, w1_raw, da_codes, da_scales, gated, g_words, g_scales, dx_banks = {}, {}, {}, {}, {}, {}, {}, {}
+        w2_raw, w2_bf, dh, da_bf, da_codes, da_scales = {}, {}, {}, {}, {}, {}
+        w1_raw, w1_bf, dx_banks, gated, g_words, g_scales = {}, {}, {}, {}, {}, {}
 
         def load_w2(e):
             w2_raw[e] = stream.tile([P, PACK, H], F32, name="w2_raw", bufs=6)
             nc.sync.dma_start(out=w2_raw[e][:], in_=w2[e].rearrange("(p j) i -> p j i", j=PACK))
 
-        def load_w1(e):
-            w1_raw[e] = stream.tile([P, PACK, K], F32, name="w1_raw", bufs=6)
-            nc.sync.dma_start(out=w1_raw[e][:], in_=w1[e].rearrange("(p j) k -> p j k", j=PACK))
+        def load_w1(e, halves):
+            rows = w1[e].rearrange("(p j) k -> p j k", j=PACK)
+            if len(halves) == 2:
+                if e % 2 == 0:
+                    side = stream.tile([P, 2 * PACK * K], F32, name="side", bufs=3)
+                    both = side[:].rearrange("p (e j k) -> p e j k", e=2, j=PACK)
+                    nc.sync.dma_start(
+                        out=side[:].rearrange("p (e r) -> p e r", e=2),
+                        in_=w1[e : e + 2].rearrange("e (p j) k -> p e (j k)", j=PACK),
+                    )
+                    for u in range(2):
+                        for h in halves:
+                            w1_raw[e + u, h] = both[:, u, :, h * P : (h + 1) * P]
+            else:
+                h = halves[0]
+                part = stream.tile([P, PACK, P], F32, name="w1_part", bufs=12)
+                nc.sync.dma_start(out=part[:], in_=rows[:, :, h * P : (h + 1) * P])
+                w1_raw[e, h] = part[:]
 
         def load_a(n):
             first, width = A_CHUNKS[n]
-            nc.sync.dma_start(out=a_sb[n][:], in_=a_rows[:, :, first : first + width])
+            side = stream.tile([P, PACK * width], F32, name="side", bufs=3)
+            a_sb[n] = side[:].rearrange("p (t s) -> p t s", t=PACK)
+            queue = nc.sync if n < 2 else nc.sync
+            queue.dma_start(out=a_sb[n], in_=a_rows[:, :, first : first + width])
 
-        def prepare_pair(q):
+        def gather_pair(q):
             cols = offs_sb[:, q * PAIR // LIST_COLS : (q + 1) * PAIR // LIST_COLS]
-            g_words[q] = keep.tile([P, PAIR], U32, name="g_words%d" % q, align_bytes=64)
-            g_scales[q] = keep.tile([P, PAIR], U8, name="g_scales%d" % q, align_bytes=64)
+            g_words[q] = stream.tile([P, PAIR], U32, name="g_words", align_bytes=64, bufs=2)
+            g_scales[q] = stream.tile([P, PAIR], U8, name="g_scales", align_bytes=64, bufs=2)
             nc.vector.tensor_copy(g_words[q][:], dy_w[:].bitcast(U32).indirect(cols))
             nc.vector.tensor_copy(g_scales[q][:], dy_s[:].bitcast(U8).indirect(cols))
+
+        def gate_pair(q):
             gate_bank = psum.tile([P, PAIR], F32, name="gate_bank")
             for u in range(2):
                 e = 2 * q + u
@@ -74,7 +96,7 @@ def tile_moe_bdx_mlp_relu_kernel(
                 )
             n = [first <= q * PAIR < first + width for first, width in A_CHUNKS].index(True)
             first = q * PAIR - A_CHUNKS[n][0]
-            gated[q] = stream.tile([P, PACK, PAIR], F32, name="gated")
+            gated[q] = stream.tile([P, PACK, PAIR], F32, name="gated", bufs=3)
             nc.vector.scalar_tensor_tensor(
                 out=gated[q][:],
                 in0=a_sb[n][:, :, first : first + PAIR],
@@ -84,22 +106,24 @@ def tile_moe_bdx_mlp_relu_kernel(
                 op1=ALU.mult,
             )
 
+        def round_w2(e):
+            w2_bf[e] = stream.tile([P, H * PACK], BF16, name="w2_bf", align_bytes=64, bufs=4)
+            nc.scalar.copy(
+                out=w2_bf[e][:].rearrange("p (t m j) -> p m j t", t=PACK, j=PACK),
+                in_=w2_raw[e][:].rearrange("p j (m t) -> p m j t", t=PACK),
+            )
+
         def first_product(e):
             q, u = divmod(e, 2)
             slots = slice(u * C, (u + 1) * C)
-            w2_bf = stream.tile([P, H * PACK], BF16, name="w2_bf", align_bytes=64)
-            nc.scalar.copy(
-                out=w2_bf[:].rearrange("p (t m j) -> p m j t", t=PACK, j=PACK),
-                in_=w2_raw[e][:].rearrange("p j (m t) -> p m j t", t=PACK),
-            )
-            w2_codes = stream.tile([P, H], U32, name="w2_codes", align_bytes=64)
-            w2_scales = stream.tile([P, H], U8, name="w2_scales", align_bytes=64)
-            nc.vector.quantize_mx(out=w2_codes[:].bitcast(FP8X4), scales=w2_scales[:], in_=w2_bf[:])
-            dh = psum.tile([P, PACK, C], F32, name="dh", bufs=3)
+            w2_codes = stream.tile([P, H], U32, name="w2_codes", align_bytes=64, bufs=3)
+            w2_scales = stream.tile([P, H], U8, name="w2_scales", align_bytes=64, bufs=3)
+            nc.vector.quantize_mx(out=w2_codes[:].bitcast(FP8X4), scales=w2_scales[:], in_=w2_bf[e][:])
+            dh[e] = psum.tile([P, PACK, C], F32, name="dh", bufs=3)
             for t in range(PACK):
                 cols = slice(t * P, (t + 1) * P)
                 nc.tensor.matmul_mx(
-                    out=dh[:, t, :],
+                    out=dh[e][:, t, :],
                     lhsT=w2_codes[:, cols].bitcast(FP8X4),
                     lhsT_scale=w2_scales[:, cols],
                     rhs=g_words[q][:, slots].bitcast(FP8X4),
@@ -107,89 +131,146 @@ def tile_moe_bdx_mlp_relu_kernel(
                     start=True,
                     stop=True,
                 )
-            da_bf = stream.tile([P, C * PACK], BF16, name="da_bf", align_bytes=64)
+
+        def round_da(e):
+            q, u = divmod(e, 2)
+            da_bf[e] = w2_bf[e + 1][:, 0 : C * PACK] if e + 1 < E else w2_bf[e][:, C * PACK : 2 * C * PACK]
             nc.vector.tensor_tensor(
-                out=da_bf[:].rearrange("p (c i t) -> p c t i", i=4, t=PACK),
-                in0=dh[:].rearrange("p t (c i) -> p c t i", i=4),
-                in1=gated[q][:, :, slots].rearrange("p t (c i) -> p c t i", i=4),
+                out=da_bf[e][:].rearrange("p (c i t) -> p c t i", i=4, t=PACK),
+                in0=dh[e][:].rearrange("p t (c i) -> p c t i", i=4),
+                in1=gated[q][:, :, u * C : (u + 1) * C].rearrange("p t (c i) -> p c t i", i=4),
                 op=ALU.mult,
             )
+
+        def quantize_da(e):
             da_codes[e] = keep.tile([P, C], U32, name="da_codes%d" % e, align_bytes=64)
             da_scales[e] = keep.tile([P, C], U8, name="da_scales%d" % e, align_bytes=64)
-            nc.vector.quantize_mx(out=da_codes[e][:].bitcast(FP8X4), scales=da_scales[e][:], in_=da_bf[:])
+            nc.vector.quantize_mx(out=da_codes[e][:].bitcast(FP8X4), scales=da_scales[e][:], in_=da_bf[e][:])
 
-        def second_product(e):
+        def round_w1(e, h):
+            on_vector = h == 0 and e % 2 == 0
+            cast = nc.vector.tensor_copy if on_vector else nc.scalar.copy
+            w1_bf[e, h] = stream.tile([P, P * PACK], BF16, name="w1_bf", align_bytes=64, bufs=12)
+            cast(
+                out=w1_bf[e, h][:].rearrange("p (c i j) -> p c j i", i=4, j=PACK),
+                in_=w1_raw[e, h].rearrange("p j (c i) -> p c j i", i=4),
+            )
+
+        def second_product(e, h):
             q, u = divmod(e, 2)
-            w1_bf = stream.tile([P, K * PACK], BF16, name="w1_bf", align_bytes=64)
-            for h, cast in ((0, nc.vector.tensor_copy), (1, nc.scalar.copy)):
-                cast(
-                    out=w1_bf[:, h * P * PACK : (h + 1) * P * PACK].rearrange("p (c i j) -> p c j i", i=4, j=PACK),
-                    in_=w1_raw[e][:, :, h * P : (h + 1) * P].rearrange("p j (c i) -> p c j i", i=4),
-                )
-            w1_codes = stream.tile([P, K], U32, name="w1_codes", align_bytes=64)
-            w1_scales = stream.tile([P, K], U8, name="w1_scales", align_bytes=64)
-            nc.vector.quantize_mx(out=w1_codes[:].bitcast(FP8X4), scales=w1_scales[:], in_=w1_bf[:])
+            w1_codes = stream.tile([P, P], U32, name="w1_codes", align_bytes=64, bufs=4)
+            w1_scales = stream.tile([P, P], U8, name="w1_scales", align_bytes=64, bufs=4)
+            nc.vector.quantize_mx(out=w1_codes[:].bitcast(FP8X4), scales=w1_scales[:], in_=w1_bf[e, h][:])
             if u == 0:
-                dx_banks[q] = psum.tile([P, K // P, PAIR], F32, name="dx_bank")
-            for h in range(K // P):
-                cols = slice(h * P, (h + 1) * P)
-                nc.tensor.matmul_mx(
-                    out=dx_banks[q][:, h, u * C : (u + 1) * C],
-                    lhsT=w1_codes[:, cols].bitcast(FP8X4),
-                    lhsT_scale=w1_scales[:, cols],
-                    rhs=da_codes[e][:].bitcast(FP8X4),
-                    rhs_scale=da_scales[e][:],
-                    start=True,
-                    stop=True,
-                )
-            if u == 1:
-                nc.scalar.copy(out=dx[:, :, q * PAIR : (q + 1) * PAIR], in_=dx_banks[q][:])
+                dx_banks[q, h] = psum.tile([P, PAIR], F32, name="dx_bank", bufs=3)
+            nc.tensor.matmul_mx(
+                out=dx_banks[q, h][:, u * C : (u + 1) * C],
+                lhsT=w1_codes[:].bitcast(FP8X4),
+                lhsT_scale=w1_scales[:],
+                rhs=da_codes[e][:].bitcast(FP8X4),
+                rhs_scale=da_scales[e][:],
+                start=True,
+                stop=True,
+            )
 
+        def keep_dx(q, h):
+            move = nc.vector.tensor_copy if h == 0 or 2 * q < WHOLE_W1 else nc.scalar.copy
+            move(out=dx[:, h, q * PAIR : (q + 1) * PAIR], in_=dx_banks[q, h][:])
+
+        half = T // 2
+        picked = [keep.tile([P, T], F32, name="picked%d" % r) for r in range(3)]
+        two = keep.tile([P, T], F32, name="two")
+        three = [keep.tile([P, T], F32, name="three%d" % h) for h in range(2)]
+
+        def pick(h, r, first, count):
+            cols = pos_sb[r][:, first // LIST_COLS : (first + count) // LIST_COLS]
+            nc.vector.tensor_copy(picked[r][:, first : first + count], dx[:, h, :].indirect(cols))
+
+        def add_two(first, count):
+            tokens = slice(first, first + count)
+            nc.vector.tensor_tensor(out=two[:, tokens], in0=picked[0][:, tokens], in1=picked[1][:, tokens], op=ALU.add)
+
+        def add_third(h, first):
+            tokens = slice(first, first + half)
+            nc.vector.tensor_tensor(out=three[h][:, tokens], in0=two[:, tokens], in1=picked[2][:, tokens], op=ALU.add)
+            nc.sync.dma_start(out=out[h * P : (h + 1) * P, tokens], in_=three[h][:, tokens])
+
+        def combine_steps(h):
+            return [
+                lambda: pick(h, 0, 0, half),
+                lambda: pick(h, 0, half, half),
+                lambda: pick(h, 1, 0, half),
+                lambda: pick(h, 1, half, half),
+                lambda: pick(h, 2, 0, half),
+                lambda: add_two(0, T),
+                lambda: pick(h, 2, half, half),
+                lambda: add_third(h, 0),
+                lambda: add_third(h, half),
+            ]
+
+        make_identity(nc, ident[:])
         nc.vector.memset(dy_s[:], 0)
+        nc.sync.dma_start(out=gate_rows[:], in_=gate.rearrange("r (e c) -> (r e) c", c=C)[0:P, :])
         load_w2(0)
         nc.sync.dma_start(offs_sb[:], offs)
         nc.sync.dma_start(out=dy_w[:], in_=dy_words[0].rearrange("p t d -> p (t d)").bitcast(I32))
         for r in range(4):
-            if r == 2:
-                load_w2(1)
             nc.sync.dma_start(out=dy_s[r:P:32, :], in_=dy_scales[0].bitcast(I32)[r:16:4, :])
-        nc.sync.dma_start(out=gate_rows[:], in_=gate.rearrange("r (e c) -> (r e) c", c=C)[0:P, :])
-        make_identity(nc, ident[:])
-        gate_turned = psum.tile([P, P], F32, name="gate_turned", bufs=1)
+        gate_turned = psum.tile([P, P], F32, name="gate_bank")
         nc.tensor.transpose(gate_turned[:], gate_rows[:], ident[:])
         nc.vector.tensor_copy(out=gate_cols[:], in_=gate_turned[:, 0:32])
 
-        for step in range(E + W1_LAG):
-            if step < E:
-                if step > 1:
-                    load_w2(step)
-                for n, (first, width) in enumerate(A_CHUNKS):
-                    if first == step * C:
-                        load_a(n)
-            if step == 2:
+        w1_loads = {step: [] for step in range(3 * E)}
+        for e in range(E - W1_LAG):
+            w1_loads[e + W1_LAG].append((e, (0, 1) if e < WHOLE_W1 else (0,)))
+        late = [(e, (0, 1) if e < WHOLE_W1 else (0,)) for e in range(E - W1_LAG, E)]
+        late += [(e, (1,)) for e in range(WHOLE_W1, E)]
+        per_step = 2
+        for n, item in enumerate(late):
+            w1_loads[E + n // per_step].append(item)
+        last_step = E + (len(late) - 1) // per_step + 2
+
+        rounded, multiplied, kept = [], [], []
+        first_combine = combine_steps(0)
+        for step in range(last_step + 1):
+            if 0 < step < E:
+                load_w2(step)
+            for n, (first, width) in enumerate(A_CHUNKS):
+                if step == (0, 2, 5, 9, 13)[n]:
+                    load_a(n)
+            if step == 3:
                 for r, pos in enumerate((pos1, pos2, pos3)):
                     nc.sync.dma_start(pos_sb[r][:], pos)
-            if step >= W1_LAG:
-                load_w1(step - W1_LAG)
+            for e, halves in w1_loads[step]:
+                load_w1(e, halves)
             if step < E:
+                round_w2(step)
                 if step % 2 == 0:
-                    prepare_pair(step // 2)
-                first_product(step)
-            if step >= W1_LAG:
-                second_product(step - W1_LAG)
-
-        half = T // 2
-        for h in range(K // P):
-            picked = [stream.tile([P, T], F32, name="picked%d" % r, bufs=2) for r in range(3)]
-            window = dx[:, h, :]
-            two = stream.tile([P, T], F32, name="two", bufs=2)
-            three = stream.tile([P, T], F32, name="three", bufs=2)
-            nc.vector.tensor_copy(picked[0][:], window.indirect(pos_sb[0][:]))
-            nc.vector.tensor_copy(picked[1][:], window.indirect(pos_sb[1][:]))
-            nc.vector.tensor_copy(picked[2][:, 0:half], window.indirect(pos_sb[2][:, 0 : half // LIST_COLS]))
-            nc.vector.tensor_tensor(out=two[:], in0=picked[0][:], in1=picked[1][:], op=ALU.add)
-            nc.vector.tensor_copy(picked[2][:, half:T], window.indirect(pos_sb[2][:, half // LIST_COLS : T // LIST_COLS]))
-            for first in (0, half):
-                tokens = slice(first, first + half)
-                nc.vector.tensor_tensor(out=three[:, tokens], in0=two[:, tokens], in1=picked[2][:, tokens], op=ALU.add)
-                nc.sync.dma_start(out=out[h * P : (h + 1) * P, tokens], in_=three[:, tokens])
+                    gather_pair(step // 2)
+            if 1 <= step <= E:
+                first_product(step - 1)
+            to_multiply, rounded = rounded, []
+            to_keep, multiplied = multiplied, []
+            for e, halves in w1_loads[step]:
+                for h in halves:
+                    round_w1(e, h)
+                    rounded.append((e, h))
+            if 2 <= step <= E + 1:
+                round_da(step - 2)
+            if step < E and step % 2 == 1:
+                gate_pair(step // 2)
+            for e, h in to_multiply:
+                second_product(e, h)
+                if e % 2 == 1:
+                    multiplied.append((e // 2, h))
+            if 2 <= step <= E + 1:
+                quantize_da(step - 2)
+            for q, h in to_keep:
+                keep_dx(q, h)
+                kept.append((q, h))
+            if sum(h == 0 for q, h in kept) == E // 2:
+                for work in first_combine[:2]:
+                    work()
+                first_combine = first_combine[2:]
+        for work in first_combine + combine_steps(1):
+            work()

@@ -16,14 +16,17 @@ U16 = mybir.dt.uint16
 U8 = mybir.dt.uint8
 FP8X4 = mybir.dt.float8_e4m3fn_x4
 ALU = mybir.AluOpType
+COPY = mybir.ActivationFunctionType.Copy
 
 P = 128
 PACK = 4
 PAIR = 2 * C
 LIST_COLS = 16
-W1_LAG = 6
-WHOLE_W1 = 6
-A_CHUNKS = [(0, 256), (256, 512), (768, 512), (1280, 512), (1792, 512)]
+W1_LAG = 5
+DA_LAG = 2
+LOAD_RING = 16
+A_CHUNKS = [(0, 256, 0), (256, 512, 2), (768, 512, 5), (1280, 512, 9), (1792, 512, 13)]
+TOKEN_CUTS = [(0, 480), (480, 288)]
 
 
 def tile_moe_bdx_mlp_relu_kernel(
@@ -42,235 +45,174 @@ def tile_moe_bdx_mlp_relu_kernel(
         dy_s = keep.tile([P, T // 4], I32, name="dy_s")
         ident = keep.tile([P, P], F32, name="ident")
         gate_rows = keep.tile([P, C], F32, name="gate_rows")
-        gate_cols = keep.tile([P, 32], F32, name="gate_cols")
-        dx = keep.tile([P, K // P, S], F32, name="dx")
+        gate_cols = keep.tile([P, E], F32, name="gate_cols")
+        dx = [keep.tile([P, S], F32, name="dx%d" % h) for h in range(K // P)]
         a_sb = {}
         a_rows = a.rearrange("(p t) s -> p t s", t=PACK)
 
-        w2_raw, w2_bf, dh, da_bf, da_codes, da_scales = {}, {}, {}, {}, {}, {}
-        w1_raw, w1_bf, dx_banks, gated, g_words, g_scales = {}, {}, {}, {}, {}, {}
+        w2_raw, w2_bf, dh_slots, dh, da_bf, da_codes, da_scales = {}, {}, {}, {}, {}, {}, {}
+        w1_raw, w1_bf, w1_codes, w1_scales, dx_banks, g_words, g_scales = {}, {}, {}, {}, {}, {}, {}
+
+        def interleave(copy, rounded, raw):
+            copy(
+                out=rounded.rearrange("p (c i j) -> p c j i", i=4, j=PACK),
+                in_=raw.rearrange("p j (c i) -> p c j i", i=4),
+            )
 
         def load_w2(e):
-            w2_raw[e] = stream.tile([P, PACK, H], F32, name="w2_raw", bufs=6)
-            nc.sync.dma_start(out=w2_raw[e][:], in_=w2[e].rearrange("(p j) i -> p j i", j=PACK))
+            w2_raw[e] = stream.tile([P, PACK * H], F32, name="loaded", align_bytes=64, bufs=LOAD_RING)
+            nc.sync.dma_start(out=w2_raw[e][:], in_=w2[e].rearrange("(p j) i -> p (j i)", j=PACK))
 
-        def load_w1(e, halves):
-            rows = w1[e].rearrange("(p j) k -> p j k", j=PACK)
-            if len(halves) == 2:
-                if e % 2 == 0:
-                    side = stream.tile([P, 2 * PACK * K], F32, name="side", bufs=3)
-                    both = side[:].rearrange("p (e j k) -> p e j k", e=2, j=PACK)
-                    nc.sync.dma_start(
-                        out=side[:].rearrange("p (e r) -> p e r", e=2),
-                        in_=w1[e : e + 2].rearrange("e (p j) k -> p e (j k)", j=PACK),
-                    )
-                    for u in range(2):
-                        for h in halves:
-                            w1_raw[e + u, h] = both[:, u, :, h * P : (h + 1) * P]
-            else:
-                h = halves[0]
-                part = stream.tile([P, PACK, P], F32, name="w1_part", bufs=12)
-                nc.sync.dma_start(out=part[:], in_=rows[:, :, h * P : (h + 1) * P])
-                w1_raw[e, h] = part[:]
+        def load_w1(e):
+            w1_raw[e] = stream.tile([P, PACK * K], F32, name="loaded", align_bytes=64, bufs=LOAD_RING)
+            nc.sync.dma_start(out=w1_raw[e][:], in_=w1[e].rearrange("(p j) k -> p (j k)", j=PACK))
 
         def load_a(n):
-            first, width = A_CHUNKS[n]
-            side = stream.tile([P, PACK * width], F32, name="side", bufs=3)
-            a_sb[n] = side[:].rearrange("p (t s) -> p t s", t=PACK)
-            queue = nc.sync if n < 2 else nc.sync
-            queue.dma_start(out=a_sb[n], in_=a_rows[:, :, first : first + width])
+            first, width, step = A_CHUNKS[n]
+            a_sb[n] = stream.tile([P, PACK, width], F32, name="loaded", align_bytes=64, bufs=LOAD_RING)
+            nc.sync.dma_start(out=a_sb[n][:], in_=a_rows[:, :, first : first + width])
 
-        def gather_pair(q):
-            cols = offs_sb[:, q * PAIR // LIST_COLS : (q + 1) * PAIR // LIST_COLS]
-            g_words[q] = stream.tile([P, PAIR], U32, name="g_words", align_bytes=64, bufs=2)
-            g_scales[q] = stream.tile([P, PAIR], U8, name="g_scales", align_bytes=64, bufs=2)
-            nc.vector.tensor_copy(g_words[q][:], dy_w[:].bitcast(U32).indirect(cols))
-            nc.vector.tensor_copy(g_scales[q][:], dy_s[:].bitcast(U8).indirect(cols))
-
-        def gate_pair(q):
-            gate_bank = psum.tile([P, PAIR], F32, name="gate_bank")
-            for u in range(2):
-                e = 2 * q + u
-                nc.tensor.transpose(
-                    gate_bank[:, u * C : (u + 1) * C], gate_cols[:, e : e + 1].to_broadcast([P, P]), ident[:]
-                )
-            n = [first <= q * PAIR < first + width for first, width in A_CHUNKS].index(True)
-            first = q * PAIR - A_CHUNKS[n][0]
-            gated[q] = stream.tile([P, PACK, PAIR], F32, name="gated", bufs=3)
-            nc.vector.scalar_tensor_tensor(
-                out=gated[q][:],
-                in0=a_sb[n][:, :, first : first + PAIR],
-                scalar=0.0,
-                in1=gate_bank[:].unsqueeze(1).to_broadcast([P, PACK, PAIR]),
-                op0=ALU.is_gt,
-                op1=ALU.mult,
-            )
+        def gather(e):
+            cols = offs_sb[:, e * C // LIST_COLS : (e + 1) * C // LIST_COLS]
+            g_words[e] = stream.tile([P, C], U32, name="g_words", align_bytes=64, bufs=2)
+            g_scales[e] = stream.tile([P, C], U8, name="g_scales", align_bytes=64, bufs=2)
+            nc.vector.tensor_copy(g_words[e][:], dy_w[:].bitcast(U32).indirect(cols))
+            nc.vector.tensor_copy(g_scales[e][:], dy_s[:].bitcast(U8).indirect(cols))
 
         def round_w2(e):
             w2_bf[e] = stream.tile([P, H * PACK], BF16, name="w2_bf", align_bytes=64, bufs=4)
-            nc.scalar.copy(
-                out=w2_bf[e][:].rearrange("p (t m j) -> p m j t", t=PACK, j=PACK),
-                in_=w2_raw[e][:].rearrange("p j (m t) -> p m j t", t=PACK),
-            )
+            interleave(nc.scalar.copy, w2_bf[e][:], w2_raw[e][:].rearrange("p (j i) -> p j i", j=PACK))
 
         def first_product(e):
-            q, u = divmod(e, 2)
-            slots = slice(u * C, (u + 1) * C)
             w2_codes = stream.tile([P, H], U32, name="w2_codes", align_bytes=64, bufs=3)
             w2_scales = stream.tile([P, H], U8, name="w2_scales", align_bytes=64, bufs=3)
             nc.vector.quantize_mx(out=w2_codes[:].bitcast(FP8X4), scales=w2_scales[:], in_=w2_bf[e][:])
-            dh[e] = psum.tile([P, PACK, C], F32, name="dh", bufs=3)
-            for t in range(PACK):
-                cols = slice(t * P, (t + 1) * P)
-                nc.tensor.matmul_mx(
-                    out=dh[e][:, t, :],
-                    lhsT=w2_codes[:, cols].bitcast(FP8X4),
-                    lhsT_scale=w2_scales[:, cols],
-                    rhs=g_words[q][:, slots].bitcast(FP8X4),
-                    rhs_scale=g_scales[q][:, slots],
-                    start=True,
-                    stop=True,
-                )
-
-        def round_da(e):
-            q, u = divmod(e, 2)
-            da_bf[e] = w2_bf[e + 1][:, 0 : C * PACK] if e + 1 < E else w2_bf[e][:, C * PACK : 2 * C * PACK]
-            nc.vector.tensor_tensor(
-                out=da_bf[e][:].rearrange("p (c i t) -> p c t i", i=4, t=PACK),
-                in0=dh[e][:].rearrange("p t (c i) -> p c t i", i=4),
-                in1=gated[q][:, :, u * C : (u + 1) * C].rearrange("p t (c i) -> p c t i", i=4),
-                op=ALU.mult,
-            )
-
-        def quantize_da(e):
-            da_codes[e] = keep.tile([P, C], U32, name="da_codes%d" % e, align_bytes=64)
-            da_scales[e] = keep.tile([P, C], U8, name="da_scales%d" % e, align_bytes=64)
-            nc.vector.quantize_mx(out=da_codes[e][:].bitcast(FP8X4), scales=da_scales[e][:], in_=da_bf[e][:])
-
-        def round_w1(e, h):
-            on_vector = h == 0 and e % 2 == 0
-            cast = nc.vector.tensor_copy if on_vector else nc.scalar.copy
-            w1_bf[e, h] = stream.tile([P, P * PACK], BF16, name="w1_bf", align_bytes=64, bufs=12)
-            cast(
-                out=w1_bf[e, h][:].rearrange("p (c i j) -> p c j i", i=4, j=PACK),
-                in_=w1_raw[e, h].rearrange("p j (c i) -> p c j i", i=4),
-            )
-
-        def second_product(e, h):
-            q, u = divmod(e, 2)
-            w1_codes = stream.tile([P, P], U32, name="w1_codes", align_bytes=64, bufs=4)
-            w1_scales = stream.tile([P, P], U8, name="w1_scales", align_bytes=64, bufs=4)
-            nc.vector.quantize_mx(out=w1_codes[:].bitcast(FP8X4), scales=w1_scales[:], in_=w1_bf[e, h][:])
-            if u == 0:
-                dx_banks[q, h] = psum.tile([P, PAIR], F32, name="dx_bank", bufs=3)
+            dh_slots[e] = psum.tile([P, H], F32, name="dh_slots", bufs=3)
             nc.tensor.matmul_mx(
-                out=dx_banks[q, h][:, u * C : (u + 1) * C],
-                lhsT=w1_codes[:].bitcast(FP8X4),
-                lhsT_scale=w1_scales[:],
-                rhs=da_codes[e][:].bitcast(FP8X4),
-                rhs_scale=da_scales[e][:],
+                out=dh_slots[e][:],
+                lhsT=g_words[e][:].bitcast(FP8X4),
+                lhsT_scale=g_scales[e][:],
+                rhs=w2_codes[:].bitcast(FP8X4),
+                rhs_scale=w2_scales[:],
                 start=True,
                 stop=True,
             )
 
-        def keep_dx(q, h):
-            move = nc.vector.tensor_copy if h == 0 or 2 * q < WHOLE_W1 else nc.scalar.copy
-            move(out=dx[:, h, q * PAIR : (q + 1) * PAIR], in_=dx_banks[q, h][:])
+        def gate_and_turn(e):
+            staged = w2_raw[min(e + 1, E - 1)][:, (e % 2) * H : (e % 2 + 1) * H]
+            nc.scalar.activation(
+                out=staged.rearrange("p (t m) -> p t m", t=PACK),
+                in_=dh_slots[e][:].rearrange("p (m t) -> p t m", t=PACK),
+                func=COPY,
+                scale=gate_cols[:, e : e + 1],
+            )
+            dh[e] = psum.tile([P, PACK, C], F32, name="dh", bufs=3)
+            for t in range(PACK):
+                nc.tensor.transpose(dh[e][:, t, :], staged[:, t * P : (t + 1) * P], ident[:])
 
-        half = T // 2
-        picked = [keep.tile([P, T], F32, name="picked%d" % r) for r in range(3)]
-        two = keep.tile([P, T], F32, name="two")
-        three = [keep.tile([P, T], F32, name="three%d" % h) for h in range(2)]
+        def round_da(e):
+            n = [first <= e * C < first + width for first, width, step in A_CHUNKS].index(True)
+            first = e * C - A_CHUNKS[n][0]
+            host = min(e + DA_LAG, E - 1)
+            da_bf[e] = w2_bf[host][:, (e % PACK) * C * PACK : (e % PACK + 1) * C * PACK]
+            nc.vector.scalar_tensor_tensor(
+                out=da_bf[e].rearrange("p (s t) -> p s t", t=PACK),
+                in0=a_sb[n][:, :, first : first + C].rearrange("p t s -> p s t"),
+                scalar=0.0,
+                in1=dh[e][:].rearrange("p t s -> p s t"),
+                op0=ALU.is_gt,
+                op1=ALU.mult,
+            )
 
-        def pick(h, r, first, count):
-            cols = pos_sb[r][:, first // LIST_COLS : (first + count) // LIST_COLS]
-            nc.vector.tensor_copy(picked[r][:, first : first + count], dx[:, h, :].indirect(cols))
+        def quantize_da(e):
+            da_codes[e] = stream.tile([P, C], U32, name="da_codes", align_bytes=64, bufs=W1_LAG + 2)
+            da_scales[e] = stream.tile([P, C], U8, name="da_scales", align_bytes=64, bufs=W1_LAG + 2)
+            nc.vector.quantize_mx(out=da_codes[e][:].bitcast(FP8X4), scales=da_scales[e][:], in_=da_bf[e])
 
-        def add_two(first, count):
-            tokens = slice(first, first + count)
-            nc.vector.tensor_tensor(out=two[:, tokens], in0=picked[0][:, tokens], in1=picked[1][:, tokens], op=ALU.add)
+        def round_w1(e):
+            if e + W1_LAG < E:
+                w1_bf[e] = w2_raw[e + W1_LAG][:, 2 * H : 3 * H].bitcast(BF16)
+            else:
+                w1_bf[e] = stream.tile([P, K * PACK], BF16, name="w1_bf", align_bytes=64, bufs=3)[:]
+            copy = nc.scalar.copy if e + W1_LAG >= E and e % 2 == 0 else nc.vector.tensor_copy
+            interleave(copy, w1_bf[e], w1_raw[e][:].rearrange("p (j k) -> p j k", j=PACK))
 
-        def add_third(h, first):
-            tokens = slice(first, first + half)
-            nc.vector.tensor_tensor(out=three[h][:, tokens], in0=two[:, tokens], in1=picked[2][:, tokens], op=ALU.add)
-            nc.sync.dma_start(out=out[h * P : (h + 1) * P, tokens], in_=three[h][:, tokens])
+        def quantize_w1(e):
+            w1_codes[e] = stream.tile([P, K], U32, name="w1_codes", align_bytes=64, bufs=4)
+            w1_scales[e] = stream.tile([P, K], U8, name="w1_scales", align_bytes=64, bufs=4)
+            nc.vector.quantize_mx(out=w1_codes[e][:].bitcast(FP8X4), scales=w1_scales[e][:], in_=w1_bf[e])
 
-        def combine_steps(h):
-            return [
-                lambda: pick(h, 0, 0, half),
-                lambda: pick(h, 0, half, half),
-                lambda: pick(h, 1, 0, half),
-                lambda: pick(h, 1, half, half),
-                lambda: pick(h, 2, 0, half),
-                lambda: add_two(0, T),
-                lambda: pick(h, 2, half, half),
-                lambda: add_third(h, 0),
-                lambda: add_third(h, half),
-            ]
+        def second_product(e):
+            q, u = divmod(e, 2)
+            if u == 0:
+                dx_banks[q] = psum.tile([P, K // P, PAIR], F32, name="dx_bank", bufs=2)
+            for h in range(K // P):
+                cols = slice(h * P, (h + 1) * P)
+                nc.tensor.matmul_mx(
+                    out=dx_banks[q][:, h, u * C : (u + 1) * C],
+                    lhsT=w1_codes[e][:, cols].bitcast(FP8X4),
+                    lhsT_scale=w1_scales[e][:, cols],
+                    rhs=da_codes[e][:].bitcast(FP8X4),
+                    rhs_scale=da_scales[e][:],
+                    start=True,
+                    stop=True,
+                )
+            if u == 1:
+                for h in range(K // P):
+                    nc.scalar.copy(out=dx[h][:, q * PAIR : (q + 1) * PAIR], in_=dx_banks[q][:, h, :])
 
         make_identity(nc, ident[:])
+        nc.gpsimd.memset(gate_rows[:], 0.0)
         nc.vector.memset(dy_s[:], 0)
-        nc.sync.dma_start(out=gate_rows[:], in_=gate.rearrange("r (e c) -> (r e) c", c=C)[0:P, :])
         load_w2(0)
-        nc.sync.dma_start(offs_sb[:], offs)
         nc.sync.dma_start(out=dy_w[:], in_=dy_words[0].rearrange("p t d -> p (t d)").bitcast(I32))
+        nc.sync.dma_start(offs_sb[:], offs)
         for r in range(4):
             nc.sync.dma_start(out=dy_s[r:P:32, :], in_=dy_scales[0].bitcast(I32)[r:16:4, :])
-        gate_turned = psum.tile([P, P], F32, name="gate_bank")
-        nc.tensor.transpose(gate_turned[:], gate_rows[:], ident[:])
-        nc.vector.tensor_copy(out=gate_cols[:], in_=gate_turned[:, 0:32])
+        load_w2(1)
+        nc.sync.dma_start(out=gate_rows[0:E, :], in_=gate[0].rearrange("(e c) -> e c", c=C))
+        gate_turned = psum.tile([P, PACK, C], F32, name="dh", bufs=3)
+        nc.tensor.transpose(gate_turned[:, 0, :], gate_rows[:], ident[:])
+        nc.scalar.copy(out=gate_cols[:], in_=gate_turned[:, 0, 0:E])
 
-        w1_loads = {step: [] for step in range(3 * E)}
-        for e in range(E - W1_LAG):
-            w1_loads[e + W1_LAG].append((e, (0, 1) if e < WHOLE_W1 else (0,)))
-        late = [(e, (0, 1) if e < WHOLE_W1 else (0,)) for e in range(E - W1_LAG, E)]
-        late += [(e, (1,)) for e in range(WHOLE_W1, E)]
-        per_step = 2
-        for n, item in enumerate(late):
-            w1_loads[E + n // per_step].append(item)
-        last_step = E + (len(late) - 1) // per_step + 2
-
-        rounded, multiplied, kept = [], [], []
-        first_combine = combine_steps(0)
-        for step in range(last_step + 1):
-            if 0 < step < E:
+        for step in range(E + W1_LAG):
+            late = step - W1_LAG
+            if 1 < step < E:
                 load_w2(step)
-            for n, (first, width) in enumerate(A_CHUNKS):
-                if step == (0, 2, 5, 9, 13)[n]:
+            for n, (first, width, load_step) in enumerate(A_CHUNKS):
+                if step == load_step:
                     load_a(n)
             if step == 3:
                 for r, pos in enumerate((pos1, pos2, pos3)):
                     nc.sync.dma_start(pos_sb[r][:], pos)
-            for e, halves in w1_loads[step]:
-                load_w1(e, halves)
+            if late >= 0:
+                load_w1(late)
             if step < E:
                 round_w2(step)
-                if step % 2 == 0:
-                    gather_pair(step // 2)
+                gather(step)
+                first_product(step)
             if 1 <= step <= E:
-                first_product(step - 1)
-            to_multiply, rounded = rounded, []
-            to_keep, multiplied = multiplied, []
-            for e, halves in w1_loads[step]:
-                for h in halves:
-                    round_w1(e, h)
-                    rounded.append((e, h))
-            if 2 <= step <= E + 1:
-                round_da(step - 2)
-            if step < E and step % 2 == 1:
-                gate_pair(step // 2)
-            for e, h in to_multiply:
-                second_product(e, h)
-                if e % 2 == 1:
-                    multiplied.append((e // 2, h))
-            if 2 <= step <= E + 1:
-                quantize_da(step - 2)
-            for q, h in to_keep:
-                keep_dx(q, h)
-                kept.append((q, h))
-            if sum(h == 0 for q, h in kept) == E // 2:
-                for work in first_combine[:2]:
-                    work()
-                first_combine = first_combine[2:]
-        for work in first_combine + combine_steps(1):
-            work()
+                gate_and_turn(step - 1)
+            if late >= 0:
+                round_w1(late)
+            if DA_LAG <= step < E + DA_LAG:
+                round_da(step - DA_LAG)
+            if late >= 0:
+                quantize_w1(late)
+            if DA_LAG <= step < E + DA_LAG:
+                quantize_da(step - DA_LAG)
+            if late >= 0:
+                second_product(late)
+
+        for h in range(K // P):
+            one = keep.tile([P, T], F32, name="one%d" % h)
+            two = keep.tile([P, T], F32, name="two%d" % h)
+            three = keep.tile([P, T], F32, name="three%d" % h)
+            nc.vector.tensor_copy(one[:], dx[h][:].indirect(pos_sb[0][:]))
+            for r, before, after in ((1, one, two), (2, two, three)):
+                for first, count in TOKEN_CUTS:
+                    tokens = slice(first, first + count)
+                    cols = pos_sb[r][:, first // LIST_COLS : (first + count) // LIST_COLS]
+                    nc.vector.tensor_tensor(after[:, tokens], dx[h][:].indirect(cols), before[:, tokens], ALU.add)
+                    if r == 2:
+                        nc.sync.dma_start(out=out[h * P : (h + 1) * P, tokens], in_=three[:, tokens])

@@ -22,10 +22,11 @@ P = 128
 PACK = 4
 PAIR = 2 * C
 LIST_COLS = 16
-W1_LAG = 5
 DA_LAG = 2
 LOAD_RING = 16
-A_CHUNKS = [(0, 256, 0), (256, 512, 2), (768, 512, 5), (1280, 512, 9), (1792, 512, 13)]
+SCALAR_W2 = 384
+DX_GROUPS = [(0, 2), (2, 4), (6, 4), (10, 4), (14, 3), (17, 1)]
+A_CHUNKS = [(0, 256, 1), (256, 512, 3), (768, 512, 7), (1280, 512, 11), (1792, 512, 15)]
 TOKEN_CUTS = [(0, 480), (480, 288)]
 
 
@@ -51,7 +52,10 @@ def tile_moe_bdx_mlp_relu_kernel(
         a_rows = a.rearrange("(p t) s -> p t s", t=PACK)
 
         w2_raw, w2_bf, dh_slots, dh, da_bf, da_codes, da_scales = {}, {}, {}, {}, {}, {}, {}
-        w1_raw, w1_bf, w1_codes, w1_scales, dx_banks, g_words, g_scales = {}, {}, {}, {}, {}, {}, {}
+        g_words, g_scales, w1_raw, w1_bf, dx_banks = {}, {}, {}, {}, {}
+
+        def loaded_tile():
+            return stream.tile([P, PACK * H], F32, name="loaded", align_bytes=64, bufs=LOAD_RING)
 
         def interleave(copy, rounded, raw):
             copy(
@@ -60,17 +64,13 @@ def tile_moe_bdx_mlp_relu_kernel(
             )
 
         def load_w2(e):
-            w2_raw[e] = stream.tile([P, PACK * H], F32, name="loaded", align_bytes=64, bufs=LOAD_RING)
+            w2_raw[e] = loaded_tile()
             nc.sync.dma_start(out=w2_raw[e][:], in_=w2[e].rearrange("(p j) i -> p (j i)", j=PACK))
-
-        def load_w1(e):
-            w1_raw[e] = stream.tile([P, PACK * K], F32, name="loaded", align_bytes=64, bufs=LOAD_RING)
-            nc.sync.dma_start(out=w1_raw[e][:], in_=w1[e].rearrange("(p j) k -> p (j k)", j=PACK))
 
         def load_a(n):
             first, width, step = A_CHUNKS[n]
-            a_sb[n] = stream.tile([P, PACK, width], F32, name="loaded", align_bytes=64, bufs=LOAD_RING)
-            nc.sync.dma_start(out=a_sb[n][:], in_=a_rows[:, :, first : first + width])
+            a_sb[n] = loaded_tile()[:, 0 : PACK * width].rearrange("p (t s) -> p t s", t=PACK)
+            nc.sync.dma_start(out=a_sb[n], in_=a_rows[:, :, first : first + width])
 
         def gather(e):
             cols = offs_sb[:, e * C // LIST_COLS : (e + 1) * C // LIST_COLS]
@@ -80,14 +80,20 @@ def tile_moe_bdx_mlp_relu_kernel(
             nc.vector.tensor_copy(g_scales[e][:], dy_s[:].bitcast(U8).indirect(cols))
 
         def round_w2(e):
-            w2_bf[e] = stream.tile([P, H * PACK], BF16, name="w2_bf", align_bytes=64, bufs=4)
-            interleave(nc.scalar.copy, w2_bf[e][:], w2_raw[e][:].rearrange("p (j i) -> p j i", j=PACK))
+            w2_bf[e] = stream.tile([P, H * PACK], BF16, name="rounded", align_bytes=64, bufs=3)
+            rows = w2_raw[e][:].rearrange("p (j i) -> p j i", j=PACK)
+            for copy, first, last in (
+                (nc.scalar.copy, 0, P),
+                (nc.scalar.copy, P, SCALAR_W2),
+                (nc.vector.tensor_copy, SCALAR_W2, H),
+            ):
+                interleave(copy, w2_bf[e][:, first * PACK : last * PACK], rows[:, :, first:last])
 
         def first_product(e):
-            w2_codes = stream.tile([P, H], U32, name="w2_codes", align_bytes=64, bufs=3)
-            w2_scales = stream.tile([P, H], U8, name="w2_scales", align_bytes=64, bufs=3)
+            w2_codes = stream.tile([P, H], U32, name="w_codes", align_bytes=64, bufs=4)
+            w2_scales = stream.tile([P, H], U8, name="w_scales", align_bytes=64, bufs=4)
             nc.vector.quantize_mx(out=w2_codes[:].bitcast(FP8X4), scales=w2_scales[:], in_=w2_bf[e][:])
-            dh_slots[e] = psum.tile([P, H], F32, name="dh_slots", bufs=3)
+            dh_slots[e] = psum.tile([P, H], F32, name="dh_slots", bufs=2)
             nc.tensor.matmul_mx(
                 out=dh_slots[e][:],
                 lhsT=g_words[e][:].bitcast(FP8X4),
@@ -99,22 +105,28 @@ def tile_moe_bdx_mlp_relu_kernel(
             )
 
         def gate_and_turn(e):
-            staged = w2_raw[min(e + 1, E - 1)][:, (e % 2) * H : (e % 2 + 1) * H]
+            if e + 1 < E:
+                staged = w2_raw[e + 1][:].rearrange("p (t i) -> p t i", t=PACK)[:, :, 0:P]
+            else:
+                staged = stream.tile([P, PACK, P], F32, name="last_staged", bufs=1)[:]
             nc.scalar.activation(
-                out=staged.rearrange("p (t m) -> p t m", t=PACK),
+                out=staged,
                 in_=dh_slots[e][:].rearrange("p (m t) -> p t m", t=PACK),
                 func=COPY,
                 scale=gate_cols[:, e : e + 1],
             )
-            dh[e] = psum.tile([P, PACK, C], F32, name="dh", bufs=3)
+            dh[e] = psum.tile([P, PACK, C], F32, name="dh", bufs=2)
             for t in range(PACK):
-                nc.tensor.transpose(dh[e][:, t, :], staged[:, t * P : (t + 1) * P], ident[:])
+                nc.tensor.transpose(dh[e][:, t, :], staged[:, t, :], ident[:])
 
         def round_da(e):
             n = [first <= e * C < first + width for first, width, step in A_CHUNKS].index(True)
             first = e * C - A_CHUNKS[n][0]
-            host = min(e + DA_LAG, E - 1)
-            da_bf[e] = w2_bf[host][:, (e % PACK) * C * PACK : (e % PACK + 1) * C * PACK]
+            if e + DA_LAG < E:
+                spent = (PACK - 1) * H + P
+                da_bf[e] = w2_raw[e + DA_LAG][:, spent : spent + C * PACK // 2].bitcast(BF16)
+            else:
+                da_bf[e] = stream.tile([P, C * PACK], BF16, name="last_da", align_bytes=64, bufs=DA_LAG)[:]
             nc.vector.scalar_tensor_tensor(
                 out=da_bf[e].rearrange("p (s t) -> p s t", t=PACK),
                 in0=a_sb[n][:, :, first : first + C].rearrange("p t s -> p s t"),
@@ -125,86 +137,50 @@ def tile_moe_bdx_mlp_relu_kernel(
             )
 
         def quantize_da(e):
-            da_codes[e] = stream.tile([P, C], U32, name="da_codes", align_bytes=64, bufs=W1_LAG + 2)
-            da_scales[e] = stream.tile([P, C], U8, name="da_scales", align_bytes=64, bufs=W1_LAG + 2)
+            da_codes[e] = keep.tile([P, C], U32, name="da_codes%d" % e, align_bytes=64)
+            da_scales[e] = keep.tile([P, C], U8, name="da_scales%d" % e, align_bytes=64)
             nc.vector.quantize_mx(out=da_codes[e][:].bitcast(FP8X4), scales=da_scales[e][:], in_=da_bf[e])
 
-        def round_w1(e):
-            if e + W1_LAG < E:
-                w1_bf[e] = w2_raw[e + W1_LAG][:, 2 * H : 3 * H].bitcast(BF16)
-            else:
-                w1_bf[e] = stream.tile([P, K * PACK], BF16, name="w1_bf", align_bytes=64, bufs=3)[:]
-            copy = nc.scalar.copy if e + W1_LAG >= E and e % 2 == 0 else nc.vector.tensor_copy
-            interleave(copy, w1_bf[e], w1_raw[e][:].rearrange("p (j k) -> p j k", j=PACK))
+        def load_w1(first, count):
+            raw = loaded_tile()[:, 0 : count * PACK * K]
+            nc.sync.dma_start(
+                out=raw.rearrange("p (u r) -> p u r", u=count),
+                in_=w1[first : first + count].rearrange("u (p j) k -> p u (j k)", j=PACK),
+            )
+            for u in range(count):
+                w1_raw[first + u] = raw[:, u * PACK * K : (u + 1) * PACK * K].rearrange("p (j k) -> p j k", j=PACK)
 
-        def quantize_w1(e):
-            w1_codes[e] = stream.tile([P, K], U32, name="w1_codes", align_bytes=64, bufs=4)
-            w1_scales[e] = stream.tile([P, K], U8, name="w1_scales", align_bytes=64, bufs=4)
-            nc.vector.quantize_mx(out=w1_codes[e][:].bitcast(FP8X4), scales=w1_scales[e][:], in_=w1_bf[e])
+        def round_w1(e):
+            w1_bf[e] = stream.tile([P, PACK * K], BF16, name="w1_bf", align_bytes=64, bufs=5)
+            on_vector = 0 if e % 4 == 1 else K
+            if on_vector > 0:
+                interleave(nc.vector.tensor_copy, w1_bf[e][:, 0 : PACK * on_vector], w1_raw[e][:, :, 0:on_vector])
+            if on_vector < K:
+                interleave(nc.scalar.copy, w1_bf[e][:, PACK * on_vector :], w1_raw[e][:, :, on_vector:K])
 
         def second_product(e):
-            q, u = divmod(e, 2)
-            if u == 0:
-                dx_banks[q] = psum.tile([P, K // P, PAIR], F32, name="dx_bank", bufs=2)
+            codes = stream.tile([P, K], U32, name="w_codes", align_bytes=64, bufs=4)
+            scales = stream.tile([P, K], U8, name="w_scales", align_bytes=64, bufs=4)
+            nc.vector.quantize_mx(out=codes[:].bitcast(FP8X4), scales=scales[:], in_=w1_bf[e][:])
+            first, count = [group for group in DX_GROUPS if group[0] <= e][-1]
+            if e == first:
+                dx_banks[first] = [psum.tile([P, count * C], F32, name="dx_bank%d" % h, bufs=2) for h in range(K // P)]
             for h in range(K // P):
                 cols = slice(h * P, (h + 1) * P)
                 nc.tensor.matmul_mx(
-                    out=dx_banks[q][:, h, u * C : (u + 1) * C],
-                    lhsT=w1_codes[e][:, cols].bitcast(FP8X4),
-                    lhsT_scale=w1_scales[e][:, cols],
+                    out=dx_banks[first][h][:, (e - first) * C : (e - first + 1) * C],
+                    lhsT=codes[:, cols].bitcast(FP8X4),
+                    lhsT_scale=scales[:, cols],
                     rhs=da_codes[e][:].bitcast(FP8X4),
                     rhs_scale=da_scales[e][:],
                     start=True,
                     stop=True,
                 )
-            if u == 1:
+            if e == first + count - 1:
                 for h in range(K // P):
-                    nc.scalar.copy(out=dx[h][:, q * PAIR : (q + 1) * PAIR], in_=dx_banks[q][:, h, :])
+                    nc.scalar.copy(out=dx[h][:, first * C : (e + 1) * C], in_=dx_banks[first][h][:])
 
-        make_identity(nc, ident[:])
-        nc.gpsimd.memset(gate_rows[:], 0.0)
-        nc.vector.memset(dy_s[:], 0)
-        load_w2(0)
-        nc.sync.dma_start(out=dy_w[:], in_=dy_words[0].rearrange("p t d -> p (t d)").bitcast(I32))
-        nc.sync.dma_start(offs_sb[:], offs)
-        for r in range(4):
-            nc.sync.dma_start(out=dy_s[r:P:32, :], in_=dy_scales[0].bitcast(I32)[r:16:4, :])
-        load_w2(1)
-        nc.sync.dma_start(out=gate_rows[0:E, :], in_=gate[0].rearrange("(e c) -> e c", c=C))
-        gate_turned = psum.tile([P, PACK, C], F32, name="dh", bufs=3)
-        nc.tensor.transpose(gate_turned[:, 0, :], gate_rows[:], ident[:])
-        nc.scalar.copy(out=gate_cols[:], in_=gate_turned[:, 0, 0:E])
-
-        for step in range(E + W1_LAG):
-            late = step - W1_LAG
-            if 1 < step < E:
-                load_w2(step)
-            for n, (first, width, load_step) in enumerate(A_CHUNKS):
-                if step == load_step:
-                    load_a(n)
-            if step == 3:
-                for r, pos in enumerate((pos1, pos2, pos3)):
-                    nc.sync.dma_start(pos_sb[r][:], pos)
-            if late >= 0:
-                load_w1(late)
-            if step < E:
-                round_w2(step)
-                gather(step)
-                first_product(step)
-            if 1 <= step <= E:
-                gate_and_turn(step - 1)
-            if late >= 0:
-                round_w1(late)
-            if DA_LAG <= step < E + DA_LAG:
-                round_da(step - DA_LAG)
-            if late >= 0:
-                quantize_w1(late)
-            if DA_LAG <= step < E + DA_LAG:
-                quantize_da(step - DA_LAG)
-            if late >= 0:
-                second_product(late)
-
-        for h in range(K // P):
+        def combine(h):
             one = keep.tile([P, T], F32, name="one%d" % h)
             two = keep.tile([P, T], F32, name="two%d" % h)
             three = keep.tile([P, T], F32, name="three%d" % h)
@@ -216,3 +192,44 @@ def tile_moe_bdx_mlp_relu_kernel(
                     nc.vector.tensor_tensor(after[:, tokens], dx[h][:].indirect(cols), before[:, tokens], ALU.add)
                     if r == 2:
                         nc.sync.dma_start(out=out[h * P : (h + 1) * P, tokens], in_=three[:, tokens])
+
+        make_identity(nc, ident[:])
+        nc.gpsimd.memset(gate_rows[:], 0.0)
+        nc.vector.memset(dy_s[:], 0)
+        load_w2(0)
+        nc.sync.dma_start(out=dy_w[:], in_=dy_words[0].rearrange("p t d -> p (t d)").bitcast(I32))
+        nc.sync.dma_start(offs_sb[:], offs)
+        for r in range(4):
+            nc.sync.dma_start(out=dy_s[r:P:32, :], in_=dy_scales[0].bitcast(I32)[r:16:4, :])
+        load_w2(1)
+        nc.sync.dma_start(out=gate_rows[0:E, :], in_=gate[0].rearrange("(e c) -> e c", c=C))
+        gate_turned = psum.tile([P, PACK, C], F32, name="dh", bufs=2)
+        nc.tensor.transpose(gate_turned[:, 0, :], gate_rows[:], ident[:])
+        nc.scalar.copy(out=gate_cols[:], in_=gate_turned[:, 0, 0:E])
+
+        for step in range(E + DA_LAG):
+            if 1 < step < E:
+                load_w2(step)
+            for n, (first, width, load_step) in enumerate(A_CHUNKS):
+                if step == load_step:
+                    load_a(n)
+            if step < E:
+                round_w2(step)
+                gather(step)
+                first_product(step)
+            if 1 <= step <= E:
+                gate_and_turn(step - 1)
+            if step >= DA_LAG:
+                round_da(step - DA_LAG)
+                quantize_da(step - DA_LAG)
+
+        for r, pos in enumerate((pos1, pos2, pos3)):
+            nc.sync.dma_start(pos_sb[r][:], pos)
+        for first, count in [(e, 2) for e in range(0, E - 2, 2)] + [(E - 2, 1), (E - 1, 1)]:
+            load_w1(first, count)
+            for e in range(first, first + count):
+                round_w1(e)
+            for e in range(first, first + count):
+                second_product(e)
+        for h in range(K // P):
+            combine(h)

@@ -23,10 +23,11 @@ PACK = 4
 PAIR = 2 * C
 LIST_COLS = 16
 DA_LAG = 2
-LOAD_RING = 16
+GATHERED = 4
+LOAD_RING = 8
 SCALAR_W2 = 384
 DX_GROUPS = [(0, 2), (2, 4), (6, 4), (10, 4), (14, 3), (17, 1)]
-A_CHUNKS = [(0, 256, 1), (256, 512, 3), (768, 512, 7), (1280, 512, 11), (1792, 512, 15)]
+A_CHUNKS = [(0, 768, 2), (768, 768, 8), (1536, 768, 14)]
 TOKEN_CUTS = [(0, 480), (480, 288)]
 
 
@@ -55,7 +56,7 @@ def tile_moe_bdx_mlp_relu_kernel(
         g_words, g_scales, w1_raw, w1_bf, dx_banks = {}, {}, {}, {}, {}
 
         def loaded_tile():
-            return stream.tile([P, PACK * H], F32, name="loaded", align_bytes=64, bufs=LOAD_RING)
+            return stream.tile([P, 2 * PACK * H], F32, name="loaded", align_bytes=64, bufs=LOAD_RING)
 
         def interleave(copy, rounded, raw):
             copy(
@@ -63,25 +64,34 @@ def tile_moe_bdx_mlp_relu_kernel(
                 in_=raw.rearrange("p j (c i) -> p c j i", i=4),
             )
 
-        def load_w2(e):
-            w2_raw[e] = loaded_tile()
-            nc.sync.dma_start(out=w2_raw[e][:], in_=w2[e].rearrange("(p j) i -> p (j i)", j=PACK))
+        def load_w2(first, count):
+            raw = loaded_tile()[:, 0 : count * PACK * H]
+            nc.sync.dma_start(
+                out=raw.rearrange("p (u r) -> p u r", u=count),
+                in_=w2[first : first + count].rearrange("u (p j) i -> p u (j i)", j=PACK),
+            )
+            for u in range(count):
+                w2_raw[first + u] = raw[:, u * PACK * H : (u + 1) * PACK * H]
 
         def load_a(n):
             first, width, step = A_CHUNKS[n]
             a_sb[n] = loaded_tile()[:, 0 : PACK * width].rearrange("p (t s) -> p t s", t=PACK)
             nc.sync.dma_start(out=a_sb[n], in_=a_rows[:, :, first : first + width])
 
-        def gather(e):
-            cols = offs_sb[:, e * C // LIST_COLS : (e + 1) * C // LIST_COLS]
-            g_words[e] = stream.tile([P, C], U32, name="g_words", align_bytes=64, bufs=2)
-            g_scales[e] = stream.tile([P, C], U8, name="g_scales", align_bytes=64, bufs=2)
-            nc.vector.tensor_copy(g_words[e][:], dy_w[:].bitcast(U32).indirect(cols))
-            nc.vector.tensor_copy(g_scales[e][:], dy_s[:].bitcast(U8).indirect(cols))
+        def gather(first):
+            count = min(GATHERED, E - first)
+            cols = offs_sb[:, first * C // LIST_COLS : (first + count) * C // LIST_COLS]
+            words = stream.tile([P, count * C], U32, name="g_words", align_bytes=64, bufs=3)
+            scales = stream.tile([P, count * C], U8, name="g_scales", align_bytes=64, bufs=3)
+            nc.vector.tensor_copy(words[:], dy_w[:].bitcast(U32).indirect(cols))
+            nc.vector.tensor_copy(scales[:], dy_s[:].bitcast(U8).indirect(cols))
+            for u in range(count):
+                g_words[first + u] = words[:, u * C : (u + 1) * C]
+                g_scales[first + u] = scales[:, u * C : (u + 1) * C]
 
         def round_w2(e):
             w2_bf[e] = stream.tile([P, H * PACK], BF16, name="rounded", align_bytes=64, bufs=3)
-            rows = w2_raw[e][:].rearrange("p (j i) -> p j i", j=PACK)
+            rows = w2_raw[e].rearrange("p (j i) -> p j i", j=PACK)
             for copy, first, last in (
                 (nc.scalar.copy, 0, P),
                 (nc.scalar.copy, P, SCALAR_W2),
@@ -96,8 +106,8 @@ def tile_moe_bdx_mlp_relu_kernel(
             dh_slots[e] = psum.tile([P, H], F32, name="dh_slots", bufs=2)
             nc.tensor.matmul_mx(
                 out=dh_slots[e][:],
-                lhsT=g_words[e][:].bitcast(FP8X4),
-                lhsT_scale=g_scales[e][:],
+                lhsT=g_words[e].bitcast(FP8X4),
+                lhsT_scale=g_scales[e],
                 rhs=w2_codes[:].bitcast(FP8X4),
                 rhs_scale=w2_scales[:],
                 start=True,
@@ -106,7 +116,7 @@ def tile_moe_bdx_mlp_relu_kernel(
 
         def gate_and_turn(e):
             if e + 1 < E:
-                staged = w2_raw[e + 1][:].rearrange("p (t i) -> p t i", t=PACK)[:, :, 0:P]
+                staged = w2_raw[e + 1].rearrange("p (t i) -> p t i", t=PACK)[:, :, 0:P]
             else:
                 staged = stream.tile([P, PACK, P], F32, name="last_staged", bufs=1)[:]
             nc.scalar.activation(
@@ -152,7 +162,7 @@ def tile_moe_bdx_mlp_relu_kernel(
 
         def round_w1(e):
             w1_bf[e] = stream.tile([P, PACK * K], BF16, name="w1_bf", align_bytes=64, bufs=5)
-            on_vector = 0 if e % 4 == 1 else K
+            on_vector = 128 if e == E - 1 else 0 if e % 4 == 1 else K
             if on_vector > 0:
                 interleave(nc.vector.tensor_copy, w1_bf[e][:, 0 : PACK * on_vector], w1_raw[e][:, :, 0:on_vector])
             if on_vector < K:
@@ -161,7 +171,12 @@ def tile_moe_bdx_mlp_relu_kernel(
         def second_product(e):
             codes = stream.tile([P, K], U32, name="w_codes", align_bytes=64, bufs=4)
             scales = stream.tile([P, K], U8, name="w_scales", align_bytes=64, bufs=4)
-            nc.vector.quantize_mx(out=codes[:].bitcast(FP8X4), scales=scales[:], in_=w1_bf[e][:])
+            for cols in [slice(0, K)] if e < E - 1 else [slice(0, P), slice(P, K)]:
+                nc.vector.quantize_mx(
+                    out=codes[:, cols].bitcast(FP8X4),
+                    scales=scales[:, cols],
+                    in_=w1_bf[e][:, PACK * cols.start : PACK * cols.stop],
+                )
             first, count = [group for group in DX_GROUPS if group[0] <= e][-1]
             if e == first:
                 dx_banks[first] = [psum.tile([P, count * C], F32, name="dx_bank%d" % h, bufs=2) for h in range(K // P)]
@@ -196,40 +211,50 @@ def tile_moe_bdx_mlp_relu_kernel(
         make_identity(nc, ident[:])
         nc.gpsimd.memset(gate_rows[:], 0.0)
         nc.vector.memset(dy_s[:], 0)
-        load_w2(0)
         nc.sync.dma_start(out=dy_w[:], in_=dy_words[0].rearrange("p t d -> p (t d)").bitcast(I32))
         nc.sync.dma_start(offs_sb[:], offs)
         for r in range(4):
             nc.sync.dma_start(out=dy_s[r:P:32, :], in_=dy_scales[0].bitcast(I32)[r:16:4, :])
-        load_w2(1)
+        load_w2(0, 1)
+        load_w2(1, 1)
         nc.sync.dma_start(out=gate_rows[0:E, :], in_=gate[0].rearrange("(e c) -> e c", c=C))
         gate_turned = psum.tile([P, PACK, C], F32, name="dh", bufs=2)
         nc.tensor.transpose(gate_turned[:, 0, :], gate_rows[:], ident[:])
         nc.scalar.copy(out=gate_cols[:], in_=gate_turned[:, 0, 0:E])
 
+        def w1_step(first, count):
+            load_w1(first, count)
+            for e in range(first, first + count):
+                round_w1(e)
+            for e in range(first, first + count):
+                second_product(e)
+
+        w1_loads = [(e, 2) for e in range(0, E - 2, 2)] + [(E - 2, 1), (E - 1, 1)]
         for step in range(E + DA_LAG):
-            if 1 < step < E:
-                load_w2(step)
+            if E - 2 <= step < E:
+                load_w2(step, 1)
+            elif 1 < step < E and step % 2 == 0:
+                load_w2(step, 2)
             for n, (first, width, load_step) in enumerate(A_CHUNKS):
                 if step == load_step:
                     load_a(n)
+            if step == 5:
+                for r, pos in enumerate((pos1, pos2, pos3)):
+                    nc.sync.dma_start(pos_sb[r][:], pos)
             if step < E:
                 round_w2(step)
-                gather(step)
+                if step % GATHERED == 0:
+                    gather(step)
                 first_product(step)
             if 1 <= step <= E:
                 gate_and_turn(step - 1)
             if step >= DA_LAG:
                 round_da(step - DA_LAG)
                 quantize_da(step - DA_LAG)
+            if False:
+                w1_step(*w1_loads.pop(0))
 
-        for r, pos in enumerate((pos1, pos2, pos3)):
-            nc.sync.dma_start(pos_sb[r][:], pos)
-        for first, count in [(e, 2) for e in range(0, E - 2, 2)] + [(E - 2, 1), (E - 1, 1)]:
-            load_w1(first, count)
-            for e in range(first, first + count):
-                round_w1(e)
-            for e in range(first, first + count):
-                second_product(e)
+        for first, count in w1_loads:
+            w1_step(first, count)
         for h in range(K // P):
             combine(h)

@@ -20,15 +20,19 @@ COPY = mybir.ActivationFunctionType.Copy
 
 P = 128
 PACK = 4
-PAIR = 2 * C
+RUN = 4
 LIST_COLS = 16
+BANKS = 8
+BANK_EXPERTS = 4
+LOAD_RING = 8
 DA_LAG = 2
 GATHERED = 4
-LOAD_RING = 8
-SCALAR_W2 = 384
-DX_GROUPS = [(0, 2), (2, 4), (6, 4), (10, 4), (14, 3), (17, 1)]
-A_CHUNKS = [(0, 768, 2), (768, 768, 8), (1536, 768, 14)]
-TOKEN_CUTS = [(0, 480), (480, 288)]
+SCALAR_W2 = 352
+A_CHUNKS = [(first, 6 * C, first // C + DA_LAG) for first in range(0, S, 6 * C)]
+LISTS_STEP = 5
+WHOLE_W1 = 12
+DX_GROUPS = [[(0, 6), (6, 6), (12, 4), (16, 2)], [(0, 6), (6, 6), (12, 6)]]
+TOKEN_CUTS = [(0, T - S // 8), (T - S // 8, S // 8)]
 
 
 def tile_moe_bdx_mlp_relu_kernel(
@@ -39,7 +43,7 @@ def tile_moe_bdx_mlp_relu_kernel(
         lists = ctx.enter_context(tc.tile_pool(name="lists", bufs=1))
         keep = ctx.enter_context(tc.tile_pool(name="keep", bufs=1))
         stream = ctx.enter_context(tc.tile_pool(name="stream", bufs=3))
-        psum = ctx.enter_context(tc.psum_pool(name="psum", bufs=2))
+        psum = ctx.enter_context(tc.psum_pool(name="psum", bufs=BANKS))
 
         offs_sb = lists.tile([P, S // LIST_COLS], U16, name="offs_sb")
         pos_sb = [lists.tile([P, T // LIST_COLS], U16, name="pos_sb%d" % r) for r in range(3)]
@@ -49,34 +53,44 @@ def tile_moe_bdx_mlp_relu_kernel(
         gate_rows = keep.tile([P, C], F32, name="gate_rows")
         gate_cols = keep.tile([P, E], F32, name="gate_cols")
         dx = [keep.tile([P, S], F32, name="dx%d" % h) for h in range(K // P)]
-        a_sb = {}
         a_rows = a.rearrange("(p t) s -> p t s", t=PACK)
 
-        w2_raw, w2_bf, dh_slots, dh, da_bf, da_codes, da_scales = {}, {}, {}, {}, {}, {}, {}
-        g_words, g_scales, w1_raw, w1_bf, dx_banks = {}, {}, {}, {}, {}
+        a_sb, g_words, g_scales, w2_raw, w2_bf = {}, {}, {}, {}, {}
+        sums, dh, da_bf, da_codes, da_scales, dx_banks = {}, {}, {}, {}, {}, {}
 
         def loaded_tile():
             return stream.tile([P, 2 * PACK * H], F32, name="loaded", align_bytes=64, bufs=LOAD_RING)
 
         def interleave(copy, rounded, raw):
             copy(
-                out=rounded.rearrange("p (c i j) -> p c j i", i=4, j=PACK),
-                in_=raw.rearrange("p j (c i) -> p c j i", i=4),
+                out=rounded.rearrange("p (c i j) -> p c j i", i=RUN, j=PACK),
+                in_=raw.rearrange("p j (c i) -> p c j i", i=RUN),
             )
 
-        def load_w2(first, count):
-            raw = loaded_tile()[:, 0 : count * PACK * H]
+        def load_experts(weights, first, count):
+            width = PACK * weights.shape[2]
+            raw = loaded_tile()[:, 0 : count * width]
             nc.sync.dma_start(
                 out=raw.rearrange("p (u r) -> p u r", u=count),
-                in_=w2[first : first + count].rearrange("u (p j) i -> p u (j i)", j=PACK),
+                in_=weights[first : first + count].rearrange("u (p j) c -> p u (j c)", j=PACK),
             )
-            for u in range(count):
-                w2_raw[first + u] = raw[:, u * PACK * H : (u + 1) * PACK * H]
+            return [raw[:, u * width : (u + 1) * width].rearrange("p (j c) -> p j c", j=PACK) for u in range(count)]
+
+        def load_w2(first, count):
+            for u, raw in enumerate(load_experts(w2, first, count)):
+                w2_raw[first + u] = raw
 
         def load_a(n):
             first, width, step = A_CHUNKS[n]
             a_sb[n] = loaded_tile()[:, 0 : PACK * width].rearrange("p (t s) -> p t s", t=PACK)
             nc.sync.dma_start(out=a_sb[n], in_=a_rows[:, :, first : first + width])
+
+        def quantize(rounded):
+            width = rounded.shape[1] // PACK
+            codes = stream.tile([P, width], U32, name="w_codes", align_bytes=64, bufs=4)
+            scales = stream.tile([P, width], U8, name="w_scales", align_bytes=64, bufs=4)
+            nc.vector.quantize_mx(out=codes[:].bitcast(FP8X4), scales=scales[:], in_=rounded)
+            return codes, scales
 
         def gather(first):
             count = min(GATHERED, E - first)
@@ -91,50 +105,45 @@ def tile_moe_bdx_mlp_relu_kernel(
 
         def round_w2(e):
             w2_bf[e] = stream.tile([P, H * PACK], BF16, name="rounded", align_bytes=64, bufs=3)
-            rows = w2_raw[e].rearrange("p (j i) -> p j i", j=PACK)
             for copy, first, last in (
                 (nc.scalar.copy, 0, P),
                 (nc.scalar.copy, P, SCALAR_W2),
                 (nc.vector.tensor_copy, SCALAR_W2, H),
             ):
-                interleave(copy, w2_bf[e][:, first * PACK : last * PACK], rows[:, :, first:last])
+                interleave(copy, w2_bf[e][:, first * PACK : last * PACK], w2_raw[e][:, :, first:last])
 
         def first_product(e):
-            w2_codes = stream.tile([P, H], U32, name="w_codes", align_bytes=64, bufs=4)
-            w2_scales = stream.tile([P, H], U8, name="w_scales", align_bytes=64, bufs=4)
-            nc.vector.quantize_mx(out=w2_codes[:].bitcast(FP8X4), scales=w2_scales[:], in_=w2_bf[e][:])
-            dh_slots[e] = psum.tile([P, H], F32, name="dh_slots", bufs=2)
+            codes, scales = quantize(w2_bf[e][:])
+            sums[e] = psum.tile([P, H], F32, name="bank")
             nc.tensor.matmul_mx(
-                out=dh_slots[e][:],
+                out=sums[e][:],
                 lhsT=g_words[e].bitcast(FP8X4),
                 lhsT_scale=g_scales[e],
-                rhs=w2_codes[:].bitcast(FP8X4),
-                rhs_scale=w2_scales[:],
+                rhs=codes[:].bitcast(FP8X4),
+                rhs_scale=scales[:],
                 start=True,
                 stop=True,
             )
 
         def gate_and_turn(e):
             if e + 1 < E:
-                staged = w2_raw[e + 1].rearrange("p (t i) -> p t i", t=PACK)[:, :, 0:P]
+                gated = w2_raw[e + 1][:, :, 0:P]
             else:
-                staged = stream.tile([P, PACK, P], F32, name="last_staged", bufs=1)[:]
+                gated = stream.tile([P, PACK, P], F32, name="last_gated", bufs=1)[:]
             nc.scalar.activation(
-                out=staged,
-                in_=dh_slots[e][:].rearrange("p (m t) -> p t m", t=PACK),
+                out=gated,
+                in_=sums[e][:].rearrange("p (m t) -> p t m", t=PACK),
                 func=COPY,
                 scale=gate_cols[:, e : e + 1],
             )
-            dh[e] = psum.tile([P, PACK, C], F32, name="dh", bufs=2)
+            dh[e] = psum.tile([P, PACK, C], F32, name="bank")
             for t in range(PACK):
-                nc.tensor.transpose(dh[e][:, t, :], staged[:, t, :], ident[:])
+                nc.tensor.transpose(dh[e][:, t, :], gated[:, t, :], ident[:])
 
         def round_da(e):
-            n = [first <= e * C < first + width for first, width, step in A_CHUNKS].index(True)
-            first = e * C - A_CHUNKS[n][0]
+            n, first = divmod(e * C, A_CHUNKS[0][1])
             if e + DA_LAG < E:
-                spent = (PACK - 1) * H + P
-                da_bf[e] = w2_raw[e + DA_LAG][:, spent : spent + C * PACK // 2].bitcast(BF16)
+                da_bf[e] = w2_raw[e + DA_LAG][:, PACK - 1, P : P + C * PACK // 2].bitcast(BF16)
             else:
                 da_bf[e] = stream.tile([P, C * PACK], BF16, name="last_da", align_bytes=64, bufs=DA_LAG)[:]
             nc.vector.scalar_tensor_tensor(
@@ -151,60 +160,61 @@ def tile_moe_bdx_mlp_relu_kernel(
             da_scales[e] = keep.tile([P, C], U8, name="da_scales%d" % e, align_bytes=64)
             nc.vector.quantize_mx(out=da_codes[e][:].bitcast(FP8X4), scales=da_scales[e][:], in_=da_bf[e])
 
-        def load_w1(first, count):
-            raw = loaded_tile()[:, 0 : count * PACK * K]
-            nc.sync.dma_start(
-                out=raw.rearrange("p (u r) -> p u r", u=count),
-                in_=w1[first : first + count].rearrange("u (p j) k -> p u (j k)", j=PACK),
+        def second_product(e, h, codes, scales, column):
+            first, count = [group for group in DX_GROUPS[h] if group[0] <= e][-1]
+            ways = 2 if count > BANK_EXPERTS else 1
+            n, u = divmod(e - first, ways)
+            if n == 0:
+                dx_banks[first, h, u] = psum.tile([P, count // ways, C], F32, name="bank")
+            cols = slice(column, column + P)
+            nc.tensor.matmul_mx(
+                out=dx_banks[first, h, u][:, n, :],
+                lhsT=codes[:, cols].bitcast(FP8X4),
+                lhsT_scale=scales[:, cols],
+                rhs=da_codes[e][:].bitcast(FP8X4),
+                rhs_scale=da_scales[e][:],
+                start=True,
+                stop=True,
             )
-            for u in range(count):
-                w1_raw[first + u] = raw[:, u * PACK * K : (u + 1) * PACK * K].rearrange("p (j k) -> p j k", j=PACK)
+            if n == count // ways - 1:
+                copy = nc.vector.tensor_copy if h == 0 and e == E - 1 else nc.scalar.copy
+                slots = dx[h][:, first * C : (first + count) * C].rearrange("p (n u c) -> p u n c", u=ways, c=C)
+                copy(out=slots[:, u], in_=dx_banks[first, h, u][:])
 
-        def round_w1(e):
-            w1_bf[e] = stream.tile([P, PACK * K], BF16, name="w1_bf", align_bytes=64, bufs=5)
-            on_vector = 128 if e == E - 1 else 0 if e % 4 == 1 else K
-            if on_vector > 0:
-                interleave(nc.vector.tensor_copy, w1_bf[e][:, 0 : PACK * on_vector], w1_raw[e][:, :, 0:on_vector])
-            if on_vector < K:
-                interleave(nc.scalar.copy, w1_bf[e][:, PACK * on_vector :], w1_raw[e][:, :, on_vector:K])
-
-        def second_product(e):
-            codes = stream.tile([P, K], U32, name="w_codes", align_bytes=64, bufs=4)
-            scales = stream.tile([P, K], U8, name="w_scales", align_bytes=64, bufs=4)
-            for cols in [slice(0, K)] if e < E - 1 else [slice(0, P), slice(P, K)]:
-                nc.vector.quantize_mx(
-                    out=codes[:, cols].bitcast(FP8X4),
-                    scales=scales[:, cols],
-                    in_=w1_bf[e][:, PACK * cols.start : PACK * cols.stop],
-                )
-            first, count = [group for group in DX_GROUPS if group[0] <= e][-1]
-            if e == first:
-                dx_banks[first] = [psum.tile([P, count * C], F32, name="dx_bank%d" % h, bufs=2) for h in range(K // P)]
-            for h in range(K // P):
-                cols = slice(h * P, (h + 1) * P)
-                nc.tensor.matmul_mx(
-                    out=dx_banks[first][h][:, (e - first) * C : (e - first + 1) * C],
-                    lhsT=codes[:, cols].bitcast(FP8X4),
-                    lhsT_scale=scales[:, cols],
-                    rhs=da_codes[e][:].bitcast(FP8X4),
-                    rhs_scale=da_scales[e][:],
-                    start=True,
-                    stop=True,
-                )
-            if e == first + count - 1:
+        def whole_pair(first):
+            opens_later_group = first in [group[0] for group in DX_GROUPS[0][1:]]
+            rounded = []
+            for u, raw in enumerate(load_experts(w1, first, 2)):
+                rounded.append(stream.tile([P, PACK * K], BF16, name="w1_bf", align_bytes=64, bufs=5))
+                on_scalar = u == 0 and not opens_later_group
+                interleave(nc.scalar.copy if on_scalar else nc.vector.tensor_copy, rounded[u][:], raw)
+            for u in range(2):
+                codes, scales = quantize(rounded[u][:])
                 for h in range(K // P):
-                    nc.scalar.copy(out=dx[h][:, first * C : (e + 1) * C], in_=dx_banks[first][h][:])
+                    second_product(first + u, h, codes, scales, h * P)
 
-        def combine(h):
+        def halves(first, count, h, copy, rounded):
+            raw = loaded_tile()[:, 0 : count * PACK * P].rearrange("p (u j k) -> p u j k", u=count, j=PACK)
+            for u in range(count):
+                rows = w1[first + u].rearrange("(p j) k -> p j k", j=PACK)
+                nc.sync.dma_start(out=raw[:, u], in_=rows[:, :, h * P : (h + 1) * P])
+            for u in range(count):
+                interleave(copy, rounded[:, u * PACK * P : (u + 1) * PACK * P], raw[:, u])
+            codes, scales = quantize(rounded[:, 0 : count * PACK * P])
+            for u in range(count):
+                second_product(first + u, h, codes, scales, u * P)
+
+        def combine(h, three):
             one = keep.tile([P, T], F32, name="one%d" % h)
             two = keep.tile([P, T], F32, name="two%d" % h)
-            three = keep.tile([P, T], F32, name="three%d" % h)
-            nc.vector.tensor_copy(one[:], dx[h][:].indirect(pos_sb[0][:]))
-            for r, before, after in ((1, one, two), (2, two, three)):
+            for r, before, after in ((0, None, one), (1, one, two), (2, two, three)):
                 for first, count in TOKEN_CUTS:
                     tokens = slice(first, first + count)
-                    cols = pos_sb[r][:, first // LIST_COLS : (first + count) // LIST_COLS]
-                    nc.vector.tensor_tensor(after[:, tokens], dx[h][:].indirect(cols), before[:, tokens], ALU.add)
+                    picked = dx[h][:].indirect(pos_sb[r][:, first // LIST_COLS : (first + count) // LIST_COLS])
+                    if r == 0:
+                        nc.vector.tensor_copy(after[:, tokens], picked)
+                    else:
+                        nc.vector.tensor_tensor(after[:, tokens], picked, before[:, tokens], ALU.add)
                     if r == 2:
                         nc.sync.dma_start(out=out[h * P : (h + 1) * P, tokens], in_=three[:, tokens])
 
@@ -218,18 +228,10 @@ def tile_moe_bdx_mlp_relu_kernel(
         load_w2(0, 1)
         load_w2(1, 1)
         nc.sync.dma_start(out=gate_rows[0:E, :], in_=gate[0].rearrange("(e c) -> e c", c=C))
-        gate_turned = psum.tile([P, PACK, C], F32, name="dh", bufs=2)
+        gate_turned = psum.tile([P, PACK, C], F32, name="bank")
         nc.tensor.transpose(gate_turned[:, 0, :], gate_rows[:], ident[:])
         nc.scalar.copy(out=gate_cols[:], in_=gate_turned[:, 0, 0:E])
 
-        def w1_step(first, count):
-            load_w1(first, count)
-            for e in range(first, first + count):
-                round_w1(e)
-            for e in range(first, first + count):
-                second_product(e)
-
-        w1_loads = [(e, 2) for e in range(0, E - 2, 2)] + [(E - 2, 1), (E - 1, 1)]
         for step in range(E + DA_LAG):
             if E - 2 <= step < E:
                 load_w2(step, 1)
@@ -238,7 +240,7 @@ def tile_moe_bdx_mlp_relu_kernel(
             for n, (first, width, load_step) in enumerate(A_CHUNKS):
                 if step == load_step:
                     load_a(n)
-            if step == 5:
+            if step == LISTS_STEP:
                 for r, pos in enumerate((pos1, pos2, pos3)):
                     nc.sync.dma_start(pos_sb[r][:], pos)
             if step < E:
@@ -251,10 +253,14 @@ def tile_moe_bdx_mlp_relu_kernel(
             if step >= DA_LAG:
                 round_da(step - DA_LAG)
                 quantize_da(step - DA_LAG)
-            if False:
-                w1_step(*w1_loads.pop(0))
 
-        for first, count in w1_loads:
-            w1_step(first, count)
-        for h in range(K // P):
-            combine(h)
+        for first in range(0, WHOLE_W1, 2):
+            whole_pair(first)
+        for first in range(WHOLE_W1, E, 2):
+            rounded = stream.tile([P, 2 * PACK * P], BF16, name="w1_bf", align_bytes=64, bufs=5)
+            halves(first, 2, 0, nc.vector.tensor_copy, rounded)
+        for first, count in ((WHOLE_W1, 2), (WHOLE_W1 + 2, E - WHOLE_W1 - 2)):
+            rounded = stream.tile([P, H * PACK], BF16, name="rounded", align_bytes=64, bufs=3)
+            halves(first, count, 1, nc.scalar.copy, rounded)
+        combine(0, rounded[:, 0 : 2 * T].bitcast(F32))
+        combine(1, keep.tile([P, T], F32, name="three")[:])

@@ -31,7 +31,7 @@ SCALAR_W2 = 352
 A_CHUNKS = [(first, 6 * C, first // C + DA_LAG) for first in range(0, S, 6 * C)]
 LISTS_STEP = 5
 WHOLE_W1 = 12
-DX_GROUPS = [[(0, 6), (6, 6), (12, 4), (16, 2)], [(0, 6), (6, 6), (12, 6)]]
+DX_GROUPS = [[(0, 6), (6, 6), (12, 4), (16, 1), (17, 1)], [(0, 6), (6, 6), (12, 6)]]
 TOKEN_CUTS = [(0, T - S // 8), (T - S // 8, S // 8)]
 
 
@@ -256,11 +256,11 @@ def tile_moe_bdx_mlp_relu_kernel(
 
         for first in range(0, WHOLE_W1, 2):
             whole_pair(first)
-        for first in range(WHOLE_W1, E, 2):
+        for first, count in [(e, 2) for e in range(WHOLE_W1, E - 2, 2)] + [(E - 2, 1), (E - 1, 1)]:
             rounded = stream.tile([P, 2 * PACK * P], BF16, name="w1_bf", align_bytes=64, bufs=5)
-            halves(first, 2, 0, nc.vector.tensor_copy, rounded)
-        for first, count in ((WHOLE_W1, 2), (WHOLE_W1 + 2, E - WHOLE_W1 - 2)):
+            halves(first, count, 0, nc.vector.tensor_copy, rounded)
+        for first in range(WHOLE_W1, E, 2):
             rounded = stream.tile([P, H * PACK], BF16, name="rounded", align_bytes=64, bufs=3)
-            halves(first, count, 1, nc.scalar.copy, rounded)
+            halves(first, 2, 1, nc.scalar.copy, rounded)
         combine(0, rounded[:, 0 : 2 * T].bitcast(F32))
         combine(1, keep.tile([P, T], F32, name="three")[:])

@@ -24,12 +24,11 @@ RUN = 4
 LIST_COLS = 16
 BANKS = 8
 BANK_EXPERTS = 4
-LOAD_RING = 8
+LOAD_RING = 12
 DA_LAG = 2
 GATHERED = 4
 SCALAR_W2 = 352
-A_CHUNKS = [(first, 6 * C, first // C + DA_LAG) for first in range(0, S, 6 * C)]
-LISTS_STEP = 5
+HEAD_EXPERTS = 2
 WHOLE_W1 = 12
 DX_GROUPS = [[(0, 6), (6, 6), (12, 4), (16, 1), (17, 1)], [(0, 6), (6, 6), (12, 6)]]
 TOKEN_CUTS = [(0, T - S // 8), (T - S // 8, S // 8)]
@@ -53,13 +52,13 @@ def tile_moe_bdx_mlp_relu_kernel(
         gate_rows = keep.tile([P, C], F32, name="gate_rows")
         gate_cols = keep.tile([P, E], F32, name="gate_cols")
         dx = [keep.tile([P, S], F32, name="dx%d" % h) for h in range(K // P)]
-        a_rows = a.rearrange("(p t) s -> p t s", t=PACK)
+        a_sb = keep.tile([P, PACK, S], F32, name="a_sb")
 
-        a_sb, g_words, g_scales, w2_raw, w2_bf = {}, {}, {}, {}, {}
+        g_words, g_scales, w2_raw, w2_bf = {}, {}, {}, {}
         sums, dh, da_bf, da_codes, da_scales, dx_banks = {}, {}, {}, {}, {}, {}
 
         def loaded_tile():
-            return stream.tile([P, 2 * PACK * H], F32, name="loaded", align_bytes=64, bufs=LOAD_RING)
+            return stream.tile([P, PACK * H], F32, name="loaded", align_bytes=64, bufs=LOAD_RING)
 
         def interleave(copy, rounded, raw):
             copy(
@@ -76,14 +75,8 @@ def tile_moe_bdx_mlp_relu_kernel(
             )
             return [raw[:, u * width : (u + 1) * width].rearrange("p (j c) -> p j c", j=PACK) for u in range(count)]
 
-        def load_w2(first, count):
-            for u, raw in enumerate(load_experts(w2, first, count)):
-                w2_raw[first + u] = raw
-
-        def load_a(n):
-            first, width, step = A_CHUNKS[n]
-            a_sb[n] = loaded_tile()[:, 0 : PACK * width].rearrange("p (t s) -> p t s", t=PACK)
-            nc.sync.dma_start(out=a_sb[n], in_=a_rows[:, :, first : first + width])
+        def load_w2(e):
+            w2_raw[e] = load_experts(w2, e, 1)[0]
 
         def quantize(rounded):
             width = rounded.shape[1] // PACK
@@ -95,8 +88,8 @@ def tile_moe_bdx_mlp_relu_kernel(
         def gather(first):
             count = min(GATHERED, E - first)
             cols = offs_sb[:, first * C // LIST_COLS : (first + count) * C // LIST_COLS]
-            words = stream.tile([P, count * C], U32, name="g_words", align_bytes=64, bufs=3)
-            scales = stream.tile([P, count * C], U8, name="g_scales", align_bytes=64, bufs=3)
+            words = keep.tile([P, count * C], U32, name="g_words%d" % first, align_bytes=64)
+            scales = keep.tile([P, count * C], U8, name="g_scales%d" % first, align_bytes=64)
             nc.vector.tensor_copy(words[:], dy_w[:].bitcast(U32).indirect(cols))
             nc.vector.tensor_copy(scales[:], dy_s[:].bitcast(U8).indirect(cols))
             for u in range(count):
@@ -105,11 +98,8 @@ def tile_moe_bdx_mlp_relu_kernel(
 
         def round_w2(e):
             w2_bf[e] = stream.tile([P, H * PACK], BF16, name="rounded", align_bytes=64, bufs=3)
-            for copy, first, last in (
-                (nc.scalar.copy, 0, P),
-                (nc.scalar.copy, P, SCALAR_W2),
-                (nc.vector.tensor_copy, SCALAR_W2, H),
-            ):
+            rest = nc.scalar.copy if e < HEAD_EXPERTS else nc.vector.tensor_copy
+            for copy, first, last in ((nc.scalar.copy, 0, P), (nc.scalar.copy, P, SCALAR_W2), (rest, SCALAR_W2, H)):
                 interleave(copy, w2_bf[e][:, first * PACK : last * PACK], w2_raw[e][:, :, first:last])
 
         def first_product(e):
@@ -141,14 +131,13 @@ def tile_moe_bdx_mlp_relu_kernel(
                 nc.tensor.transpose(dh[e][:, t, :], gated[:, t, :], ident[:])
 
         def round_da(e):
-            n, first = divmod(e * C, A_CHUNKS[0][1])
             if e + DA_LAG < E:
                 da_bf[e] = w2_raw[e + DA_LAG][:, PACK - 1, P : P + C * PACK // 2].bitcast(BF16)
             else:
                 da_bf[e] = stream.tile([P, C * PACK], BF16, name="last_da", align_bytes=64, bufs=DA_LAG)[:]
             nc.vector.scalar_tensor_tensor(
                 out=da_bf[e].rearrange("p (s t) -> p s t", t=PACK),
-                in0=a_sb[n][:, :, first : first + C].rearrange("p t s -> p s t"),
+                in0=a_sb[:, :, e * C : (e + 1) * C].rearrange("p t s -> p s t"),
                 scalar=0.0,
                 in1=dh[e][:].rearrange("p t s -> p s t"),
                 op0=ALU.is_gt,
@@ -225,24 +214,17 @@ def tile_moe_bdx_mlp_relu_kernel(
         nc.sync.dma_start(offs_sb[:], offs)
         for r in range(4):
             nc.sync.dma_start(out=dy_s[r:P:32, :], in_=dy_scales[0].bitcast(I32)[r:16:4, :])
-        load_w2(0, 1)
-        load_w2(1, 1)
+        for e in range(HEAD_EXPERTS):
+            load_w2(e)
         nc.sync.dma_start(out=gate_rows[0:E, :], in_=gate[0].rearrange("(e c) -> e c", c=C))
+        nc.sync.dma_start(out=a_sb[:], in_=a.rearrange("(p t) s -> p t s", t=PACK))
         gate_turned = psum.tile([P, PACK, C], F32, name="bank")
         nc.tensor.transpose(gate_turned[:, 0, :], gate_rows[:], ident[:])
         nc.scalar.copy(out=gate_cols[:], in_=gate_turned[:, 0, 0:E])
 
         for step in range(E + DA_LAG):
-            if E - 2 <= step < E:
-                load_w2(step, 1)
-            elif 1 < step < E and step % 2 == 0:
-                load_w2(step, 2)
-            for n, (first, width, load_step) in enumerate(A_CHUNKS):
-                if step == load_step:
-                    load_a(n)
-            if step == LISTS_STEP:
-                for r, pos in enumerate((pos1, pos2, pos3)):
-                    nc.sync.dma_start(pos_sb[r][:], pos)
+            if HEAD_EXPERTS <= step < E:
+                load_w2(step)
             if step < E:
                 round_w2(step)
                 if step % GATHERED == 0:
@@ -259,6 +241,8 @@ def tile_moe_bdx_mlp_relu_kernel(
         for first, count in [(e, 2) for e in range(WHOLE_W1, E - 2, 2)] + [(E - 2, 1), (E - 1, 1)]:
             rounded = stream.tile([P, 2 * PACK * P], BF16, name="w1_bf", align_bytes=64, bufs=5)
             halves(first, count, 0, nc.vector.tensor_copy, rounded)
+        for r, pos in enumerate((pos1, pos2, pos3)):
+            nc.sync.dma_start(pos_sb[r][:], pos)
         for first in range(WHOLE_W1, E, 2):
             rounded = stream.tile([P, H * PACK], BF16, name="rounded", align_bytes=64, bufs=3)
             halves(first, 2, 1, nc.scalar.copy, rounded)

@@ -27,11 +27,12 @@ BANK_EXPERTS = 4
 LOAD_RING = 12
 DA_LAG = 2
 GATHERED = 4
-SCALAR_W2 = 352
-HEAD_EXPERTS = 2
-WHOLE_W1 = 12
-DX_GROUPS = [[(0, 6), (6, 6), (12, 4), (16, 1), (17, 1)], [(0, 6), (6, 6), (12, 6)]]
+SCALAR_W2 = 320
+HEAD_EXPERTS = 1
+WHOLE_W1 = 14
+DX_GROUPS = [[(0, 4), (4, 6), (10, 4), (14, 2), (16, 2)], [(0, 4), (4, 6), (10, 4), (14, 2), (16, 2)]]
 TOKEN_CUTS = [(0, T - S // 8), (T - S // 8, S // 8)]
+LAST_CUTS = [(0, 384), (384, 288), (672, 96)]
 
 
 def tile_moe_bdx_mlp_relu_kernel(
@@ -171,11 +172,11 @@ def tile_moe_bdx_mlp_relu_kernel(
                 copy(out=slots[:, u], in_=dx_banks[first, h, u][:])
 
         def whole_pair(first):
-            opens_later_group = first in [group[0] for group in DX_GROUPS[0][1:]]
+            opens_later_group = first in [group[0] for group in DX_GROUPS[0][1:3]]
             rounded = []
             for u, raw in enumerate(load_experts(w1, first, 2)):
                 rounded.append(stream.tile([P, PACK * K], BF16, name="w1_bf", align_bytes=64, bufs=5))
-                on_scalar = u == 0 and not opens_later_group
+                on_scalar = first < DX_GROUPS[0][1][0] or (u == 0 and not opens_later_group)
                 interleave(nc.scalar.copy if on_scalar else nc.vector.tensor_copy, rounded[u][:], raw)
             for u in range(2):
                 codes, scales = quantize(rounded[u][:])
@@ -197,7 +198,7 @@ def tile_moe_bdx_mlp_relu_kernel(
             one = keep.tile([P, T], F32, name="one%d" % h)
             two = keep.tile([P, T], F32, name="two%d" % h)
             for r, before, after in ((0, None, one), (1, one, two), (2, two, three)):
-                for first, count in TOKEN_CUTS:
+                for first, count in LAST_CUTS if (h, r) == (1, 2) else TOKEN_CUTS:
                     tokens = slice(first, first + count)
                     picked = dx[h][:].indirect(pos_sb[r][:, first // LIST_COLS : (first + count) // LIST_COLS])
                     if r == 0:
@@ -238,13 +239,14 @@ def tile_moe_bdx_mlp_relu_kernel(
 
         for first in range(0, WHOLE_W1, 2):
             whole_pair(first)
-        for first, count in [(e, 2) for e in range(WHOLE_W1, E - 2, 2)] + [(E - 2, 1), (E - 1, 1)]:
-            rounded = stream.tile([P, 2 * PACK * P], BF16, name="w1_bf", align_bytes=64, bufs=5)
-            halves(first, count, 0, nc.vector.tensor_copy, rounded)
+        late = stream.tile([P, H * PACK], BF16, name="rounded", align_bytes=64, bufs=3)
+        for e in range(WHOLE_W1, E):
+            rounded = late
+            if e < E - 1:
+                rounded = stream.tile([P, 2 * PACK * P], BF16, name="w1_bf", align_bytes=64, bufs=5)
+            halves(e, 1, 0, nc.vector.tensor_copy if e % 2 else nc.scalar.copy, rounded)
         for r, pos in enumerate((pos1, pos2, pos3)):
             nc.sync.dma_start(pos_sb[r][:], pos)
-        for first in range(WHOLE_W1, E, 2):
-            rounded = stream.tile([P, H * PACK], BF16, name="rounded", align_bytes=64, bufs=3)
-            halves(first, 2, 1, nc.scalar.copy, rounded)
+        halves(WHOLE_W1, E - WHOLE_W1, 1, nc.scalar.copy, rounded)
         combine(0, rounded[:, 0 : 2 * T].bitcast(F32))
         combine(1, keep.tile([P, T], F32, name="three")[:])

@@ -17,6 +17,7 @@ U8 = mybir.dt.uint8
 FP8X4 = mybir.dt.float8_e4m3fn_x4
 ALU = mybir.AluOpType
 COPY = mybir.ActivationFunctionType.Copy
+SIGN = mybir.ActivationFunctionType.Sign
 
 P = 128
 PACK = 4
@@ -27,7 +28,8 @@ BANK_EXPERTS = 4
 LOAD_RING = 12
 DA_LAG = 2
 GATHERED = 4
-SCALAR_W2 = 320
+SCALAR_W2 = 288
+SCALAR_MASK = 8 * C
 HEAD_EXPERTS = 1
 WHOLE_W1 = 14
 DX_GROUPS = [[(0, 4), (4, 6), (10, 4), (14, 2), (16, 2)], [(0, 4), (4, 6), (10, 4), (14, 2), (16, 2)]]
@@ -53,7 +55,9 @@ def tile_moe_bdx_mlp_relu_kernel(
         gate_rows = keep.tile([P, C], F32, name="gate_rows")
         gate_cols = keep.tile([P, E], F32, name="gate_cols")
         dx = [keep.tile([P, S], F32, name="dx%d" % h) for h in range(K // P)]
-        a_sb = keep.tile([P, PACK, S], F32, name="a_sb")
+        a_sb = [keep.tile([P, 2 * S], F32, name="a_sb%d" % u) for u in range(2)]
+        mask = keep.tile([P, 2, 2 * S], BF16, name="mask")
+        a_rows = a.rearrange("(p u v) s -> u p (v s)", u=2, v=2)
 
         g_words, g_scales, w2_raw, w2_bf = {}, {}, {}, {}
         sums, dh, da_bf, da_codes, da_scales, dx_banks = {}, {}, {}, {}, {}, {}
@@ -78,6 +82,15 @@ def tile_moe_bdx_mlp_relu_kernel(
 
         def load_w2(e):
             w2_raw[e] = load_experts(w2, e, 1)[0]
+
+        def make_mask(u, first, last, on_scalar):
+            pairs = mask[:, u, 2 * first : 2 * last]
+            rows = a_sb[u][:].rearrange("p (v s) -> p s v", v=2)[:, first:last, :]
+            if on_scalar:
+                nc.scalar.activation(out=pairs.rearrange("p (s v) -> p s v", v=2), in_=rows, func=SIGN)
+                nc.vector.tensor_scalar_max(pairs, pairs, 0.0)
+            else:
+                nc.vector.tensor_single_scalar(pairs.rearrange("p (s v) -> p s v", v=2), rows, 0.0, ALU.is_gt)
 
         def quantize(rounded):
             width = rounded.shape[1] // PACK
@@ -118,31 +131,29 @@ def tile_moe_bdx_mlp_relu_kernel(
 
         def gate_and_turn(e):
             if e + 1 < E:
-                gated = w2_raw[e + 1][:, :, 0:P]
+                gated = w2_raw[e + 1][:, 0:2, 0:P]
             else:
-                gated = stream.tile([P, PACK, P], F32, name="last_gated", bufs=1)[:]
+                gated = stream.tile([P, 2, P], F32, name="last_gated", bufs=1)[:]
             nc.scalar.activation(
-                out=gated,
-                in_=sums[e][:].rearrange("p (m t) -> p t m", t=PACK),
+                out=gated.bitcast(BF16).rearrange("p u (m v) -> p u m v", v=2),
+                in_=sums[e][:].rearrange("p (m u v) -> p u m v", u=2, v=2),
                 func=COPY,
                 scale=gate_cols[:, e : e + 1],
             )
-            dh[e] = psum.tile([P, PACK, C], F32, name="bank")
-            for t in range(PACK):
-                nc.tensor.transpose(dh[e][:, t, :], gated[:, t, :], ident[:])
+            dh[e] = psum.tile([P, 2, C], F32, name="bank")
+            for u in range(2):
+                nc.tensor.transpose(dh[e][:, u, :], gated[:, u, :], ident[:])
 
         def round_da(e):
             if e + DA_LAG < E:
                 da_bf[e] = w2_raw[e + DA_LAG][:, PACK - 1, P : P + C * PACK // 2].bitcast(BF16)
             else:
                 da_bf[e] = stream.tile([P, C * PACK], BF16, name="last_da", align_bytes=64, bufs=DA_LAG)[:]
-            nc.vector.scalar_tensor_tensor(
-                out=da_bf[e].rearrange("p (s t) -> p s t", t=PACK),
-                in0=a_sb[:, :, e * C : (e + 1) * C].rearrange("p t s -> p s t"),
-                scalar=0.0,
-                in1=dh[e][:].rearrange("p t s -> p s t"),
-                op0=ALU.is_gt,
-                op1=ALU.mult,
+            nc.vector.tensor_tensor(
+                out=da_bf[e].rearrange("p (s u v) -> p s u v", u=2, v=2),
+                in0=dh[e][:].bitcast(BF16).rearrange("p u (s v) -> p s u v", v=2),
+                in1=mask[:, :, 2 * e * C : 2 * (e + 1) * C].rearrange("p u (s v) -> p s u v", v=2),
+                op=ALU.mult,
             )
 
         def quantize_da(e):
@@ -195,8 +206,8 @@ def tile_moe_bdx_mlp_relu_kernel(
                 second_product(first + u, h, codes, scales, u * P)
 
         def combine(h, three):
-            one = keep.tile([P, T], F32, name="one%d" % h)
-            two = keep.tile([P, T], F32, name="two%d" % h)
+            one = a_sb[h][:, 0:T]
+            two = a_sb[h][:, T : 2 * T]
             for r, before, after in ((0, None, one), (1, one, two), (2, two, three)):
                 for first, count in LAST_CUTS if (h, r) == (1, 2) else TOKEN_CUTS:
                     tokens = slice(first, first + count)
@@ -215,13 +226,18 @@ def tile_moe_bdx_mlp_relu_kernel(
         nc.sync.dma_start(offs_sb[:], offs)
         for r in range(4):
             nc.sync.dma_start(out=dy_s[r:P:32, :], in_=dy_scales[0].bitcast(I32)[r:16:4, :])
+        nc.sync.dma_start(out=a_sb[0][:], in_=a_rows[0])
         for e in range(HEAD_EXPERTS):
             load_w2(e)
         nc.sync.dma_start(out=gate_rows[0:E, :], in_=gate[0].rearrange("(e c) -> e c", c=C))
-        nc.sync.dma_start(out=a_sb[:], in_=a.rearrange("(p t) s -> p t s", t=PACK))
+        nc.sync.dma_start(out=a_sb[1][:], in_=a_rows[1])
         gate_turned = psum.tile([P, PACK, C], F32, name="bank")
         nc.tensor.transpose(gate_turned[:, 0, :], gate_rows[:], ident[:])
         nc.scalar.copy(out=gate_cols[:], in_=gate_turned[:, 0, 0:E])
+
+        make_mask(0, 0, S, True)
+        make_mask(1, 0, SCALAR_MASK, True)
+        make_mask(1, SCALAR_MASK, S, False)
 
         for step in range(E + DA_LAG):
             if HEAD_EXPERTS <= step < E:
@@ -249,4 +265,4 @@ def tile_moe_bdx_mlp_relu_kernel(
             nc.sync.dma_start(pos_sb[r][:], pos)
         halves(WHOLE_W1, E - WHOLE_W1, 1, nc.scalar.copy, rounded)
         combine(0, rounded[:, 0 : 2 * T].bitcast(F32))
-        combine(1, keep.tile([P, T], F32, name="three")[:])
+        combine(1, a_sb[1][:, 2 * T : 3 * T])

@@ -32,7 +32,7 @@ SCALAR_W2 = 288
 SCALAR_MASK = 8 * C
 HEAD_EXPERTS = 1
 WHOLE_W1 = 14
-DX_GROUPS = [[(0, 4), (4, 6), (10, 4), (14, 2), (16, 2)], [(0, 4), (4, 6), (10, 4), (14, 2), (16, 2)]]
+DX_GROUPS = [[(0, 4), (4, 6), (10, 4), (14, 2), (16, 1), (17, 1)], [(0, 4), (4, 6), (10, 4), (14, 2), (16, 2)]]
 TOKEN_CUTS = [(0, T - S // 8), (T - S // 8, S // 8)]
 LAST_CUTS = [(0, 384), (384, 288), (672, 96)]
 
@@ -178,7 +178,7 @@ def tile_moe_bdx_mlp_relu_kernel(
                 stop=True,
             )
             if n == count // ways - 1:
-                copy = nc.vector.tensor_copy if h == 0 and e == E - 1 else nc.scalar.copy
+                copy = nc.vector.tensor_copy if h == 0 and e >= E - 2 else nc.scalar.copy
                 slots = dx[h][:, first * C : (first + count) * C].rearrange("p (n u c) -> p u n c", u=ways, c=C)
                 copy(out=slots[:, u], in_=dx_banks[first, h, u][:])
 
@@ -204,6 +204,7 @@ def tile_moe_bdx_mlp_relu_kernel(
             codes, scales = quantize(rounded[:, 0 : count * PACK * P])
             for u in range(count):
                 second_product(first + u, h, codes, scales, u * P)
+            return raw.rearrange("p u j k -> p (u j k)")
 
         def combine(h, three):
             one = a_sb[h][:, 0:T]
@@ -224,9 +225,9 @@ def tile_moe_bdx_mlp_relu_kernel(
         nc.vector.memset(dy_s[:], 0)
         nc.sync.dma_start(out=dy_w[:], in_=dy_words[0].rearrange("p t d -> p (t d)").bitcast(I32))
         nc.sync.dma_start(offs_sb[:], offs)
+        nc.sync.dma_start(out=a_sb[0][:], in_=a_rows[0])
         for r in range(4):
             nc.sync.dma_start(out=dy_s[r:P:32, :], in_=dy_scales[0].bitcast(I32)[r:16:4, :])
-        nc.sync.dma_start(out=a_sb[0][:], in_=a_rows[0])
         for e in range(HEAD_EXPERTS):
             load_w2(e)
         nc.sync.dma_start(out=gate_rows[0:E, :], in_=gate[0].rearrange("(e c) -> e c", c=C))
@@ -263,6 +264,6 @@ def tile_moe_bdx_mlp_relu_kernel(
             halves(e, 1, 0, nc.vector.tensor_copy if e % 2 else nc.scalar.copy, rounded)
         for r, pos in enumerate((pos1, pos2, pos3)):
             nc.sync.dma_start(pos_sb[r][:], pos)
-        halves(WHOLE_W1, E - WHOLE_W1, 1, nc.scalar.copy, rounded)
-        combine(0, rounded[:, 0 : 2 * T].bitcast(F32))
+        spent = halves(WHOLE_W1, E - WHOLE_W1, 1, nc.scalar.copy, rounded)
+        combine(0, spent[:, spent.shape[1] - T :])
         combine(1, a_sb[1][:, 2 * T : 3 * T])

@@ -21,6 +21,7 @@ SIGN = mybir.ActivationFunctionType.Sign
 
 P = 128
 PACK = 4
+PAIR = 2
 RUN = 4
 LIST_COLS = 16
 BANKS = 8
@@ -30,11 +31,11 @@ DA_LAG = 2
 GATHERED = 4
 SCALAR_W2 = 288
 SCALAR_MASK = 8 * C
-HEAD_EXPERTS = 1
-WHOLE_W1 = 14
-DX_GROUPS = [[(0, 4), (4, 6), (10, 4), (14, 2), (16, 1), (17, 1)], [(0, 4), (4, 6), (10, 4), (14, 2), (16, 2)]]
+WHOLE_W1 = 12
+FULL_BANKS = [(first, BANK_EXPERTS) for first in range(0, E - 2, BANK_EXPERTS)]
+DX_GROUPS = [FULL_BANKS + [(E - 2, 1), (E - 1, 1)], FULL_BANKS + [(E - 2, 2)]]
 TOKEN_CUTS = [(0, T - S // 8), (T - S // 8, S // 8)]
-LAST_CUTS = [(0, 384), (384, 288), (672, 96)]
+LAST_CUTS = [(0, T // 2), (T // 2, 3 * T // 8), (7 * T // 8, T // 8)]
 
 
 def tile_moe_bdx_mlp_relu_kernel(
@@ -55,9 +56,9 @@ def tile_moe_bdx_mlp_relu_kernel(
         gate_rows = keep.tile([P, C], F32, name="gate_rows")
         gate_cols = keep.tile([P, E], F32, name="gate_cols")
         dx = [keep.tile([P, S], F32, name="dx%d" % h) for h in range(K // P)]
-        a_sb = [keep.tile([P, 2 * S], F32, name="a_sb%d" % u) for u in range(2)]
-        mask = keep.tile([P, 2, 2 * S], BF16, name="mask")
-        a_rows = a.rearrange("(p u v) s -> u p (v s)", u=2, v=2)
+        a_sb = [keep.tile([P, PAIR * S], F32, name="a_sb%d" % u) for u in range(PACK // PAIR)]
+        a_rows = a.rearrange("(p u v) s -> u p (v s)", u=PACK // PAIR, v=PAIR)
+        mask = keep.tile([P, PACK // PAIR, PAIR * S], BF16, name="mask")
 
         g_words, g_scales, w2_raw, w2_bf = {}, {}, {}, {}
         sums, dh, da_bf, da_codes, da_scales, dx_banks = {}, {}, {}, {}, {}, {}
@@ -84,13 +85,13 @@ def tile_moe_bdx_mlp_relu_kernel(
             w2_raw[e] = load_experts(w2, e, 1)[0]
 
         def make_mask(u, first, last, on_scalar):
-            pairs = mask[:, u, 2 * first : 2 * last]
-            rows = a_sb[u][:].rearrange("p (v s) -> p s v", v=2)[:, first:last, :]
+            pairs = mask[:, u, PAIR * first : PAIR * last]
+            rows = a_sb[u][:].rearrange("p (v s) -> p s v", v=PAIR)[:, first:last, :]
             if on_scalar:
-                nc.scalar.activation(out=pairs.rearrange("p (s v) -> p s v", v=2), in_=rows, func=SIGN)
+                nc.scalar.activation(out=pairs.rearrange("p (s v) -> p s v", v=PAIR), in_=rows, func=SIGN)
                 nc.vector.tensor_scalar_max(pairs, pairs, 0.0)
             else:
-                nc.vector.tensor_single_scalar(pairs.rearrange("p (s v) -> p s v", v=2), rows, 0.0, ALU.is_gt)
+                nc.vector.tensor_single_scalar(pairs.rearrange("p (s v) -> p s v", v=PAIR), rows, 0.0, ALU.is_gt)
 
         def quantize(rounded):
             width = rounded.shape[1] // PACK
@@ -112,7 +113,7 @@ def tile_moe_bdx_mlp_relu_kernel(
 
         def round_w2(e):
             w2_bf[e] = stream.tile([P, H * PACK], BF16, name="rounded", align_bytes=64, bufs=3)
-            rest = nc.scalar.copy if e < HEAD_EXPERTS else nc.vector.tensor_copy
+            rest = nc.scalar.copy if e == 0 else nc.vector.tensor_copy
             for copy, first, last in ((nc.scalar.copy, 0, P), (nc.scalar.copy, P, SCALAR_W2), (rest, SCALAR_W2, H)):
                 interleave(copy, w2_bf[e][:, first * PACK : last * PACK], w2_raw[e][:, :, first:last])
 
@@ -131,28 +132,28 @@ def tile_moe_bdx_mlp_relu_kernel(
 
         def gate_and_turn(e):
             if e + 1 < E:
-                gated = w2_raw[e + 1][:, 0:2, 0:P]
+                gated = w2_raw[e + 1][:, 0 : PACK // PAIR, 0:P]
             else:
-                gated = stream.tile([P, 2, P], F32, name="last_gated", bufs=1)[:]
+                gated = stream.tile([P, PACK // PAIR, P], F32, name="last_gated", bufs=1)[:]
             nc.scalar.activation(
-                out=gated.bitcast(BF16).rearrange("p u (m v) -> p u m v", v=2),
-                in_=sums[e][:].rearrange("p (m u v) -> p u m v", u=2, v=2),
+                out=gated.bitcast(BF16).rearrange("p u (m v) -> p u m v", v=PAIR),
+                in_=sums[e][:].rearrange("p (m u v) -> p u m v", u=PACK // PAIR, v=PAIR),
                 func=COPY,
                 scale=gate_cols[:, e : e + 1],
             )
-            dh[e] = psum.tile([P, 2, C], F32, name="bank")
-            for u in range(2):
+            dh[e] = psum.tile([P, PACK // PAIR, C], F32, name="bank")
+            for u in range(PACK // PAIR):
                 nc.tensor.transpose(dh[e][:, u, :], gated[:, u, :], ident[:])
 
-        def round_da(e):
+        def mask_da(e):
             if e + DA_LAG < E:
-                da_bf[e] = w2_raw[e + DA_LAG][:, PACK - 1, P : P + C * PACK // 2].bitcast(BF16)
+                da_bf[e] = w2_raw[e + DA_LAG][:, PACK - 1, P : P + C * PACK // PAIR].bitcast(BF16)
             else:
                 da_bf[e] = stream.tile([P, C * PACK], BF16, name="last_da", align_bytes=64, bufs=DA_LAG)[:]
             nc.vector.tensor_tensor(
-                out=da_bf[e].rearrange("p (s u v) -> p s u v", u=2, v=2),
-                in0=dh[e][:].bitcast(BF16).rearrange("p u (s v) -> p s u v", v=2),
-                in1=mask[:, :, 2 * e * C : 2 * (e + 1) * C].rearrange("p u (s v) -> p s u v", v=2),
+                out=da_bf[e].rearrange("p (s u v) -> p s u v", u=PACK // PAIR, v=PAIR),
+                in0=dh[e][:].bitcast(BF16).rearrange("p u (s v) -> p s u v", v=PAIR),
+                in1=mask[:, :, PAIR * e * C : PAIR * (e + 1) * C].rearrange("p u (s v) -> p s u v", v=PAIR),
                 op=ALU.mult,
             )
 
@@ -163,13 +164,11 @@ def tile_moe_bdx_mlp_relu_kernel(
 
         def second_product(e, h, codes, scales, column):
             first, count = [group for group in DX_GROUPS[h] if group[0] <= e][-1]
-            ways = 2 if count > BANK_EXPERTS else 1
-            n, u = divmod(e - first, ways)
-            if n == 0:
-                dx_banks[first, h, u] = psum.tile([P, count // ways, C], F32, name="bank")
+            if e == first:
+                dx_banks[first, h] = psum.tile([P, count * C], F32, name="bank")
             cols = slice(column, column + P)
             nc.tensor.matmul_mx(
-                out=dx_banks[first, h, u][:, n, :],
+                out=dx_banks[first, h][:, (e - first) * C : (e - first + 1) * C],
                 lhsT=codes[:, cols].bitcast(FP8X4),
                 lhsT_scale=scales[:, cols],
                 rhs=da_codes[e][:].bitcast(FP8X4),
@@ -177,30 +176,28 @@ def tile_moe_bdx_mlp_relu_kernel(
                 start=True,
                 stop=True,
             )
-            if n == count // ways - 1:
-                copy = nc.vector.tensor_copy if h == 0 and e >= E - 2 else nc.scalar.copy
-                slots = dx[h][:, first * C : (first + count) * C].rearrange("p (n u c) -> p u n c", u=ways, c=C)
-                copy(out=slots[:, u], in_=dx_banks[first, h, u][:])
+            if e == first + count - 1:
+                copy = nc.vector.tensor_copy if h == 0 and count == 1 else nc.scalar.copy
+                copy(out=dx[h][:, first * C : (first + count) * C], in_=dx_banks[first, h][:])
 
         def whole_pair(first):
-            opens_later_group = first in [group[0] for group in DX_GROUPS[0][1:3]]
             rounded = []
             for u, raw in enumerate(load_experts(w1, first, 2)):
                 rounded.append(stream.tile([P, PACK * K], BF16, name="w1_bf", align_bytes=64, bufs=5))
-                on_scalar = first < DX_GROUPS[0][1][0] or (u == 0 and not opens_later_group)
+                on_scalar = first < BANK_EXPERTS or (u == 0 and first % BANK_EXPERTS != 0)
                 interleave(nc.scalar.copy if on_scalar else nc.vector.tensor_copy, rounded[u][:], raw)
             for u in range(2):
                 codes, scales = quantize(rounded[u][:])
                 for h in range(K // P):
                     second_product(first + u, h, codes, scales, h * P)
 
-        def halves(first, count, h, copy, rounded):
+        def halves(first, count, h, copies, rounded):
             raw = loaded_tile()[:, 0 : count * PACK * P].rearrange("p (u j k) -> p u j k", u=count, j=PACK)
             for u in range(count):
                 rows = w1[first + u].rearrange("(p j) k -> p j k", j=PACK)
                 nc.sync.dma_start(out=raw[:, u], in_=rows[:, :, h * P : (h + 1) * P])
             for u in range(count):
-                interleave(copy, rounded[:, u * PACK * P : (u + 1) * PACK * P], raw[:, u])
+                interleave(copies[u % len(copies)], rounded[:, u * PACK * P : (u + 1) * PACK * P], raw[:, u])
             codes, scales = quantize(rounded[:, 0 : count * PACK * P])
             for u in range(count):
                 second_product(first + u, h, codes, scales, u * P)
@@ -228,8 +225,7 @@ def tile_moe_bdx_mlp_relu_kernel(
         nc.sync.dma_start(out=a_sb[0][:], in_=a_rows[0])
         for r in range(4):
             nc.sync.dma_start(out=dy_s[r:P:32, :], in_=dy_scales[0].bitcast(I32)[r:16:4, :])
-        for e in range(HEAD_EXPERTS):
-            load_w2(e)
+        load_w2(0)
         nc.sync.dma_start(out=gate_rows[0:E, :], in_=gate[0].rearrange("(e c) -> e c", c=C))
         nc.sync.dma_start(out=a_sb[1][:], in_=a_rows[1])
         gate_turned = psum.tile([P, PACK, C], F32, name="bank")
@@ -241,7 +237,7 @@ def tile_moe_bdx_mlp_relu_kernel(
         make_mask(1, SCALAR_MASK, S, False)
 
         for step in range(E + DA_LAG):
-            if HEAD_EXPERTS <= step < E:
+            if 1 <= step < E:
                 load_w2(step)
             if step < E:
                 round_w2(step)
@@ -251,19 +247,22 @@ def tile_moe_bdx_mlp_relu_kernel(
             if 1 <= step <= E:
                 gate_and_turn(step - 1)
             if step >= DA_LAG:
-                round_da(step - DA_LAG)
+                mask_da(step - DA_LAG)
                 quantize_da(step - DA_LAG)
+
+        def small_rounded_tile():
+            return stream.tile([P, PACK * K], BF16, name="w1_bf", align_bytes=64, bufs=5)
 
         for first in range(0, WHOLE_W1, 2):
             whole_pair(first)
-        late = stream.tile([P, H * PACK], BF16, name="rounded", align_bytes=64, bufs=3)
-        for e in range(WHOLE_W1, E):
-            rounded = late
-            if e < E - 1:
-                rounded = stream.tile([P, 2 * PACK * P], BF16, name="w1_bf", align_bytes=64, bufs=5)
-            halves(e, 1, 0, nc.vector.tensor_copy if e % 2 else nc.scalar.copy, rounded)
+        late_rounded = stream.tile([P, H * PACK], BF16, name="rounded", align_bytes=64, bufs=3)
+        for first in range(WHOLE_W1, E - 2, 2):
+            halves(first, 2, 0, [nc.scalar.copy, nc.vector.tensor_copy], small_rounded_tile())
+        halves(E - 2, 1, 0, [nc.vector.tensor_copy], small_rounded_tile())
+        halves(E - 1, 1, 0, [nc.vector.tensor_copy], late_rounded)
         for r, pos in enumerate((pos1, pos2, pos3)):
             nc.sync.dma_start(pos_sb[r][:], pos)
-        spent = halves(WHOLE_W1, E - WHOLE_W1, 1, nc.scalar.copy, rounded)
+        halves(WHOLE_W1, BANK_EXPERTS, 1, [nc.scalar.copy], late_rounded)
+        spent = halves(E - 2, 2, 1, [nc.scalar.copy], small_rounded_tile())
         combine(0, spent[:, spent.shape[1] - T :])
         combine(1, a_sb[1][:, 2 * T : 3 * T])

@@ -26,11 +26,12 @@ RUN = 4
 LIST_COLS = 16
 BANKS = 8
 BANK_EXPERTS = 4
-LOAD_RING = 12
+LOAD_RING = 6
 DA_LAG = 2
 GATHERED = 4
 SCALAR_W2 = 288
 SCALAR_MASK = 8 * C
+PAIRED_W2 = 12
 WHOLE_W1 = 12
 FULL_BANKS = [(first, BANK_EXPERTS) for first in range(0, E - 2, BANK_EXPERTS)]
 DX_GROUPS = [FULL_BANKS + [(E - 2, 1), (E - 1, 1)], FULL_BANKS + [(E - 2, 2)]]
@@ -64,7 +65,7 @@ def tile_moe_bdx_mlp_relu_kernel(
         sums, dh, da_bf, da_codes, da_scales, dx_banks = {}, {}, {}, {}, {}, {}
 
         def loaded_tile():
-            return stream.tile([P, PACK * H], F32, name="loaded", align_bytes=64, bufs=LOAD_RING)
+            return stream.tile([P, 2 * PACK * H], F32, name="loaded", align_bytes=64, bufs=LOAD_RING)
 
         def interleave(copy, rounded, raw):
             copy(
@@ -81,8 +82,9 @@ def tile_moe_bdx_mlp_relu_kernel(
             )
             return [raw[:, u * width : (u + 1) * width].rearrange("p (j c) -> p j c", j=PACK) for u in range(count)]
 
-        def load_w2(e):
-            w2_raw[e] = load_experts(w2, e, 1)[0]
+        def load_w2(first, count):
+            for u, raw in enumerate(load_experts(w2, first, count)):
+                w2_raw[first + u] = raw
 
         def make_mask(u, first, last, on_scalar):
             pairs = mask[:, u, PAIR * first : PAIR * last]
@@ -225,7 +227,7 @@ def tile_moe_bdx_mlp_relu_kernel(
         nc.sync.dma_start(out=a_sb[0][:], in_=a_rows[0])
         for r in range(4):
             nc.sync.dma_start(out=dy_s[r:P:32, :], in_=dy_scales[0].bitcast(I32)[r:16:4, :])
-        load_w2(0)
+        load_w2(0, 1)
         nc.sync.dma_start(out=gate_rows[0:E, :], in_=gate[0].rearrange("(e c) -> e c", c=C))
         nc.sync.dma_start(out=a_sb[1][:], in_=a_rows[1])
         gate_turned = psum.tile([P, PACK, C], F32, name="bank")
@@ -237,8 +239,10 @@ def tile_moe_bdx_mlp_relu_kernel(
         make_mask(1, SCALAR_MASK, S, False)
 
         for step in range(E + DA_LAG):
-            if 1 <= step < E:
-                load_w2(step)
+            if PAIRED_W2 < step < E:
+                load_w2(step, 1)
+            elif step < PAIRED_W2 and step % 2 == 1:
+                load_w2(step, 2)
             if step < E:
                 round_w2(step)
                 if step % GATHERED == 0:

@@ -27,14 +27,18 @@ LIST_COLS = 16
 BANKS = 8
 BANK_EXPERTS = 4
 LOAD_RING = 6
-DA_LAG = 2
+W2_LOADS = [(0, 1)] + [(first, 2) for first in range(1, E - 1, 2)] + [(E - 1, 1)]
+DA_LAG = 3
 GATHERED = 4
-SCALAR_W2 = 288
+SCALAR_W2 = 256
 SCALAR_MASK = 8 * C
-PAIRED_W2 = 12
-WHOLE_W1 = 12
+PAIRED_W2 = 16
+WHOLE_W1 = 6
 FULL_BANKS = [(first, BANK_EXPERTS) for first in range(0, E - 2, BANK_EXPERTS)]
-DX_GROUPS = [FULL_BANKS + [(E - 2, 1), (E - 1, 1)], FULL_BANKS + [(E - 2, 2)]]
+LATE_BANKS = [(first, BANK_EXPERTS) for first in range(WHOLE_W1, E, BANK_EXPERTS)]
+WHOLE_BANKS = [(0, BANK_EXPERTS), (BANK_EXPERTS, 2)]
+DX_GROUPS = [WHOLE_BANKS + LATE_BANKS[:2] + [(E - 4, 2), (E - 2, 1), (E - 1, 1)], WHOLE_BANKS + LATE_BANKS]
+WIDE = 8
 TOKEN_CUTS = [(0, T - S // 8), (T - S // 8, S // 8)]
 LAST_CUTS = [(0, T // 2), (T // 2, 3 * T // 8), (7 * T // 8, T // 8)]
 
@@ -59,10 +63,10 @@ def tile_moe_bdx_mlp_relu_kernel(
         dx = [keep.tile([P, S], F32, name="dx%d" % h) for h in range(K // P)]
         a_sb = [keep.tile([P, PAIR * S], F32, name="a_sb%d" % u) for u in range(PACK // PAIR)]
         a_rows = a.rearrange("(p u v) s -> u p (v s)", u=PACK // PAIR, v=PAIR)
-        mask = keep.tile([P, PACK // PAIR, PAIR * S], BF16, name="mask")
+        mask = keep.tile([P, PACK // PAIR, PAIR * S], BF16, name="mask", align_bytes=64)
 
-        g_words, g_scales, w2_raw, w2_bf = {}, {}, {}, {}
-        sums, dh, da_bf, da_codes, da_scales, dx_banks = {}, {}, {}, {}, {}, {}
+        g_words, g_scales, w2_tiles, w2_raw, w2_bf = {}, {}, {}, {}, {}
+        sums, dh, da_codes, da_scales, dx_banks = {}, {}, {}, {}, {}
 
         def loaded_tile():
             return stream.tile([P, 2 * PACK * H], F32, name="loaded", align_bytes=64, bufs=LOAD_RING)
@@ -73,9 +77,9 @@ def tile_moe_bdx_mlp_relu_kernel(
                 in_=raw.rearrange("p j (c i) -> p c j i", i=RUN),
             )
 
-        def load_experts(weights, first, count):
+        def load_experts(weights, first, count, tile):
             width = PACK * weights.shape[2]
-            raw = loaded_tile()[:, 0 : count * width]
+            raw = tile[:, 0 : count * width]
             nc.sync.dma_start(
                 out=raw.rearrange("p (u r) -> p u r", u=count),
                 in_=weights[first : first + count].rearrange("u (p j) c -> p u (j c)", j=PACK),
@@ -83,7 +87,8 @@ def tile_moe_bdx_mlp_relu_kernel(
             return [raw[:, u * width : (u + 1) * width].rearrange("p (j c) -> p j c", j=PACK) for u in range(count)]
 
         def load_w2(first, count):
-            for u, raw in enumerate(load_experts(w2, first, count)):
+            w2_tiles[first] = loaded_tile()
+            for u, raw in enumerate(load_experts(w2, first, count, w2_tiles[first])):
                 w2_raw[first + u] = raw
 
         def make_mask(u, first, last, on_scalar):
@@ -97,8 +102,9 @@ def tile_moe_bdx_mlp_relu_kernel(
 
         def quantize(rounded):
             width = rounded.shape[1] // PACK
-            codes = stream.tile([P, width], U32, name="w_codes", align_bytes=64, bufs=4)
-            scales = stream.tile([P, width], U8, name="w_scales", align_bytes=64, bufs=4)
+            kind, ring = ("w", 4) if width <= H else ("wide", 1)
+            codes = stream.tile([P, width], U32, name=kind + "_codes", align_bytes=64, bufs=ring)
+            scales = stream.tile([P, width], U8, name=kind + "_scales", align_bytes=64, bufs=ring)
             nc.vector.quantize_mx(out=codes[:].bitcast(FP8X4), scales=scales[:], in_=rounded)
             return codes, scales
 
@@ -113,10 +119,12 @@ def tile_moe_bdx_mlp_relu_kernel(
                 g_words[first + u] = words[:, u * C : (u + 1) * C]
                 g_scales[first + u] = scales[:, u * C : (u + 1) * C]
 
-        def round_w2(e):
+        def round_w2(e, u):
             w2_bf[e] = stream.tile([P, H * PACK], BF16, name="rounded", align_bytes=64, bufs=3)
             rest = nc.scalar.copy if e == 0 else nc.vector.tensor_copy
-            for copy, first, last in ((nc.scalar.copy, 0, P), (nc.scalar.copy, P, SCALAR_W2), (rest, SCALAR_W2, H)):
+            copies = (nc.scalar.copy, rest) if u == 0 else (rest, nc.scalar.copy)
+            for n, copy in enumerate(copies):
+                first, last = n * H // 2, (n + 1) * H // 2
                 interleave(copy, w2_bf[e][:, first * PACK : last * PACK], w2_raw[e][:, :, first:last])
 
         def first_product(e):
@@ -132,11 +140,8 @@ def tile_moe_bdx_mlp_relu_kernel(
                 stop=True,
             )
 
-        def gate_and_turn(e):
-            if e + 1 < E:
-                gated = w2_raw[e + 1][:, 0 : PACK // PAIR, 0:P]
-            else:
-                gated = stream.tile([P, PACK // PAIR, P], F32, name="last_gated", bufs=1)[:]
+        def gate_and_turn(e, words):
+            gated = words.rearrange("p (u m) -> p u m", m=P)
             nc.scalar.activation(
                 out=gated.bitcast(BF16).rearrange("p u (m v) -> p u m v", v=PAIR),
                 in_=sums[e][:].rearrange("p (m u v) -> p u m v", u=PACK // PAIR, v=PAIR),
@@ -147,22 +152,21 @@ def tile_moe_bdx_mlp_relu_kernel(
             for u in range(PACK // PAIR):
                 nc.tensor.transpose(dh[e][:, u, :], gated[:, u, :], ident[:])
 
-        def mask_da(e):
-            if e + DA_LAG < E:
-                da_bf[e] = w2_raw[e + DA_LAG][:, PACK - 1, P : P + C * PACK // PAIR].bitcast(BF16)
-            else:
-                da_bf[e] = stream.tile([P, C * PACK], BF16, name="last_da", align_bytes=64, bufs=DA_LAG)[:]
+        def mask_da(e, rounded):
             nc.vector.tensor_tensor(
-                out=da_bf[e].rearrange("p (s u v) -> p s u v", u=PACK // PAIR, v=PAIR),
+                out=rounded.rearrange("p (s u v) -> p s u v", u=PACK // PAIR, v=PAIR),
                 in0=dh[e][:].bitcast(BF16).rearrange("p u (s v) -> p s u v", v=PAIR),
                 in1=mask[:, :, PAIR * e * C : PAIR * (e + 1) * C].rearrange("p u (s v) -> p s u v", v=PAIR),
                 op=ALU.mult,
             )
 
-        def quantize_da(e):
-            da_codes[e] = keep.tile([P, C], U32, name="da_codes%d" % e, align_bytes=64)
-            da_scales[e] = keep.tile([P, C], U8, name="da_scales%d" % e, align_bytes=64)
-            nc.vector.quantize_mx(out=da_codes[e][:].bitcast(FP8X4), scales=da_scales[e][:], in_=da_bf[e])
+        def quantize_da(first, count, rounded):
+            codes = keep.tile([P, count * C], U32, name="da_codes%d" % first, align_bytes=64)
+            scales = keep.tile([P, count * C], U8, name="da_scales%d" % first, align_bytes=64)
+            nc.vector.quantize_mx(out=codes[:].bitcast(FP8X4), scales=scales[:], in_=rounded)
+            for u in range(count):
+                da_codes[first + u] = codes[:, u * C : (u + 1) * C]
+                da_scales[first + u] = scales[:, u * C : (u + 1) * C]
 
         def second_product(e, h, codes, scales, column):
             first, count = [group for group in DX_GROUPS[h] if group[0] <= e][-1]
@@ -173,8 +177,8 @@ def tile_moe_bdx_mlp_relu_kernel(
                 out=dx_banks[first, h][:, (e - first) * C : (e - first + 1) * C],
                 lhsT=codes[:, cols].bitcast(FP8X4),
                 lhsT_scale=scales[:, cols],
-                rhs=da_codes[e][:].bitcast(FP8X4),
-                rhs_scale=da_scales[e][:],
+                rhs=da_codes[e].bitcast(FP8X4),
+                rhs_scale=da_scales[e],
                 start=True,
                 stop=True,
             )
@@ -184,40 +188,53 @@ def tile_moe_bdx_mlp_relu_kernel(
 
         def whole_pair(first):
             rounded = []
-            for u, raw in enumerate(load_experts(w1, first, 2)):
+            for u, raw in enumerate(load_experts(w1, first, 2, loaded_tile())):
                 rounded.append(stream.tile([P, PACK * K], BF16, name="w1_bf", align_bytes=64, bufs=5))
-                on_scalar = first < BANK_EXPERTS or (u == 0 and first % BANK_EXPERTS != 0)
+                on_scalar = u == 0 and first < BANK_EXPERTS
                 interleave(nc.scalar.copy if on_scalar else nc.vector.tensor_copy, rounded[u][:], raw)
             for u in range(2):
                 codes, scales = quantize(rounded[u][:])
                 for h in range(K // P):
                     second_product(first + u, h, codes, scales, h * P)
 
-        def halves(first, count, h, copies, rounded):
-            raw = loaded_tile()[:, 0 : count * PACK * P].rearrange("p (u j k) -> p u j k", u=count, j=PACK)
-            for u in range(count):
-                rows = w1[first + u].rearrange("(p j) k -> p j k", j=PACK)
-                nc.sync.dma_start(out=raw[:, u], in_=rows[:, :, h * P : (h + 1) * P])
-            for u in range(count):
-                interleave(copies[u % len(copies)], rounded[:, u * PACK * P : (u + 1) * PACK * P], raw[:, u])
-            codes, scales = quantize(rounded[:, 0 : count * PACK * P])
+        def load_halves(first, count, h, copies, rounded):
+            flat = loaded_tile()[:, 0 : count * PACK * P]
+            rows = w1[first : first + count].rearrange("u (p j) k -> p j u k", j=PACK)
+            nc.sync.dma_start(
+                out=flat.rearrange("p (j u k) -> p j u k", u=count, j=PACK), in_=rows[:, :, :, h * P : (h + 1) * P]
+            )
+            raw = flat.rearrange("p (j c) -> p j c", j=PACK)
+            share = count * P // len(copies)
+            for n, copy in enumerate(copies):
+                interleave(copy, rounded[:, n * share * PACK : (n + 1) * share * PACK], raw[:, :, n * share : (n + 1) * share])
+            return flat
+
+        def multiply_halves(first, count, h, rounded):
+            codes, scales = quantize(rounded)
             for u in range(count):
                 second_product(first + u, h, codes, scales, u * P)
-            return raw.rearrange("p u j k -> p (u j k)")
 
-        def combine(h, three):
-            one = a_sb[h][:, 0:T]
-            two = a_sb[h][:, T : 2 * T]
-            for r, before, after in ((0, None, one), (1, one, two), (2, two, three)):
-                for first, count in LAST_CUTS if (h, r) == (1, 2) else TOKEN_CUTS:
-                    tokens = slice(first, first + count)
-                    picked = dx[h][:].indirect(pos_sb[r][:, first // LIST_COLS : (first + count) // LIST_COLS])
-                    if r == 0:
-                        nc.vector.tensor_copy(after[:, tokens], picked)
-                    else:
-                        nc.vector.tensor_tensor(after[:, tokens], picked, before[:, tokens], ALU.add)
-                    if r == 2:
-                        nc.sync.dma_start(out=out[h * P : (h + 1) * P, tokens], in_=three[:, tokens])
+        def first_halves(first, count, copies):
+            rounded = stream.tile([P, PACK * K], BF16, name="w1_bf", align_bytes=64, bufs=5)[:, 0 : count * PACK * P]
+            load_halves(first, count, 0, copies, rounded)
+            multiply_halves(first, count, 0, rounded)
+
+        def pick(h, r, first, count, before, after):
+            picked = dx[h][:].indirect(pos_sb[r][:, first // LIST_COLS : (first + count) // LIST_COLS])
+            if r == 0:
+                nc.vector.tensor_copy(after, picked)
+            else:
+                nc.vector.tensor_tensor(after, picked, before, ALU.add)
+            if r == 2:
+                nc.sync.dma_start(out=out[h * P : (h + 1) * P, first : first + count], in_=after)
+
+        def partial(h, r, first, count):
+            return a_sb[h][:, r * T + first : r * T + first + count]
+
+        def pick_round(h, r, cuts):
+            for first, count in cuts:
+                before = partial(h, r - 1, first, count) if r else None
+                pick(h, r, first, count, before, partial(h, r, first, count))
 
         make_identity(nc, ident[:])
         nc.gpsimd.memset(gate_rows[:], 0.0)
@@ -238,35 +255,69 @@ def tile_moe_bdx_mlp_relu_kernel(
         make_mask(1, 0, SCALAR_MASK, True)
         make_mask(1, SCALAR_MASK, S, False)
 
-        for step in range(E + DA_LAG):
-            if PAIRED_W2 < step < E:
-                load_w2(step, 1)
-            elif step < PAIRED_W2 and step % 2 == 1:
-                load_w2(step, 2)
-            if step < E:
-                round_w2(step)
-                if step % GATHERED == 0:
-                    gather(step)
-                first_product(step)
-            if 1 <= step <= E:
-                gate_and_turn(step - 1)
-            if step >= DA_LAG:
-                mask_da(step - DA_LAG)
-                quantize_da(step - DA_LAG)
-
-        def small_rounded_tile():
-            return stream.tile([P, PACK * K], BF16, name="w1_bf", align_bytes=64, bufs=5)
+        round_w2(0, 0)
+        for first in range(0, E, GATHERED):
+            gather(first)
+            if first == 0:
+                first_product(0)
+        zone = C * PACK // PAIR
+        last_load = len(W2_LOADS) - 1
+        for step in range(1, last_load + 3):
+            tile_first, loaded = W2_LOADS[min(step, last_load)]
+            late = max(step - last_load, 0)
+            if not late:
+                load_w2(tile_first, loaded)
+                for u in range(loaded):
+                    round_w2(tile_first + u, u)
+            else:
+                loaded = 0
+            tile = w2_tiles[tile_first]
+            if step >= 2:
+                first, count = W2_LOADS[step - 2]
+                start = PACK * H - zone + late * 2 * zone
+                da_bf = tile[:, start : start + count * zone].bitcast(BF16)
+                for u in range(count):
+                    mask_da(first + u, da_bf[:, u * C * PACK : (u + 1) * C * PACK])
+            if loaded:
+                first_product(tile_first)
+            if step >= 2:
+                quantize_da(first, count, da_bf)
+            if loaded == 2:
+                first_product(tile_first + 1)
+            if step - 1 <= last_load:
+                first, count = W2_LOADS[step - 1]
+                for u in range(count):
+                    start = 2 * PACK * H - 2 * zone if late else u * (2 * PACK * H - zone)
+                    gate_and_turn(first + u, tile[:, start : start + zone])
 
         for first in range(0, WHOLE_W1, 2):
             whole_pair(first)
-        late_rounded = stream.tile([P, H * PACK], BF16, name="rounded", align_bytes=64, bufs=3)
-        for first in range(WHOLE_W1, E - 2, 2):
-            halves(first, 2, 0, [nc.scalar.copy, nc.vector.tensor_copy], small_rounded_tile())
-        halves(E - 2, 1, 0, [nc.vector.tensor_copy], small_rounded_tile())
-        halves(E - 1, 1, 0, [nc.vector.tensor_copy], late_rounded)
+        for first in range(WHOLE_W1, E - 4, BANK_EXPERTS):
+            rounded = stream.tile([P, H * PACK], BF16, name="rounded", align_bytes=64, bufs=3)
+            load_halves(first, 2, 0, [nc.scalar.copy], rounded[:, 0 : 2 * PACK * P])
+            load_halves(first + 2, 2, 0, [nc.vector.tensor_copy], rounded[:, 2 * PACK * P :])
+            multiply_halves(first, BANK_EXPERTS, 0, rounded[:])
+        first_halves(E - 4, 2, [nc.scalar.copy, nc.vector.tensor_copy])
+        first_halves(E - 2, 1, [nc.vector.tensor_copy])
+        first_halves(E - 1, 1, [nc.vector.tensor_copy])
         for r, pos in enumerate((pos1, pos2, pos3)):
             nc.sync.dma_start(pos_sb[r][:], pos)
-        halves(WHOLE_W1, BANK_EXPERTS, 1, [nc.scalar.copy], late_rounded)
-        spent = halves(E - 2, 2, 1, [nc.scalar.copy], small_rounded_tile())
-        combine(0, spent[:, spent.shape[1] - T :])
-        combine(1, a_sb[1][:, 2 * T : 3 * T])
+        late = mask[:].rearrange("p u s -> p (u s)")
+        spent = {}
+
+        def late_rounded(first, count):
+            return late[:, (first - WHOLE_W1) * PACK * P : (first - WHOLE_W1 + count) * PACK * P]
+
+        for first in range(WHOLE_W1, E, 2):
+            spent[first] = load_halves(first, 2, 1, [nc.scalar.copy], late_rounded(first, 2))
+            if first + 2 == WHOLE_W1 + WIDE:
+                multiply_halves(WHOLE_W1, WIDE, 1, late_rounded(WHOLE_W1, WIDE))
+            elif first >= WHOLE_W1 + WIDE:
+                multiply_halves(first, 2, 1, late_rounded(first, 2))
+        pick_round(0, 0, TOKEN_CUTS)
+        pick_round(0, 1, TOKEN_CUTS)
+        for (first, count), tile in zip(TOKEN_CUTS, (spent[WHOLE_W1 + WIDE - 2], spent[E - 2])):
+            pick(0, 2, first, count, partial(0, 1, first, count), tile[:, 0:count])
+        pick_round(1, 0, TOKEN_CUTS)
+        pick_round(1, 1, TOKEN_CUTS)
+        pick_round(1, 2, LAST_CUTS)

@@ -28,18 +28,17 @@ BANKS = 8
 BANK_EXPERTS = 4
 LOAD_RING = 6
 W2_LOADS = [(0, 1)] + [(first, 2) for first in range(1, E - 1, 2)] + [(E - 1, 1)]
+EARLY_A = 14
 DA_LAG = 3
 GATHERED = 4
 SCALAR_W2 = 256
-SCALAR_MASK = 8 * C
+SCALAR_MASK = 8
 PAIRED_W2 = 16
-WHOLE_W1 = 6
-FULL_BANKS = [(first, BANK_EXPERTS) for first in range(0, E - 2, BANK_EXPERTS)]
-LATE_BANKS = [(first, BANK_EXPERTS) for first in range(WHOLE_W1, E, BANK_EXPERTS)]
-WHOLE_BANKS = [(0, BANK_EXPERTS), (BANK_EXPERTS, 2)]
-DX_GROUPS = [WHOLE_BANKS + LATE_BANKS[:2] + [(E - 4, 2), (E - 2, 1), (E - 1, 1)], WHOLE_BANKS + LATE_BANKS]
-WIDE = 8
-TOKEN_CUTS = [(0, T - S // 8), (T - S // 8, S // 8)]
+WHOLE_W1 = 8
+DX_GROUPS = [(0, 3), (3, 4), (7, 4), (11, 4), (15, 2), (17, 1)]
+FIRST_HALVES = [(8, 9), (10, 11), (12, 13), (14, 15), (16,), (17,)]
+SECOND_HALVES = [(8, 9), (11, 12), (10, 14), (13, 15), (16,), (17,)]
+TOKEN_CUTS = [(0, T // 2), (T // 2, T // 2)]
 LAST_CUTS = [(0, T // 2), (T // 2, 3 * T // 8), (7 * T // 8, T // 8)]
 
 
@@ -61,11 +60,13 @@ def tile_moe_bdx_mlp_relu_kernel(
         gate_rows = keep.tile([P, C], F32, name="gate_rows")
         gate_cols = keep.tile([P, E], F32, name="gate_cols")
         dx = [keep.tile([P, S], F32, name="dx%d" % h) for h in range(K // P)]
-        a_sb = [keep.tile([P, PAIR * S], F32, name="a_sb%d" % u) for u in range(PACK // PAIR)]
-        a_rows = a.rearrange("(p u v) s -> u p (v s)", u=PACK // PAIR, v=PAIR)
-        mask = keep.tile([P, PACK // PAIR, PAIR * S], BF16, name="mask", align_bytes=64)
+        a_early = keep.tile([P, PACK * EARLY_A * C], F32, name="a_early")
+        a_late = keep.tile([P, PACK * (E - EARLY_A) * C], F32, name="a_late")
+        a_rows = a.rearrange("(p j) s -> p j s", j=PACK)
+        mask = keep.tile([P, PACK * S], BF16, name="mask", align_bytes=64)
 
         g_words, g_scales, w2_tiles, w2_raw, w2_bf = {}, {}, {}, {}, {}
+        dx_done = set()
         sums, dh, da_codes, da_scales, dx_banks = {}, {}, {}, {}, {}
 
         def loaded_tile():
@@ -91,20 +92,27 @@ def tile_moe_bdx_mlp_relu_kernel(
             for u, raw in enumerate(load_experts(w2, first, count, w2_tiles[first])):
                 w2_raw[first + u] = raw
 
-        def make_mask(u, first, last, on_scalar):
-            pairs = mask[:, u, PAIR * first : PAIR * last]
-            rows = a_sb[u][:].rearrange("p (v s) -> p s v", v=PAIR)[:, first:last, :]
+        def load_a(tile, first, last):
+            rows = tile[:].rearrange("p (j s) -> p j s", j=PACK)
+            nc.sync.dma_start(out=rows, in_=a_rows[:, :, first * C : last * C])
+            return rows
+
+        def sign_of(out, in_):
+            nc.scalar.activation(out=out, in_=in_, func=SIGN)
+
+        def positive(out, in_):
+            nc.vector.tensor_single_scalar(out, in_, 0.0, ALU.is_gt)
+
+        def make_mask(first, last, rows, on_scalar):
+            part = mask[:, PACK * first * C : PACK * last * C]
+            interleave(sign_of if on_scalar else positive, part, rows)
             if on_scalar:
-                nc.scalar.activation(out=pairs.rearrange("p (s v) -> p s v", v=PAIR), in_=rows, func=SIGN)
-                nc.vector.tensor_scalar_max(pairs, pairs, 0.0)
-            else:
-                nc.vector.tensor_single_scalar(pairs.rearrange("p (s v) -> p s v", v=PAIR), rows, 0.0, ALU.is_gt)
+                nc.vector.tensor_scalar_max(part, part, 0.0)
 
         def quantize(rounded):
             width = rounded.shape[1] // PACK
-            kind, ring = ("w", 4) if width <= H else ("wide", 1)
-            codes = stream.tile([P, width], U32, name=kind + "_codes", align_bytes=64, bufs=ring)
-            scales = stream.tile([P, width], U8, name=kind + "_scales", align_bytes=64, bufs=ring)
+            codes = stream.tile([P, width], U32, name="w_codes", align_bytes=64, bufs=5)
+            scales = stream.tile([P, width], U8, name="w_scales", align_bytes=64, bufs=5)
             nc.vector.quantize_mx(out=codes[:].bitcast(FP8X4), scales=scales[:], in_=rounded)
             return codes, scales
 
@@ -120,7 +128,7 @@ def tile_moe_bdx_mlp_relu_kernel(
                 g_scales[first + u] = scales[:, u * C : (u + 1) * C]
 
         def round_w2(e, u):
-            w2_bf[e] = stream.tile([P, H * PACK], BF16, name="rounded", align_bytes=64, bufs=3)
+            w2_bf[e] = rounded_tile()
             rest = nc.scalar.copy if e == 0 else nc.vector.tensor_copy
             copies = (nc.scalar.copy, rest) if u == 0 else (rest, nc.scalar.copy)
             for n, copy in enumerate(copies):
@@ -156,7 +164,7 @@ def tile_moe_bdx_mlp_relu_kernel(
             nc.vector.tensor_tensor(
                 out=rounded.rearrange("p (s u v) -> p s u v", u=PACK // PAIR, v=PAIR),
                 in0=dh[e][:].bitcast(BF16).rearrange("p u (s v) -> p s u v", v=PAIR),
-                in1=mask[:, :, PAIR * e * C : PAIR * (e + 1) * C].rearrange("p u (s v) -> p s u v", v=PAIR),
+                in1=mask[:, PACK * e * C : PACK * (e + 1) * C].rearrange("p (s u v) -> p s u v", u=PACK // PAIR, v=PAIR),
                 op=ALU.mult,
             )
 
@@ -169,9 +177,10 @@ def tile_moe_bdx_mlp_relu_kernel(
                 da_scales[first + u] = scales[:, u * C : (u + 1) * C]
 
         def second_product(e, h, codes, scales, column):
-            first, count = [group for group in DX_GROUPS[h] if group[0] <= e][-1]
-            if e == first:
+            first, count = [group for group in DX_GROUPS if group[0] <= e][-1]
+            if (first, h) not in dx_banks:
                 dx_banks[first, h] = psum.tile([P, count * C], F32, name="bank")
+            dx_done.add((e, h))
             cols = slice(column, column + P)
             nc.tensor.matmul_mx(
                 out=dx_banks[first, h][:, (e - first) * C : (e - first + 1) * C],
@@ -182,42 +191,40 @@ def tile_moe_bdx_mlp_relu_kernel(
                 start=True,
                 stop=True,
             )
-            if e == first + count - 1:
-                copy = nc.vector.tensor_copy if h == 0 and count == 1 else nc.scalar.copy
+            if all((member, h) in dx_done for member in range(first, first + count)):
+                copy = nc.vector.tensor_copy if count == 1 else nc.scalar.copy
                 copy(out=dx[h][:, first * C : (first + count) * C], in_=dx_banks[first, h][:])
 
+        def rounded_tile():
+            return stream.tile([P, H * PACK], BF16, name="rounded", align_bytes=64, bufs=5)
+
         def whole_pair(first):
-            rounded = []
-            for u, raw in enumerate(load_experts(w1, first, 2, loaded_tile())):
-                rounded.append(stream.tile([P, PACK * K], BF16, name="w1_bf", align_bytes=64, bufs=5))
-                on_scalar = u == 0 and first < BANK_EXPERTS
-                interleave(nc.scalar.copy if on_scalar else nc.vector.tensor_copy, rounded[u][:], raw)
+            rounded = rounded_tile()
+            tile = loaded_tile()
+            for u, raw in enumerate(load_experts(w1, first, 2, tile)):
+                copy = nc.scalar.copy if u else nc.vector.tensor_copy
+                interleave(copy, rounded[:, u * PACK * K : (u + 1) * PACK * K], raw)
             for u in range(2):
-                codes, scales = quantize(rounded[u][:])
+                codes, scales = quantize(rounded[:, u * PACK * K : (u + 1) * PACK * K])
                 for h in range(K // P):
                     second_product(first + u, h, codes, scales, h * P)
+            return tile
 
-        def load_halves(first, count, h, copies, rounded):
+        def load_halves(experts, h, copy, rounded):
+            count = len(experts)
             flat = loaded_tile()[:, 0 : count * PACK * P]
-            rows = w1[first : first + count].rearrange("u (p j) k -> p j u k", j=PACK)
+            chosen = w1[experts[0] : experts[-1] + 1 : max(experts[-1] - experts[0], 1)]
+            rows = chosen.rearrange("u (p j) k -> p j u k", j=PACK)
             nc.sync.dma_start(
                 out=flat.rearrange("p (j u k) -> p j u k", u=count, j=PACK), in_=rows[:, :, :, h * P : (h + 1) * P]
             )
-            raw = flat.rearrange("p (j c) -> p j c", j=PACK)
-            share = count * P // len(copies)
-            for n, copy in enumerate(copies):
-                interleave(copy, rounded[:, n * share * PACK : (n + 1) * share * PACK], raw[:, :, n * share : (n + 1) * share])
+            interleave(copy, rounded, flat.rearrange("p (j c) -> p j c", j=PACK))
             return flat
 
-        def multiply_halves(first, count, h, rounded):
+        def multiply_halves(experts, h, rounded):
             codes, scales = quantize(rounded)
-            for u in range(count):
-                second_product(first + u, h, codes, scales, u * P)
-
-        def first_halves(first, count, copies):
-            rounded = stream.tile([P, PACK * K], BF16, name="w1_bf", align_bytes=64, bufs=5)[:, 0 : count * PACK * P]
-            load_halves(first, count, 0, copies, rounded)
-            multiply_halves(first, count, 0, rounded)
+            for u, e in enumerate(experts):
+                second_product(e, h, codes, scales, u * P)
 
         def pick(h, r, first, count, before, after):
             picked = dx[h][:].indirect(pos_sb[r][:, first // LIST_COLS : (first + count) // LIST_COLS])
@@ -229,7 +236,8 @@ def tile_moe_bdx_mlp_relu_kernel(
                 nc.sync.dma_start(out=out[h * P : (h + 1) * P, first : first + count], in_=after)
 
         def partial(h, r, first, count):
-            return a_sb[h][:, r * T + first : r * T + first + count]
+            start = (3 * h + r) * T + first
+            return a_early[:, start : start + count]
 
         def pick_round(h, r, cuts):
             for first, count in cuts:
@@ -241,19 +249,15 @@ def tile_moe_bdx_mlp_relu_kernel(
         nc.vector.memset(dy_s[:], 0)
         nc.sync.dma_start(out=dy_w[:], in_=dy_words[0].rearrange("p t d -> p (t d)").bitcast(I32))
         nc.sync.dma_start(offs_sb[:], offs)
-        nc.sync.dma_start(out=a_sb[0][:], in_=a_rows[0])
+        load_w2(0, 1)
         for r in range(4):
             nc.sync.dma_start(out=dy_s[r:P:32, :], in_=dy_scales[0].bitcast(I32)[r:16:4, :])
-        load_w2(0, 1)
         nc.sync.dma_start(out=gate_rows[0:E, :], in_=gate[0].rearrange("(e c) -> e c", c=C))
-        nc.sync.dma_start(out=a_sb[1][:], in_=a_rows[1])
+        early_rows = load_a(a_early, 0, EARLY_A)
         gate_turned = psum.tile([P, PACK, C], F32, name="bank")
         nc.tensor.transpose(gate_turned[:, 0, :], gate_rows[:], ident[:])
         nc.scalar.copy(out=gate_cols[:], in_=gate_turned[:, 0, 0:E])
 
-        make_mask(0, 0, S, True)
-        make_mask(1, 0, SCALAR_MASK, True)
-        make_mask(1, SCALAR_MASK, S, False)
 
         round_w2(0, 0)
         for first in range(0, E, GATHERED):
@@ -261,63 +265,75 @@ def tile_moe_bdx_mlp_relu_kernel(
             if first == 0:
                 first_product(0)
         zone = C * PACK // PAIR
-        last_load = len(W2_LOADS) - 1
-        for step in range(1, last_load + 3):
-            tile_first, loaded = W2_LOADS[min(step, last_load)]
-            late = max(step - last_load, 0)
-            if not late:
-                load_w2(tile_first, loaded)
-                for u in range(loaded):
-                    round_w2(tile_first + u, u)
-            else:
-                loaded = 0
-            tile = w2_tiles[tile_first]
-            if step >= 2:
-                first, count = W2_LOADS[step - 2]
-                start = PACK * H - zone + late * 2 * zone
-                da_bf = tile[:, start : start + count * zone].bitcast(BF16)
-                for u in range(count):
-                    mask_da(first + u, da_bf[:, u * C * PACK : (u + 1) * C * PACK])
-            if loaded:
-                first_product(tile_first)
-            if step >= 2:
-                quantize_da(first, count, da_bf)
-            if loaded == 2:
-                first_product(tile_first + 1)
-            if step - 1 <= last_load:
-                first, count = W2_LOADS[step - 1]
-                for u in range(count):
-                    start = 2 * PACK * H - 2 * zone if late else u * (2 * PACK * H - zone)
-                    gate_and_turn(first + u, tile[:, start : start + zone])
+        make_mask(0, SCALAR_MASK, early_rows[:, :, 0 : SCALAR_MASK * C], True)
+        make_mask(SCALAR_MASK, EARLY_A, early_rows[:, :, SCALAR_MASK * C :], False)
 
-        for first in range(0, WHOLE_W1, 2):
-            whole_pair(first)
-        for first in range(WHOLE_W1, E - 4, BANK_EXPERTS):
-            rounded = stream.tile([P, H * PACK], BF16, name="rounded", align_bytes=64, bufs=3)
-            load_halves(first, 2, 0, [nc.scalar.copy], rounded[:, 0 : 2 * PACK * P])
-            load_halves(first + 2, 2, 0, [nc.vector.tensor_copy], rounded[:, 2 * PACK * P :])
-            multiply_halves(first, BANK_EXPERTS, 0, rounded[:])
-        first_halves(E - 4, 2, [nc.scalar.copy, nc.vector.tensor_copy])
-        first_halves(E - 2, 1, [nc.vector.tensor_copy])
-        first_halves(E - 1, 1, [nc.vector.tensor_copy])
+        def mask_load(n, tile, start):
+            first, count = W2_LOADS[n]
+            da_bf = tile[:, start : start + count * zone].bitcast(BF16)
+            for u in range(count):
+                mask_da(first + u, da_bf[:, u * C * PACK : (u + 1) * C * PACK])
+            return first, count, da_bf
+
+        def gate_load(n, tile, starts):
+            first, count = W2_LOADS[n]
+            for u in range(count):
+                gate_and_turn(first + u, tile[:, starts[u] : starts[u] + zone])
+
+        middle = PACK * H
+        last = len(W2_LOADS) - 1
+        for n in range(1, last):
+            first, count = W2_LOADS[n]
+            load_w2(first, count)
+            for u in range(count):
+                round_w2(first + u, u)
+            masked = mask_load(n - 2, w2_tiles[first], middle - zone) if n >= 2 else None
+            first_product(first)
+            if masked:
+                quantize_da(*masked)
+            first_product(first + 1)
+            gate_load(n - 1, w2_tiles[first], (0, 2 * middle - zone))
+        make_mask(EARLY_A, E, load_a(a_late, EARLY_A, E), False)
+        tile = w2_tiles[W2_LOADS[last - 1][0]]
+        gate_load(last - 1, tile, (H, middle + H))
+        quantize_da(*mask_load(last - 2, tile, 2 * H))
+        load_w2(E - 1, 1)
+        tile = w2_tiles[E - 1]
+        round_w2(E - 1, 0)
+        first_product(E - 1)
+        quantize_da(*mask_load(last - 1, tile, middle - zone))
+
+        unit = PACK * P
+        def first_halves(experts, copy):
+            rounded = rounded_tile()[:, 0 : len(experts) * unit]
+            load_halves(experts, 0, copy, rounded)
+            multiply_halves(experts, 0, rounded)
+
+        whole_pair(0)
+        gate_load(last, whole_pair(2), (PACK * K,))
+        first_halves(FIRST_HALVES[0], nc.scalar.copy)
+        quantize_da(*mask_load(last, whole_pair(4), 0))
+        whole_pair(6)
+        first_halves(FIRST_HALVES[2], nc.scalar.copy)
+        for n in (1, 3, 4, 5):
+            first_halves(FIRST_HALVES[n], nc.vector.tensor_copy)
         for r, pos in enumerate((pos1, pos2, pos3)):
             nc.sync.dma_start(pos_sb[r][:], pos)
-        late = mask[:].rearrange("p u s -> p (u s)")
-        spent = {}
-
-        def late_rounded(first, count):
-            return late[:, (first - WHOLE_W1) * PACK * P : (first - WHOLE_W1 + count) * PACK * P]
-
-        for first in range(WHOLE_W1, E, 2):
-            spent[first] = load_halves(first, 2, 1, [nc.scalar.copy], late_rounded(first, 2))
-            if first + 2 == WHOLE_W1 + WIDE:
-                multiply_halves(WHOLE_W1, WIDE, 1, late_rounded(WHOLE_W1, WIDE))
-            elif first >= WHOLE_W1 + WIDE:
-                multiply_halves(first, 2, 1, late_rounded(first, 2))
+        late = mask[:]
+        spent, late_rounded, start = [], [], 0
+        for experts in SECOND_HALVES:
+            late_rounded.append(late[:, start : start + len(experts) * unit])
+            spent.append(load_halves(experts, 1, nc.scalar.copy, late_rounded[-1]))
+            start = start + len(experts) * unit
+        multiply_halves(SECOND_HALVES[0] + SECOND_HALVES[1], 1, late[:, 0 : 4 * unit])
+        for n in range(2, len(SECOND_HALVES)):
+            multiply_halves(SECOND_HALVES[n], 1, late_rounded[n])
+        (front, width), (back, width) = TOKEN_CUTS
         pick_round(0, 0, TOKEN_CUTS)
-        pick_round(0, 1, TOKEN_CUTS)
-        for (first, count), tile in zip(TOKEN_CUTS, (spent[WHOLE_W1 + WIDE - 2], spent[E - 2])):
-            pick(0, 2, first, count, partial(0, 1, first, count), tile[:, 0:count])
+        pick_round(0, 1, TOKEN_CUTS[:1])
+        pick(0, 1, back, width, partial(0, 0, back, width), spent[1][:, 0:width])
+        pick(0, 2, front, width, partial(0, 1, front, width), spent[2][:, 0:width])
+        pick(0, 2, back, width, spent[1][:, 0:width], spent[-1][:, 0:width])
         pick_round(1, 0, TOKEN_CUTS)
         pick_round(1, 1, TOKEN_CUTS)
         pick_round(1, 2, LAST_CUTS)

@@ -35,7 +35,10 @@ SCALAR_W2 = 256
 SCALAR_MASK = 8
 PAIRED_W2 = 16
 WHOLE_W1 = 8
-DX_GROUPS = [(0, 3), (3, 4), (7, 4), (11, 4), (15, 2), (17, 1)]
+DX_GROUPS = [
+    [(0, 3), (3, 4), (7, 3), (10, 4), (14, 2), (16, 2)],
+    [(0, 3), (3, 4), (7, 4), (11, 4), (15, 2), (17, 1)],
+]
 FIRST_HALVES = [(8, 9), (10, 11), (12, 13), (14, 15), (16,), (17,)]
 SECOND_HALVES = [(8, 9), (11, 12), (10, 14), (13, 15), (16,), (17,)]
 TOKEN_CUTS = [(0, T // 2), (T // 2, T // 2)]
@@ -177,7 +180,7 @@ def tile_moe_bdx_mlp_relu_kernel(
                 da_scales[first + u] = scales[:, u * C : (u + 1) * C]
 
         def second_product(e, h, codes, scales, column):
-            first, count = [group for group in DX_GROUPS if group[0] <= e][-1]
+            first, count = [group for group in DX_GROUPS[h] if group[0] <= e][-1]
             if (first, h) not in dx_banks:
                 dx_banks[first, h] = psum.tile([P, count * C], F32, name="bank")
             dx_done.add((e, h))
@@ -192,7 +195,7 @@ def tile_moe_bdx_mlp_relu_kernel(
                 stop=True,
             )
             if all((member, h) in dx_done for member in range(first, first + count)):
-                copy = nc.vector.tensor_copy if count == 1 else nc.scalar.copy
+                copy = nc.vector.tensor_copy if first + count == E else nc.scalar.copy
                 copy(out=dx[h][:, first * C : (first + count) * C], in_=dx_banks[first, h][:])
 
         def rounded_tile():
@@ -245,14 +248,14 @@ def tile_moe_bdx_mlp_relu_kernel(
                 pick(h, r, first, count, before, partial(h, r, first, count))
 
         make_identity(nc, ident[:])
-        nc.gpsimd.memset(gate_rows[:], 0.0)
+        nc.vector.memset(gate_rows[:], 0.0)
         nc.vector.memset(dy_s[:], 0)
         nc.sync.dma_start(out=dy_w[:], in_=dy_words[0].rearrange("p t d -> p (t d)").bitcast(I32))
         nc.sync.dma_start(offs_sb[:], offs)
         load_w2(0, 1)
         for r in range(4):
-            nc.sync.dma_start(out=dy_s[r:P:32, :], in_=dy_scales[0].bitcast(I32)[r:16:4, :])
-        nc.sync.dma_start(out=gate_rows[0:E, :], in_=gate[0].rearrange("(e c) -> e c", c=C))
+            nc.scalar.dma_start(out=dy_s[r:P:32, :], in_=dy_scales[0].bitcast(I32)[r:16:4, :])
+        nc.scalar.dma_start(out=gate_rows[0:E, :], in_=gate[0].rearrange("(e c) -> e c", c=C))
         early_rows = load_a(a_early, 0, EARLY_A)
         gate_turned = psum.tile([P, PACK, C], F32, name="bank")
         nc.tensor.transpose(gate_turned[:, 0, :], gate_rows[:], ident[:])
@@ -317,14 +320,15 @@ def tile_moe_bdx_mlp_relu_kernel(
         first_halves(FIRST_HALVES[2], nc.scalar.copy)
         for n in (1, 3, 4, 5):
             first_halves(FIRST_HALVES[n], nc.vector.tensor_copy)
-        for r, pos in enumerate((pos1, pos2, pos3)):
-            nc.sync.dma_start(pos_sb[r][:], pos)
         late = mask[:]
         spent, late_rounded, start = [], [], 0
         for experts in SECOND_HALVES:
             late_rounded.append(late[:, start : start + len(experts) * unit])
             spent.append(load_halves(experts, 1, nc.scalar.copy, late_rounded[-1]))
             start = start + len(experts) * unit
+            if experts == SECOND_HALVES[0]:
+                for r, pos in enumerate((pos1, pos2, pos3)):
+                    nc.sync.dma_start(pos_sb[r][:], pos)
         multiply_halves(SECOND_HALVES[0] + SECOND_HALVES[1], 1, late[:, 0 : 4 * unit])
         for n in range(2, len(SECOND_HALVES)):
             multiply_halves(SECOND_HALVES[n], 1, late_rounded[n])

@@ -97,7 +97,8 @@ def tile_moe_bdx_mlp_relu_kernel(
 
         def load_a(tile, first, last):
             rows = tile[:].rearrange("p (j s) -> p j s", j=PACK)
-            nc.sync.dma_start(out=rows, in_=a_rows[:, :, first * C : last * C])
+            for j in range(0, PACK, PAIR):
+                nc.sync.dma_start(out=rows[:, j : j + PAIR], in_=a_rows[:, j : j + PAIR, first * C : last * C])
             return rows
 
         def sign_of(out, in_):

@@ -25,23 +25,22 @@ PAIR = 2
 RUN = 4
 LIST_COLS = 16
 BANKS = 8
-BANK_EXPERTS = 4
 LOAD_RING = 6
+CODE_RING = 5
+GATHERED = 4
+ONE_W2 = PACK * H
+STAGED = C * PACK // PAIR
+HALF_W1 = PACK * P
 W2_LOADS = [(0, 1)] + [(first, 2) for first in range(1, E - 1, 2)] + [(E - 1, 1)]
 EARLY_A = 14
-DA_LAG = 3
-GATHERED = 4
-SCALAR_W2 = 256
 SCALAR_MASK = 8
-PAIRED_W2 = 16
-WHOLE_W1 = 8
 DX_GROUPS = [
     [(0, 3), (3, 4), (7, 3), (10, 4), (14, 2), (16, 2)],
     [(0, 3), (3, 4), (7, 4), (11, 4), (15, 2), (17, 1)],
 ]
-FIRST_HALVES = [(8, 9), (10, 11), (12, 13), (14, 15), (16,), (17,)]
 SECOND_HALVES = [(8, 9), (11, 12), (10, 14), (13, 15), (16,), (17,)]
 TOKEN_CUTS = [(0, T // 2), (T // 2, T // 2)]
+SHORT_CUT = T // 4
 LAST_CUTS = [(0, T // 2), (T // 2, 3 * T // 8), (7 * T // 8, T // 8)]
 
 
@@ -69,15 +68,18 @@ def tile_moe_bdx_mlp_relu_kernel(
         mask = keep.tile([P, PACK * S], BF16, name="mask", align_bytes=64)
 
         g_words, g_scales, w2_tiles, w2_raw, w2_bf = {}, {}, {}, {}, {}
-        dx_done = set()
         sums, dh, da_codes, da_scales, dx_banks = {}, {}, {}, {}, {}
+        dx_done = set()
 
         def loaded_tile():
-            return stream.tile([P, 2 * PACK * H], F32, name="loaded", align_bytes=64, bufs=LOAD_RING)
+            return stream.tile([P, 2 * ONE_W2], F32, name="loaded", align_bytes=64, bufs=LOAD_RING)
 
-        def interleave(copy, rounded, raw):
-            copy(
-                out=rounded.rearrange("p (c i j) -> p c j i", i=RUN, j=PACK),
+        def rounded_tile():
+            return stream.tile([P, ONE_W2], BF16, name="rounded", align_bytes=64, bufs=CODE_RING)
+
+        def interleave(convert, result, raw):
+            convert(
+                out=result.rearrange("p (c i j) -> p c j i", i=RUN, j=PACK),
                 in_=raw.rearrange("p j (c i) -> p c j i", i=RUN),
             )
 
@@ -115,8 +117,8 @@ def tile_moe_bdx_mlp_relu_kernel(
 
         def quantize(rounded):
             width = rounded.shape[1] // PACK
-            codes = stream.tile([P, width], U32, name="w_codes", align_bytes=64, bufs=5)
-            scales = stream.tile([P, width], U8, name="w_scales", align_bytes=64, bufs=5)
+            codes = stream.tile([P, width], U32, name="w_codes", align_bytes=64, bufs=CODE_RING)
+            scales = stream.tile([P, width], U8, name="w_scales", align_bytes=64, bufs=CODE_RING)
             nc.vector.quantize_mx(out=codes[:].bitcast(FP8X4), scales=scales[:], in_=rounded)
             return codes, scales
 
@@ -165,10 +167,11 @@ def tile_moe_bdx_mlp_relu_kernel(
                 nc.tensor.transpose(dh[e][:, u, :], gated[:, u, :], ident[:])
 
         def mask_da(e, rounded):
+            own_mask = mask[:, PACK * e * C : PACK * (e + 1) * C]
             nc.vector.tensor_tensor(
                 out=rounded.rearrange("p (s u v) -> p s u v", u=PACK // PAIR, v=PAIR),
                 in0=dh[e][:].bitcast(BF16).rearrange("p u (s v) -> p s u v", v=PAIR),
-                in1=mask[:, PACK * e * C : PACK * (e + 1) * C].rearrange("p (s u v) -> p s u v", u=PACK // PAIR, v=PAIR),
+                in1=own_mask.rearrange("p (s u v) -> p s u v", u=PACK // PAIR, v=PAIR),
                 op=ALU.mult,
             )
 
@@ -179,6 +182,18 @@ def tile_moe_bdx_mlp_relu_kernel(
             for u in range(count):
                 da_codes[first + u] = codes[:, u * C : (u + 1) * C]
                 da_scales[first + u] = scales[:, u * C : (u + 1) * C]
+
+        def gate_load(n, tile, starts):
+            first, count = W2_LOADS[n]
+            for u in range(count):
+                gate_and_turn(first + u, tile[:, starts[u] : starts[u] + STAGED])
+
+        def mask_load(n, tile, start):
+            first, count = W2_LOADS[n]
+            da_bf = tile[:, start : start + count * STAGED].bitcast(BF16)
+            for u in range(count):
+                mask_da(first + u, da_bf[:, u * C * PACK : (u + 1) * C * PACK])
+            return first, count, da_bf
 
         def second_product(e, h, codes, scales, column):
             first, count = [group for group in DX_GROUPS[h] if group[0] <= e][-1]
@@ -196,11 +211,8 @@ def tile_moe_bdx_mlp_relu_kernel(
                 stop=True,
             )
             if all((member, h) in dx_done for member in range(first, first + count)):
-                copy = nc.vector.tensor_copy if first + count == E else nc.scalar.copy
+                copy = nc.vector.tensor_copy if h == 0 and first + count == E else nc.scalar.copy
                 copy(out=dx[h][:, first * C : (first + count) * C], in_=dx_banks[first, h][:])
-
-        def rounded_tile():
-            return stream.tile([P, H * PACK], BF16, name="rounded", align_bytes=64, bufs=5)
 
         def whole_pair(first):
             rounded = rounded_tile()
@@ -216,19 +228,25 @@ def tile_moe_bdx_mlp_relu_kernel(
 
         def load_halves(experts, h, copy, rounded):
             count = len(experts)
-            flat = loaded_tile()[:, 0 : count * PACK * P]
+            tile = loaded_tile()
+            flat = tile[:, 0 : count * HALF_W1]
             chosen = w1[experts[0] : experts[-1] + 1 : max(experts[-1] - experts[0], 1)]
             rows = chosen.rearrange("u (p j) k -> p j u k", j=PACK)
             nc.sync.dma_start(
                 out=flat.rearrange("p (j u k) -> p j u k", u=count, j=PACK), in_=rows[:, :, :, h * P : (h + 1) * P]
             )
             interleave(copy, rounded, flat.rearrange("p (j c) -> p j c", j=PACK))
-            return flat
+            return tile
 
         def multiply_halves(experts, h, rounded):
             codes, scales = quantize(rounded)
             for u, e in enumerate(experts):
                 second_product(e, h, codes, scales, u * P)
+
+        def first_halves(experts, copy):
+            rounded = rounded_tile()[:, 0 : len(experts) * HALF_W1]
+            load_halves(experts, 0, copy, rounded)
+            multiply_halves(experts, 0, rounded)
 
         def pick(h, r, first, count, before, after):
             picked = dx[h][:].indirect(pos_sb[r][:, first // LIST_COLS : (first + count) // LIST_COLS])
@@ -262,83 +280,64 @@ def tile_moe_bdx_mlp_relu_kernel(
         nc.tensor.transpose(gate_turned[:, 0, :], gate_rows[:], ident[:])
         nc.scalar.copy(out=gate_cols[:], in_=gate_turned[:, 0, 0:E])
 
-
         round_w2(0, 0)
         for first in range(0, E, GATHERED):
             gather(first)
             if first == 0:
                 first_product(0)
-        zone = C * PACK // PAIR
         make_mask(0, SCALAR_MASK, early_rows[:, :, 0 : SCALAR_MASK * C], True)
         make_mask(SCALAR_MASK, EARLY_A, early_rows[:, :, SCALAR_MASK * C :], False)
 
-        def mask_load(n, tile, start):
-            first, count = W2_LOADS[n]
-            da_bf = tile[:, start : start + count * zone].bitcast(BF16)
-            for u in range(count):
-                mask_da(first + u, da_bf[:, u * C * PACK : (u + 1) * C * PACK])
-            return first, count, da_bf
-
-        def gate_load(n, tile, starts):
-            first, count = W2_LOADS[n]
-            for u in range(count):
-                gate_and_turn(first + u, tile[:, starts[u] : starts[u] + zone])
-
-        middle = PACK * H
-        last = len(W2_LOADS) - 1
-        for n in range(1, last):
+        last_load = len(W2_LOADS) - 1
+        for n in range(1, last_load):
             first, count = W2_LOADS[n]
             load_w2(first, count)
             for u in range(count):
                 round_w2(first + u, u)
-            masked = mask_load(n - 2, w2_tiles[first], middle - zone) if n >= 2 else None
+            masked = mask_load(n - 2, w2_tiles[first], ONE_W2 - STAGED) if n >= 2 else None
             first_product(first)
             if masked:
                 quantize_da(*masked)
             first_product(first + 1)
-            gate_load(n - 1, w2_tiles[first], (0, 2 * middle - zone))
+            gate_load(n - 1, w2_tiles[first], (0, 2 * ONE_W2 - STAGED))
         make_mask(EARLY_A, E, load_a(a_late, EARLY_A, E), False)
-        tile = w2_tiles[W2_LOADS[last - 1][0]]
-        gate_load(last - 1, tile, (H, middle + H))
-        quantize_da(*mask_load(last - 2, tile, 2 * H))
+        last_pair = w2_tiles[W2_LOADS[last_load - 1][0]]
+        gate_load(last_load - 1, last_pair, (H, ONE_W2 + H))
+        quantize_da(*mask_load(last_load - 2, last_pair, 2 * H))
         load_w2(E - 1, 1)
-        tile = w2_tiles[E - 1]
         round_w2(E - 1, 0)
         first_product(E - 1)
-        quantize_da(*mask_load(last - 1, tile, middle - zone))
-
-        unit = PACK * P
-        def first_halves(experts, copy):
-            rounded = rounded_tile()[:, 0 : len(experts) * unit]
-            load_halves(experts, 0, copy, rounded)
-            multiply_halves(experts, 0, rounded)
+        quantize_da(*mask_load(last_load - 1, w2_tiles[E - 1], ONE_W2 - STAGED))
 
         whole_pair(0)
-        gate_load(last, whole_pair(2), (PACK * K,))
-        first_halves(FIRST_HALVES[0], nc.scalar.copy)
-        quantize_da(*mask_load(last, whole_pair(4), 0))
+        gate_load(last_load, whole_pair(2), (PACK * K,))
+        first_halves((8, 9), nc.scalar.copy)
+        quantize_da(*mask_load(last_load, whole_pair(4), 0))
         whole_pair(6)
-        first_halves(FIRST_HALVES[2], nc.scalar.copy)
-        for n in (1, 3, 4, 5):
-            first_halves(FIRST_HALVES[n], nc.vector.tensor_copy)
-        late = mask[:]
-        spent, late_rounded, start = [], [], 0
+        first_halves((11, 12), nc.scalar.copy)
+        first_halves((10, 15), nc.vector.tensor_copy)
+        first_halves((13, 14), nc.vector.tensor_copy)
+        first_halves((16,), nc.scalar.copy)
+        first_halves((17,), nc.vector.tensor_copy)
+
+        spent, late_bf, start = [], [], 0
         for experts in SECOND_HALVES:
-            late_rounded.append(late[:, start : start + len(experts) * unit])
-            spent.append(load_halves(experts, 1, nc.scalar.copy, late_rounded[-1]))
-            start = start + len(experts) * unit
+            late_bf.append(mask[:, start : start + len(experts) * HALF_W1])
+            spent.append(load_halves(experts, 1, nc.scalar.copy, late_bf[-1]))
+            start = start + len(experts) * HALF_W1
             if experts == SECOND_HALVES[0]:
                 for r, pos in enumerate((pos1, pos2, pos3)):
                     nc.sync.dma_start(pos_sb[r][:], pos)
-        multiply_halves(SECOND_HALVES[0] + SECOND_HALVES[1], 1, late[:, 0 : 4 * unit])
+        first_two = SECOND_HALVES[0] + SECOND_HALVES[1]
+        multiply_halves(first_two, 1, mask[:, 0 : len(first_two) * HALF_W1])
         for n in range(2, len(SECOND_HALVES)):
-            multiply_halves(SECOND_HALVES[n], 1, late_rounded[n])
-        (front, width), (back, width) = TOKEN_CUTS
+            multiply_halves(SECOND_HALVES[n], 1, late_bf[n])
+        long_cut = T - SHORT_CUT
         pick_round(0, 0, TOKEN_CUTS)
-        pick_round(0, 1, TOKEN_CUTS[:1])
-        pick(0, 1, back, width, partial(0, 0, back, width), spent[1][:, 0:width])
-        pick(0, 2, front, width, partial(0, 1, front, width), spent[2][:, 0:width])
-        pick(0, 2, back, width, spent[1][:, 0:width], spent[-1][:, 0:width])
+        pick_round(0, 1, [(0, SHORT_CUT)])
+        pick(0, 1, SHORT_CUT, long_cut, partial(0, 0, SHORT_CUT, long_cut), spent[1][:, 0:long_cut])
+        pick(0, 2, 0, SHORT_CUT, partial(0, 1, 0, SHORT_CUT), spent[2][:, 0:SHORT_CUT])
+        pick(0, 2, SHORT_CUT, long_cut, spent[1][:, 0:long_cut], spent[-1][:, 0:long_cut])
         pick_round(1, 0, TOKEN_CUTS)
         pick_round(1, 1, TOKEN_CUTS)
         pick_round(1, 2, LAST_CUTS)

@@ -41,7 +41,6 @@ DX_GROUPS = [
 SECOND_HALVES = [(8, 9), (11, 12), (10, 14), (13, 15), (16,), (17,)]
 TOKEN_CUTS = [(0, T // 2), (T // 2, T // 2)]
 SHORT_CUT = T // 4
-LAST_CUTS = [(0, T // 2), (T // 2, 3 * T // 8), (7 * T // 8, T // 8)]
 
 
 def tile_moe_bdx_mlp_relu_kernel(
@@ -338,6 +337,36 @@ def tile_moe_bdx_mlp_relu_kernel(
         pick(0, 1, SHORT_CUT, long_cut, partial(0, 0, SHORT_CUT, long_cut), spent[1][:, 0:long_cut])
         pick(0, 2, 0, SHORT_CUT, partial(0, 1, 0, SHORT_CUT), spent[2][:, 0:SHORT_CUT])
         pick(0, 2, SHORT_CUT, long_cut, spent[1][:, 0:long_cut], spent[-1][:, 0:long_cut])
-        pick_round(1, 0, TOKEN_CUTS)
-        pick_round(1, 1, TOKEN_CUTS)
-        pick_round(1, 2, LAST_CUTS)
+
+        def picked(r, cut):
+            return dx[1][:].indirect(pos_sb[r][:, cut.start // LIST_COLS : cut.stop // LIST_COLS])
+
+        def scalar_pick(r, cut, result):
+            nc.scalar.activation(out=result[:, cut], in_=picked(r, cut), func=COPY)
+
+        def adding_pick(r, cut, before, result):
+            nc.vector.tensor_tensor(result[:, cut], picked(r, cut), before[:, cut], ALU.add)
+
+        def add(cut, left, right):
+            nc.vector.tensor_tensor(total[:, cut], left[:, cut], right[:, cut], ALU.add)
+
+        def store(cut):
+            nc.sync.dma_start(out=out[P : 2 * P, cut], in_=total[:, cut])
+
+        one, two, three, total = [partial(1, r, 0, T) for r in range(4)]
+        own, wide, late, rest, tail = slice(0, 224), slice(224, 544), slice(544, T), slice(544, 672), slice(672, T)
+        nc.vector.tensor_copy(three[:, own], picked(2, own))
+        scalar_pick(0, wide, one)
+        adding_pick(1, own, three, two)
+        scalar_pick(0, own, one)
+        adding_pick(2, wide, one, three)
+        scalar_pick(1, wide, two)
+        add(own, two, one)
+        scalar_pick(0, late, one)
+        add(wide, three, two)
+        store(slice(0, late.start))
+        adding_pick(2, late, one, three)
+        for cut in (rest, tail):
+            scalar_pick(1, cut, two)
+            add(cut, three, two)
+            store(cut)

@@ -40,7 +40,6 @@ DX_GROUPS = [
 ]
 SECOND_HALVES = [(8, 9), (11, 12), (10, 14), (13, 15), (16,), (17,)]
 TOKEN_CUTS = [(0, T // 2), (T // 2, T // 2)]
-SHORT_CUT = T // 4
 
 
 def tile_moe_bdx_mlp_relu_kernel(
@@ -331,12 +330,12 @@ def tile_moe_bdx_mlp_relu_kernel(
         multiply_halves(first_two, 1, mask[:, 0 : len(first_two) * HALF_W1])
         for n in range(2, len(SECOND_HALVES)):
             multiply_halves(SECOND_HALVES[n], 1, late_bf[n])
-        long_cut = T - SHORT_CUT
+        half = T // 2
         pick_round(0, 0, TOKEN_CUTS)
-        pick_round(0, 1, [(0, SHORT_CUT)])
-        pick(0, 1, SHORT_CUT, long_cut, partial(0, 0, SHORT_CUT, long_cut), spent[1][:, 0:long_cut])
-        pick(0, 2, 0, SHORT_CUT, partial(0, 1, 0, SHORT_CUT), spent[2][:, 0:SHORT_CUT])
-        pick(0, 2, SHORT_CUT, long_cut, spent[1][:, 0:long_cut], spent[-1][:, 0:long_cut])
+        pick(0, 1, 0, half, partial(0, 0, 0, half), spent[2][:, 0:half])
+        pick(0, 1, half, half, partial(0, 0, half, half), spent[-1][:, 0:half])
+        pick(0, 2, 0, half, spent[2][:, 0:half], spent[-1][:, half:T])
+        pick(0, 2, half, half, spent[-1][:, 0:half], partial(0, 2, half, half))
 
         def picked(r, cut):
             return dx[1][:].indirect(pos_sb[r][:, cut.start // LIST_COLS : cut.stop // LIST_COLS])
@@ -354,19 +353,16 @@ def tile_moe_bdx_mlp_relu_kernel(
             nc.sync.dma_start(out=out[P : 2 * P, cut], in_=total[:, cut])
 
         one, two, three, total = [partial(1, r, 0, T) for r in range(4)]
-        own, wide, late, rest, tail = slice(0, 224), slice(224, 544), slice(544, T), slice(544, 672), slice(672, T)
-        nc.vector.tensor_copy(three[:, own], picked(2, own))
-        scalar_pick(0, wide, one)
-        adding_pick(1, own, three, two)
-        scalar_pick(0, own, one)
-        adding_pick(2, wide, one, three)
-        scalar_pick(1, wide, two)
-        add(own, two, one)
-        scalar_pick(0, late, one)
-        add(wide, three, two)
-        store(slice(0, late.start))
-        adding_pick(2, late, one, three)
-        for cut in (rest, tail):
+        wide, middle, small = slice(0, half), slice(half, 5 * T // 6), slice(5 * T // 6, T)
+        for cut in (wide, middle, small):
+            scalar_pick(0, cut, one)
+        for cut in (middle, small):
             scalar_pick(1, cut, two)
+        adding_pick(2, wide, one, three)
+        adding_pick(2, middle, one, three)
+        adding_pick(1, wide, three, total)
+        store(wide)
+        adding_pick(2, small, one, three)
+        for cut in (middle, small):
             add(cut, three, two)
             store(cut)

@@ -35,10 +35,11 @@ W2_LOADS = [(0, 1)] + [(first, 2) for first in range(1, E - 1, 2)] + [(E - 1, 1)
 EARLY_A = 14
 SCALAR_MASK = 8
 DX_GROUPS = [
-    [(0, 3), (3, 4), (7, 3), (10, 4), (14, 2), (16, 2)],
-    [(0, 3), (3, 4), (7, 4), (11, 4), (15, 2), (17, 1)],
+    [(0, 3), (3, 4), (7, 4), (11, 4), (15, 3)],
+    [(0, 3), (3, 3), (6, 4), (10, 4), (14, 4)],
 ]
-SECOND_HALVES = [(8, 9), (11, 12), (10, 14), (13, 15), (16,), (17,)]
+SECOND_HALVES = [(6, 7), (10, 11), (8, 12), (9, 13), (14, 15), (16,), (17,)]
+LAST_CUTS = [(0, 352), (352, 256), (608, 160)]
 TOKEN_CUTS = [(0, T // 2), (T // 2, T // 2)]
 
 
@@ -309,33 +310,35 @@ def tile_moe_bdx_mlp_relu_kernel(
 
         whole_pair(0)
         gate_load(last_load, whole_pair(2), (PACK * K,))
-        first_halves((8, 9), nc.scalar.copy)
+        first_halves((6, 7), nc.scalar.copy)
         quantize_da(*mask_load(last_load, whole_pair(4), 0))
-        whole_pair(6)
-        first_halves((11, 12), nc.scalar.copy)
-        first_halves((10, 15), nc.vector.tensor_copy)
-        first_halves((13, 14), nc.vector.tensor_copy)
+        for first in range(8, 16, 4):
+            first_halves((first, first + 1), nc.scalar.copy)
+            first_halves((first + 2, first + 3), nc.vector.tensor_copy)
         first_halves((16,), nc.scalar.copy)
         first_halves((17,), nc.vector.tensor_copy)
 
         spent, late_bf, start = [], [], 0
         for experts in SECOND_HALVES:
             late_bf.append(mask[:, start : start + len(experts) * HALF_W1])
-            spent.append(load_halves(experts, 1, nc.scalar.copy, late_bf[-1]))
+            copy = nc.scalar.copy if len(experts) > 1 else nc.vector.tensor_copy
+            spent.append(load_halves(experts, 1, copy, late_bf[-1]))
             start = start + len(experts) * HALF_W1
             if experts == SECOND_HALVES[0]:
                 for r, pos in enumerate((pos1, pos2, pos3)):
                     nc.sync.dma_start(pos_sb[r][:], pos)
-        first_two = SECOND_HALVES[0] + SECOND_HALVES[1]
-        multiply_halves(first_two, 1, mask[:, 0 : len(first_two) * HALF_W1])
-        for n in range(2, len(SECOND_HALVES)):
-            multiply_halves(SECOND_HALVES[n], 1, late_bf[n])
+        for n in range(0, 4, 2):
+            both = SECOND_HALVES[n] + SECOND_HALVES[n + 1]
+            multiply_halves(both, 1, mask[:, 2 * n * HALF_W1 : 2 * (n + 2) * HALF_W1])
+        multiply_halves(SECOND_HALVES[4], 1, late_bf[4])
+        multiply_halves((E - 2, E - 1), 1, mask[:, start - 2 * HALF_W1 : start])
         half = T // 2
         pick_round(0, 0, TOKEN_CUTS)
-        pick(0, 1, 0, half, partial(0, 0, 0, half), spent[2][:, 0:half])
-        pick(0, 1, half, half, partial(0, 0, half, half), spent[-1][:, 0:half])
-        pick(0, 2, 0, half, spent[2][:, 0:half], spent[-1][:, half:T])
-        pick(0, 2, half, half, spent[-1][:, 0:half], partial(0, 2, half, half))
+        pick(0, 1, 0, half, partial(0, 0, 0, half), spent[1][:, 0:half])
+        last_bf = mask[:, start - 2 * HALF_W1 : start].bitcast(F32)[:, 0:half]
+        pick(0, 1, half, half, partial(0, 0, half, half), last_bf)
+        pick(0, 2, 0, half, spent[1][:, 0:half], spent[-1][:, 0:half])
+        pick(0, 2, half, half, last_bf, spent[-1][:, half:T])
 
         def picked(r, cut):
             return dx[1][:].indirect(pos_sb[r][:, cut.start // LIST_COLS : cut.stop // LIST_COLS])
@@ -353,16 +356,12 @@ def tile_moe_bdx_mlp_relu_kernel(
             nc.sync.dma_start(out=out[P : 2 * P, cut], in_=total[:, cut])
 
         one, two, three, total = [partial(1, r, 0, T) for r in range(4)]
-        wide, middle, small = slice(0, half), slice(half, 5 * T // 6), slice(5 * T // 6, T)
-        for cut in (wide, middle, small):
-            scalar_pick(0, cut, one)
-        for cut in (middle, small):
-            scalar_pick(1, cut, two)
-        adding_pick(2, wide, one, three)
-        adding_pick(2, middle, one, three)
-        adding_pick(1, wide, three, total)
-        store(wide)
-        adding_pick(2, small, one, three)
-        for cut in (middle, small):
-            add(cut, three, two)
-            store(cut)
+        cuts = [slice(first, first + count) for first, count in LAST_CUTS]
+        for n in range(len(cuts) + 1):
+            if n < len(cuts):
+                scalar_pick(0, cuts[n], one)
+                adding_pick(2, cuts[n], one, three)
+            if n:
+                scalar_pick(1, cuts[n - 1], two)
+                add(cuts[n - 1], three, two)
+                store(cuts[n - 1])

@@ -39,8 +39,8 @@ DX_GROUPS = [
     [(0, 3), (3, 3), (6, 4), (10, 4), (14, 4)],
 ]
 SECOND_HALVES = [(6, 7), (10, 11), (8, 12), (9, 13), (14, 15), (16,), (17,)]
-LAST_CUTS = [(0, 352), (352, 256), (608, 160)]
-TOKEN_CUTS = [(0, T // 2), (T // 2, T // 2)]
+HALF_T = T // 2
+LAST_CUTS = [(0, 384), (384, 160), (544, 224)]
 
 
 def tile_moe_bdx_mlp_relu_kernel(
@@ -247,23 +247,20 @@ def tile_moe_bdx_mlp_relu_kernel(
             load_halves(experts, 0, copy, rounded)
             multiply_halves(experts, 0, rounded)
 
-        def pick(h, r, first, count, before, after):
-            picked = dx[h][:].indirect(pos_sb[r][:, first // LIST_COLS : (first + count) // LIST_COLS])
-            if r == 0:
-                nc.vector.tensor_copy(after, picked)
-            else:
-                nc.vector.tensor_tensor(after, picked, before, ALU.add)
-            if r == 2:
-                nc.sync.dma_start(out=out[h * P : (h + 1) * P, first : first + count], in_=after)
+        def picked(h, r, cut):
+            return dx[h][:].indirect(pos_sb[r][:, cut.start // LIST_COLS : cut.stop // LIST_COLS])
 
-        def partial(h, r, first, count):
-            start = (3 * h + r) * T + first
-            return a_early[:, start : start + count]
+        def scalar_pick(h, r, cut, result):
+            nc.scalar.activation(out=result, in_=picked(h, r, cut), func=COPY)
 
-        def pick_round(h, r, cuts):
-            for first, count in cuts:
-                before = partial(h, r - 1, first, count) if r else None
-                pick(h, r, first, count, before, partial(h, r, first, count))
+        def adding_pick(h, r, cut, before, result):
+            nc.vector.tensor_tensor(result, picked(h, r, cut), before, ALU.add)
+
+        def store(h, cut, result):
+            nc.sync.dma_start(out=out[h * P : (h + 1) * P, cut], in_=result)
+
+        def token_row(n):
+            return a_early[:, n * T : (n + 1) * T]
 
         make_identity(nc, ident[:])
         nc.vector.memset(gate_rows[:], 0.0)
@@ -312,56 +309,44 @@ def tile_moe_bdx_mlp_relu_kernel(
         gate_load(last_load, whole_pair(2), (PACK * K,))
         first_halves((6, 7), nc.scalar.copy)
         quantize_da(*mask_load(last_load, whole_pair(4), 0))
-        for first in range(8, 16, 4):
+        for first in range(8, E - 2, 4):
             first_halves((first, first + 1), nc.scalar.copy)
             first_halves((first + 2, first + 3), nc.vector.tensor_copy)
-        first_halves((16,), nc.scalar.copy)
-        first_halves((17,), nc.vector.tensor_copy)
+        first_halves((E - 2,), nc.scalar.copy)
+        first_halves((E - 1,), nc.vector.tensor_copy)
 
-        spent, late_bf, start = [], [], 0
+        spent, start = [], 0
         for experts in SECOND_HALVES:
-            late_bf.append(mask[:, start : start + len(experts) * HALF_W1])
             copy = nc.scalar.copy if len(experts) > 1 else nc.vector.tensor_copy
-            spent.append(load_halves(experts, 1, copy, late_bf[-1]))
+            spent.append(load_halves(experts, 1, copy, mask[:, start : start + len(experts) * HALF_W1]))
             start = start + len(experts) * HALF_W1
             if experts == SECOND_HALVES[0]:
                 for r, pos in enumerate((pos1, pos2, pos3)):
                     nc.sync.dma_start(pos_sb[r][:], pos)
-        for n in range(0, 4, 2):
-            both = SECOND_HALVES[n] + SECOND_HALVES[n + 1]
-            multiply_halves(both, 1, mask[:, 2 * n * HALF_W1 : 2 * (n + 2) * HALF_W1])
-        multiply_halves(SECOND_HALVES[4], 1, late_bf[4])
-        multiply_halves((E - 2, E - 1), 1, mask[:, start - 2 * HALF_W1 : start])
-        half = T // 2
-        pick_round(0, 0, TOKEN_CUTS)
-        pick(0, 1, 0, half, partial(0, 0, 0, half), spent[1][:, 0:half])
-        last_bf = mask[:, start - 2 * HALF_W1 : start].bitcast(F32)[:, 0:half]
-        pick(0, 1, half, half, partial(0, 0, half, half), last_bf)
-        pick(0, 2, 0, half, spent[1][:, 0:half], spent[-1][:, 0:half])
-        pick(0, 2, half, half, last_bf, spent[-1][:, half:T])
+        late = [e for experts in SECOND_HALVES for e in experts]
+        for begin, end in ((0, 4), (4, 8), (8, 10), (10, 12)):
+            last_bf = mask[:, begin * HALF_W1 : end * HALF_W1]
+            multiply_halves(late[begin:end], 1, last_bf)
 
-        def picked(r, cut):
-            return dx[1][:].indirect(pos_sb[r][:, cut.start // LIST_COLS : cut.stop // LIST_COLS])
+        low, high = slice(0, HALF_T), slice(HALF_T, T)
+        for cut in (low, high):
+            nc.vector.tensor_copy(token_row(0)[:, cut], picked(0, 0, cut))
+        two_low, two_high = spent[1][:, 0:HALF_T], last_bf.bitcast(F32)[:, 0:HALF_T]
+        adding_pick(0, 1, low, token_row(0)[:, low], two_low)
+        adding_pick(0, 1, high, token_row(0)[:, high], two_high)
+        for cut, two_results in ((low, two_low), (high, two_high)):
+            adding_pick(0, 2, cut, two_results, spent[-1][:, cut])
+            store(0, cut, spent[-1][:, cut])
 
-        def scalar_pick(r, cut, result):
-            nc.scalar.activation(out=result[:, cut], in_=picked(r, cut), func=COPY)
-
-        def adding_pick(r, cut, before, result):
-            nc.vector.tensor_tensor(result[:, cut], picked(r, cut), before[:, cut], ALU.add)
-
-        def add(cut, left, right):
-            nc.vector.tensor_tensor(total[:, cut], left[:, cut], right[:, cut], ALU.add)
-
-        def store(cut):
-            nc.sync.dma_start(out=out[P : 2 * P, cut], in_=total[:, cut])
-
-        one, two, three, total = [partial(1, r, 0, T) for r in range(4)]
-        cuts = [slice(first, first + count) for first, count in LAST_CUTS]
-        for n in range(len(cuts) + 1):
-            if n < len(cuts):
-                scalar_pick(0, cuts[n], one)
-                adding_pick(2, cuts[n], one, three)
-            if n:
-                scalar_pick(1, cuts[n - 1], two)
-                add(cuts[n - 1], three, two)
-                store(cuts[n - 1])
+        one, two, three, total = [token_row(n) for n in range(3, 7)]
+        wide, small, late_cut = [slice(first, first + count) for first, count in LAST_CUTS]
+        for cut in (wide, small, late_cut):
+            scalar_pick(1, 0, cut, one[:, cut])
+            adding_pick(1, 2, cut, one[:, cut], three[:, cut])
+        for cut in (wide, small, late_cut):
+            if cut == small:
+                adding_pick(1, 1, cut, three[:, cut], total[:, cut])
+            else:
+                scalar_pick(1, 1, cut, two[:, cut])
+                nc.vector.tensor_tensor(total[:, cut], three[:, cut], two[:, cut], ALU.add)
+            store(1, cut, total[:, cut])

from contextlib import ExitStack

import concourse.mybir as mybir
from concourse.masks import make_identity

K, T, E, C, H, N = 256, 768, 18, 128, 512, 512
S = E * C
FLOPS = 2 * S * (N * H + H * K)
BYTES = 4 * (E * N * H + E * H * K + H * S + S + K * T) + N * T + 16 * T + 2 * 128 * (S + 3 * T) // 16

F32 = mybir.dt.float32
BF16 = mybir.dt.bfloat16
I32 = mybir.dt.int32
U32 = mybir.dt.uint32
U16 = mybir.dt.uint16
U8 = mybir.dt.uint8
FP8X4 = mybir.dt.float8_e4m3fn_x4
ALU = mybir.AluOpType
COPY = mybir.ActivationFunctionType.Copy
SIGN = mybir.ActivationFunctionType.Sign

P = 128
PACK = 4
PAIR = 2
RUN = 4
LIST_COLS = 16
BANKS = 8
LOAD_RING = 6
CODE_RING = 5
GATHERED = 4
ONE_W2 = PACK * H
STAGED = C * PACK // PAIR
HALF_W1 = PACK * P
W2_LOADS = [(0, 1)] + [(first, 2) for first in range(1, E - 1, 2)] + [(E - 1, 1)]
EARLY_A = 14
SCALAR_MASK = 8
DX_GROUPS = [
    [(0, 3), (3, 4), (7, 4), (11, 4), (15, 3)],
    [(0, 3), (3, 3), (6, 4), (10, 4), (14, 4)],
]
SECOND_HALVES = [(6, 7), (10, 11), (8, 12), (9, 13), (14, 15), (16,), (17,)]
HALF_T = T // 2
LAST_CUTS = [(0, 384), (384, 160), (544, 224)]


def tile_moe_bdx_mlp_relu_kernel(
    tc, dy_words, dy_scales, a, w2, w1, gate, offs, pos1, pos2, pos3, out
):
    nc = tc.nc
    with ExitStack() as ctx:
        lists = ctx.enter_context(tc.tile_pool(name="lists", bufs=1))
        keep = ctx.enter_context(tc.tile_pool(name="keep", bufs=1))
        stream = ctx.enter_context(tc.tile_pool(name="stream", bufs=3))
        psum = ctx.enter_context(tc.psum_pool(name="psum", bufs=BANKS))

        offs_sb = lists.tile([P, S // LIST_COLS], U16, name="offs_sb")
        pos_sb = [lists.tile([P, T // LIST_COLS], U16, name="pos_sb%d" % r) for r in range(3)]
        dy_w = keep.tile([P, T], I32, name="dy_w")
        dy_s = keep.tile([P, T // 4], I32, name="dy_s")
        ident = keep.tile([P, P], F32, name="ident")
        gate_rows = keep.tile([P, C], F32, name="gate_rows")
        gate_cols = keep.tile([P, E], F32, name="gate_cols")
        dx = [keep.tile([P, S], F32, name="dx%d" % h) for h in range(K // P)]
        a_early = keep.tile([P, PACK * EARLY_A * C], F32, name="a_early")
        a_late = keep.tile([P, PACK * (E - EARLY_A) * C], F32, name="a_late")
        a_rows = a.rearrange("(p j) s -> p j s", j=PACK)
        mask = keep.tile([P, PACK * S], BF16, name="mask", align_bytes=64)

        g_words, g_scales, w2_tiles, w2_raw, w2_bf = {}, {}, {}, {}, {}
        sums, dh, da_codes, da_scales, dx_banks = {}, {}, {}, {}, {}
        dx_done = set()

        def loaded_tile():
            return stream.tile([P, 2 * ONE_W2], F32, name="loaded", align_bytes=64, bufs=LOAD_RING)

        def rounded_tile():
            return stream.tile([P, ONE_W2], BF16, name="rounded", align_bytes=64, bufs=CODE_RING)

        def interleave(convert, result, raw):
            convert(
                out=result.rearrange("p (c i j) -> p c j i", i=RUN, j=PACK),
                in_=raw.rearrange("p j (c i) -> p c j i", i=RUN),
            )

        def load_experts(weights, first, count, tile):
            width = PACK * weights.shape[2]
            raw = tile[:, 0 : count * width]
            nc.sync.dma_start(
                out=raw.rearrange("p (u r) -> p u r", u=count),
                in_=weights[first : first + count].rearrange("u (p j) c -> p u (j c)", j=PACK),
            )
            return [raw[:, u * width : (u + 1) * width].rearrange("p (j c) -> p j c", j=PACK) for u in range(count)]

        def load_w2(first, count):
            w2_tiles[first] = loaded_tile()
            for u, raw in enumerate(load_experts(w2, first, count, w2_tiles[first])):
                w2_raw[first + u] = raw

        def load_a(tile, first, last):
            rows = tile[:].rearrange("p (j s) -> p j s", j=PACK)
            for j in range(0, PACK, PAIR):
                nc.sync.dma_start(out=rows[:, j : j + PAIR], in_=a_rows[:, j : j + PAIR, first * C : last * C])
            return rows

        def sign_of(out, in_):
            nc.scalar.activation(out=out, in_=in_, func=SIGN)

        def positive(out, in_):
            nc.vector.tensor_single_scalar(out, in_, 0.0, ALU.is_gt)

        def make_mask(first, last, rows, on_scalar):
            part = mask[:, PACK * first * C : PACK * last * C]
            interleave(sign_of if on_scalar else positive, part, rows)
            if on_scalar:
                nc.vector.tensor_scalar_max(part, part, 0.0)

        def quantize(rounded):
            width = rounded.shape[1] // PACK
            codes = stream.tile([P, width], U32, name="w_codes", align_bytes=64, bufs=CODE_RING)
            scales = stream.tile([P, width], U8, name="w_scales", align_bytes=64, bufs=CODE_RING)
            nc.vector.quantize_mx(out=codes[:].bitcast(FP8X4), scales=scales[:], in_=rounded)
            return codes, scales

        def gather(first):
            count = min(GATHERED, E - first)
            cols = offs_sb[:, first * C // LIST_COLS : (first + count) * C // LIST_COLS]
            words = keep.tile([P, count * C], U32, name="g_words%d" % first, align_bytes=64)
            scales = keep.tile([P, count * C], U8, name="g_scales%d" % first, align_bytes=64)
            nc.vector.tensor_copy(words[:], dy_w[:].bitcast(U32).indirect(cols))
            nc.vector.tensor_copy(scales[:], dy_s[:].bitcast(U8).indirect(cols))
            for u in range(count):
                g_words[first + u] = words[:, u * C : (u + 1) * C]
                g_scales[first + u] = scales[:, u * C : (u + 1) * C]

        def round_w2(e, u):
            w2_bf[e] = rounded_tile()
            rest = nc.scalar.copy if e == 0 else nc.vector.tensor_copy
            copies = (nc.scalar.copy, rest) if u == 0 else (rest, nc.scalar.copy)
            for n, copy in enumerate(copies):
                first, last = n * H // 2, (n + 1) * H // 2
                interleave(copy, w2_bf[e][:, first * PACK : last * PACK], w2_raw[e][:, :, first:last])

        def first_product(e):
            codes, scales = quantize(w2_bf[e][:])
            sums[e] = psum.tile([P, H], F32, name="bank")
            nc.tensor.matmul_mx(
                out=sums[e][:],
                lhsT=g_words[e].bitcast(FP8X4),
                lhsT_scale=g_scales[e],
                rhs=codes[:].bitcast(FP8X4),
                rhs_scale=scales[:],
                start=True,
                stop=True,
            )

        def gate_and_turn(e, words):
            gated = words.rearrange("p (u m) -> p u m", m=P)
            nc.scalar.activation(
                out=gated.bitcast(BF16).rearrange("p u (m v) -> p u m v", v=PAIR),
                in_=sums[e][:].rearrange("p (m u v) -> p u m v", u=PACK // PAIR, v=PAIR),
                func=COPY,
                scale=gate_cols[:, e : e + 1],
            )
            dh[e] = psum.tile([P, PACK // PAIR, C], F32, name="bank")
            for u in range(PACK // PAIR):
                nc.tensor.transpose(dh[e][:, u, :], gated[:, u, :], ident[:])

        def mask_da(e, rounded):
            own_mask = mask[:, PACK * e * C : PACK * (e + 1) * C]
            nc.vector.tensor_tensor(
                out=rounded.rearrange("p (s u v) -> p s u v", u=PACK // PAIR, v=PAIR),
                in0=dh[e][:].bitcast(BF16).rearrange("p u (s v) -> p s u v", v=PAIR),
                in1=own_mask.rearrange("p (s u v) -> p s u v", u=PACK // PAIR, v=PAIR),
                op=ALU.mult,
            )

        def quantize_da(first, count, rounded):
            codes = keep.tile([P, count * C], U32, name="da_codes%d" % first, align_bytes=64)
            scales = keep.tile([P, count * C], U8, name="da_scales%d" % first, align_bytes=64)
            nc.vector.quantize_mx(out=codes[:].bitcast(FP8X4), scales=scales[:], in_=rounded)
            for u in range(count):
                da_codes[first + u] = codes[:, u * C : (u + 1) * C]
                da_scales[first + u] = scales[:, u * C : (u + 1) * C]

        def gate_load(n, tile, starts):
            first, count = W2_LOADS[n]
            for u in range(count):
                gate_and_turn(first + u, tile[:, starts[u] : starts[u] + STAGED])

        def mask_load(n, tile, start):
            first, count = W2_LOADS[n]
            da_bf = tile[:, start : start + count * STAGED].bitcast(BF16)
            for u in range(count):
                mask_da(first + u, da_bf[:, u * C * PACK : (u + 1) * C * PACK])
            return first, count, da_bf

        def second_product(e, h, codes, scales, column):
            first, count = [group for group in DX_GROUPS[h] if group[0] <= e][-1]
            if (first, h) not in dx_banks:
                dx_banks[first, h] = psum.tile([P, count * C], F32, name="bank")
            dx_done.add((e, h))
            cols = slice(column, column + P)
            nc.tensor.matmul_mx(
                out=dx_banks[first, h][:, (e - first) * C : (e - first + 1) * C],
                lhsT=codes[:, cols].bitcast(FP8X4),
                lhsT_scale=scales[:, cols],
                rhs=da_codes[e].bitcast(FP8X4),
                rhs_scale=da_scales[e],
                start=True,
                stop=True,
            )
            if all((member, h) in dx_done for member in range(first, first + count)):
                copy = nc.vector.tensor_copy if h == 0 and first + count == E else nc.scalar.copy
                copy(out=dx[h][:, first * C : (first + count) * C], in_=dx_banks[first, h][:])

        def whole_pair(first):
            rounded = rounded_tile()
            tile = loaded_tile()
            for u, raw in enumerate(load_experts(w1, first, 2, tile)):
                copy = nc.scalar.copy if u else nc.vector.tensor_copy
                interleave(copy, rounded[:, u * PACK * K : (u + 1) * PACK * K], raw)
            for u in range(2):
                codes, scales = quantize(rounded[:, u * PACK * K : (u + 1) * PACK * K])
                for h in range(K // P):
                    second_product(first + u, h, codes, scales, h * P)
            return tile

        def load_halves(experts, h, copy, rounded):
            count = len(experts)
            tile = loaded_tile()
            flat = tile[:, 0 : count * HALF_W1]
            chosen = w1[experts[0] : experts[-1] + 1 : max(experts[-1] - experts[0], 1)]
            rows = chosen.rearrange("u (p j) k -> p j u k", j=PACK)
            nc.sync.dma_start(
                out=flat.rearrange("p (j u k) -> p j u k", u=count, j=PACK), in_=rows[:, :, :, h * P : (h + 1) * P]
            )
            interleave(copy, rounded, flat.rearrange("p (j c) -> p j c", j=PACK))
            return tile

        def multiply_halves(experts, h, rounded):
            codes, scales = quantize(rounded)
            for u, e in enumerate(experts):
                second_product(e, h, codes, scales, u * P)

        def first_halves(experts, copy):
            rounded = rounded_tile()[:, 0 : len(experts) * HALF_W1]
            load_halves(experts, 0, copy, rounded)
            multiply_halves(experts, 0, rounded)

        def picked(h, r, cut):
            return dx[h][:].indirect(pos_sb[r][:, cut.start // LIST_COLS : cut.stop // LIST_COLS])

        def scalar_pick(h, r, cut, result):
            nc.scalar.activation(out=result, in_=picked(h, r, cut), func=COPY)

        def adding_pick(h, r, cut, before, result):
            nc.vector.tensor_tensor(result, picked(h, r, cut), before, ALU.add)

        def store(h, cut, result):
            nc.sync.dma_start(out=out[h * P : (h + 1) * P, cut], in_=result)

        def token_row(n):
            return a_early[:, n * T : (n + 1) * T]

        make_identity(nc, ident[:])
        nc.vector.memset(gate_rows[:], 0.0)
        nc.vector.memset(dy_s[:], 0)
        nc.sync.dma_start(out=dy_w[:], in_=dy_words[0].rearrange("p t d -> p (t d)").bitcast(I32))
        nc.sync.dma_start(offs_sb[:], offs)
        load_w2(0, 1)
        for r in range(4):
            nc.scalar.dma_start(out=dy_s[r:P:32, :], in_=dy_scales[0].bitcast(I32)[r:16:4, :])
        nc.scalar.dma_start(out=gate_rows[0:E, :], in_=gate[0].rearrange("(e c) -> e c", c=C))
        early_rows = load_a(a_early, 0, EARLY_A)
        gate_turned = psum.tile([P, PACK, C], F32, name="bank")
        nc.tensor.transpose(gate_turned[:, 0, :], gate_rows[:], ident[:])
        nc.scalar.copy(out=gate_cols[:], in_=gate_turned[:, 0, 0:E])

        round_w2(0, 0)
        for first in range(0, E, GATHERED):
            gather(first)
            if first == 0:
                first_product(0)
        make_mask(0, SCALAR_MASK, early_rows[:, :, 0 : SCALAR_MASK * C], True)
        make_mask(SCALAR_MASK, EARLY_A, early_rows[:, :, SCALAR_MASK * C :], False)

        last_load = len(W2_LOADS) - 1
        for n in range(1, last_load):
            first, count = W2_LOADS[n]
            load_w2(first, count)
            for u in range(count):
                round_w2(first + u, u)
            masked = mask_load(n - 2, w2_tiles[first], ONE_W2 - STAGED) if n >= 2 else None
            first_product(first)
            if masked:
                quantize_da(*masked)
            first_product(first + 1)
            gate_load(n - 1, w2_tiles[first], (0, 2 * ONE_W2 - STAGED))
        make_mask(EARLY_A, E, load_a(a_late, EARLY_A, E), False)
        last_pair = w2_tiles[W2_LOADS[last_load - 1][0]]
        gate_load(last_load - 1, last_pair, (H, ONE_W2 + H))
        quantize_da(*mask_load(last_load - 2, last_pair, 2 * H))
        load_w2(E - 1, 1)
        round_w2(E - 1, 0)
        first_product(E - 1)
        quantize_da(*mask_load(last_load - 1, w2_tiles[E - 1], ONE_W2 - STAGED))

        whole_pair(0)
        gate_load(last_load, whole_pair(2), (PACK * K,))
        first_halves((6, 7), nc.scalar.copy)
        quantize_da(*mask_load(last_load, whole_pair(4), 0))
        for first in range(8, E - 2, 4):
            first_halves((first, first + 1), nc.scalar.copy)
            first_halves((first + 2, first + 3), nc.vector.tensor_copy)
        first_halves((E - 2,), nc.scalar.copy)
        first_halves((E - 1,), nc.vector.tensor_copy)

        spent, start = [], 0
        for experts in SECOND_HALVES:
            copy = nc.scalar.copy if len(experts) > 1 else nc.vector.tensor_copy
            spent.append(load_halves(experts, 1, copy, mask[:, start : start + len(experts) * HALF_W1]))
            start = start + len(experts) * HALF_W1
            if experts == SECOND_HALVES[0]:
                for r, pos in enumerate((pos1, pos2, pos3)):
                    nc.sync.dma_start(pos_sb[r][:], pos)
        late = [e for experts in SECOND_HALVES for e in experts]
        for begin, end in ((0, 4), (4, 8), (8, 10), (10, 12)):
            last_bf = mask[:, begin * HALF_W1 : end * HALF_W1]
            multiply_halves(late[begin:end], 1, last_bf)

        low, high = slice(0, HALF_T), slice(HALF_T, T)
        for cut in (low, high):
            nc.vector.tensor_copy(token_row(0)[:, cut], picked(0, 0, cut))
        two_low, two_high = spent[1][:, 0:HALF_T], last_bf.bitcast(F32)[:, 0:HALF_T]
        adding_pick(0, 1, low, token_row(0)[:, low], two_low)
        adding_pick(0, 1, high, token_row(0)[:, high], two_high)
        for cut, two_results in ((low, two_low), (high, two_high)):
            adding_pick(0, 2, cut, two_results, spent[-1][:, cut])
            store(0, cut, spent[-1][:, cut])

        one, two, three, total = [token_row(n) for n in range(3, 7)]
        wide, small, late_cut = [slice(first, first + count) for first, count in LAST_CUTS]
        for cut in (wide, small, late_cut):
            scalar_pick(1, 0, cut, one[:, cut])
            adding_pick(1, 2, cut, one[:, cut], three[:, cut])
        for cut in (wide, small, late_cut):
            if cut == small:
                adding_pick(1, 1, cut, three[:, cut], total[:, cut])
            else:
                scalar_pick(1, 1, cut, two[:, cut])
                nc.vector.tensor_tensor(total[:, cut], three[:, cut], two[:, cut], ALU.add)
            store(1, cut, total[:, cut])
